import numpy as np, ml_dtypes
CORES = [1,5,17,21,33,37,49,53]
N = 8
import mx_ref
BF = ml_dtypes.bfloat16
def gentries(a):
    return np.ascontiguousarray(a.reshape(8, 16, -1).transpose(0, 2, 1)).reshape(8, -1)
def gtable(e):
    e = np.asarray(e); return np.ascontiguousarray(e.reshape(8, -1, 16).transpose(0, 2, 1)).reshape(128, -1).astype(np.int32)
def gcols(t, e):
    v = np.concatenate([t.reshape(8, 16, -1, 4), np.zeros((8, 16, 1, 4), BF)], axis=2)
    return np.ascontiguousarray(np.stack([v[g][:, e[g]] for g in range(8)])).reshape(128, -1)
def gpick(z, e):
    return np.concatenate([z[16 * g:16 * g + 16][:, e[g]] for g in range(8)])
def tile(rs):
    return np.stack(rs, axis=2).reshape(128, -1).astype(BF)
def pick(q, e):
    c = np.concatenate([q[0].reshape(128, -1, 4), np.zeros((128, 1, 4), np.uint8)], axis=1); s = np.concatenate([q[1], np.ones((16, 1), np.uint8)], axis=1)
    return (np.ascontiguousarray(c[:, e].reshape(128, -1)), np.ascontiguousarray(s[:, e]))
def join(*qs):
    return (np.concatenate([q[0] for q in qs], axis=1), np.concatenate([q[1] for q in qs], axis=1))
def put(q, e, v):
    c, s = q[0].reshape(128, -1, 4).copy(), q[1].copy(); c[:, e] = v[0].reshape(128, -1, 4); s[:, e] = v[1]
    return (c.reshape(128, -1), s)
def pk(c, s):
    return (np.ascontiguousarray(c), mx_ref.live(s))
def emit(q):
    return q[0], q[1]
def packed(v, rng):
    q = [mx_ref.quantize(np.ascontiguousarray(v[r])) for r in range(N)]
    return np.stack([a for a, b in q]), np.stack([mx_ref.plane(b, rng) for a, b in q])
def values_of_codes():
    e, c = np.zeros((128, 128, 4), np.float32), np.zeros((128, 2, 4), np.uint8)
    e[np.arange(128), np.arange(128), 0] = 1
    c[:127, :, 0] = np.arange(256).reshape(2, 128).T[:127]
    return mx_ref.matmul(mx_ref.quantize(e.reshape(128, 512).astype(BF)), (c.reshape(128, 8), np.full((16, 2), 127, np.uint8))).T.reshape(-1).astype(np.float64)
CODE_VALUE, SCALE_VALUE = values_of_codes(), 2.0 ** (np.arange(256) - 127.0)
def decode(q):
    return (CODE_VALUE[q[0]].reshape(16, 8, -1, 4) * SCALE_VALUE[q[1]][:, None, :, None] + 0.0).reshape(128, -1).astype(np.float32)
def f(rng, *shape):
    return mx_ref.flush((rng.standard_normal(shape, dtype=np.float32) * np.exp2(rng.integers(-2, 3, shape[:-1] + (1,)))).astype(BF))
def wide(rng, *shape, cols=0):
    v = rng.standard_normal(shape, dtype=np.float32) * np.exp2(rng.integers(-12, 13, shape)).astype(np.float32)
    if cols: v *= np.repeat(np.exp2(rng.integers(-cols, cols + 1, shape[:-2] + (1, shape[-1] // 4))) * (rng.random(shape[:-2] + (1, shape[-1] // 4)) > 0.0625), 4, axis=-1).astype(np.float32)
    return mx_ref.flush(v.astype(BF))
C, L, M, R = 256, 6, 32, 3
def big(v):
    v = v.astype(np.float32)
    v[np.abs(v) < np.float32(2.0 ** -16)] = 0
    return v.astype(BF)
def numbers_of(rng):
    return {"x": big(f(rng, N, 128, 4 * C)), "u": np.array(f(rng, N, 128, 512)), "v": np.array(f(rng, N, 128, 512))}
def some_links(rng):
    w = rng.choice([8, 16, 32, C], (8, 1, 1))
    return (np.arange(C) + 1 + (rng.random((8, 2, C)) * w).astype(np.int64)) % C
def links_of(rng):
    return np.stack([gtable(some_links(rng).reshape(8, 2 * C)) for r in range(N)])
def layers(rng):
    return big(f(rng, N, 128, 2048)).reshape(N, 8, 16, 4, 8, 16, 4)
def weights(rng, w):
    c, p = packed(np.ascontiguousarray(w).reshape(N, 128, 2048), rng)
    return {"wc": c, "ws": p}
def setup_inputs(rng):
    return {**numbers_of(rng), "nb": links_of(rng), **weights(rng, layers(rng))}
def setup_inputs_ties(rng):
    d = numbers_of(rng)
    o = rng.permutation(N)
    k = rng.integers(-1, 3, (N, 8, C))
    k[o[1]] = rng.integers(-3, 0, (8, C))
    k[o[2]] = 1
    x = d["x"].reshape(N, 8, 16, C, 4)
    x[:, :, 0] = 0
    x[:, :, 0, :, 0] = k.astype(np.float32).astype(BF)
    u = d["u"].reshape(N, 128, 128, 4)
    u[:, :, ::16] = 0
    for h in range(0, 128, 16): u[:, h, h, 0] = 1
    u[o[0], :, ::16] = 0
    w = layers(rng)
    w[:, :, :, :, :, 0] = 0
    return {"x": x.reshape(N, 128, 4 * C), "u": u.reshape(N, 128, 512), "v": d["v"], "nb": links_of(rng), **weights(rng, w)}
def setup_inputs_near(rng):
    d = numbers_of(rng)
    x = d["x"].astype(np.float32).reshape(N, 8, 16, C, 4)
    x[:, :, 0] = 0
    x[:, :, 8:] = 0
    s = rng.integers(0, 16, (N, 8, C))
    s = ((s[:, :, :, None] >> np.arange(4)) & 1) * np.exp2(np.arange(4) - 23.0)
    u = d["u"].reshape(N, 128, 128, 4)
    u[:, :, ::16] = 0
    nb = np.stack([some_links(rng) for r in range(N)])
    n = np.arange(C)
    first = n // 3 * 3 % (C - C % 3)
    o = rng.permutation(N) % 4
    for r in range(N):
        k = 1.0 if o[r] == 0 else 2.0 ** -30
        if o[r] < 2:
            x[r, :, 0, :, 0] = rng.choice([-1.0, 1.0], (8, C))
            x[r, :, 11, :, 0] = 2.0 ** -10
            x[r, :, 8] = s[r]
            g, e = rng.integers(8), rng.permutation(C)
            nb[r, g, 0, e], nb[r, g, 1, e] = e[first + (n + 1) % 3], e[first + (n + 2) % 3]
            x[r, g, 0, C - 1, 0] = 1.0
            x[r, g, 8, C - 1] = np.exp2(np.arange(4) - 23.0)
        elif o[r] == 2:
            x[r, :, 8, :, 0] = rng.integers(-1, 3, (8, C)) * 2.0 ** -29
            for g in rng.permutation(8)[:4]: x[r, g, 8, rng.integers(C), 0] = rng.choice([-1.0, 1.0]) * 2.0 ** 29
        else:
            x[r, :, 0, :, 0] = rng.choice([0.0, 0.0, 0.0, 0.0, 0.0, 0.0, 1.0, -1.0], (8, C))
            x[r, :, 8] = s[r] * rng.choice([-1.0, 1.0], (8, C, 1))
        for h in range(0, 128, 16):
            u[r, h, h, 0] = 1.0 if o[r] == 3 else 0.0 if o[r] == 2 else k
            u[r, h + 8, h] = k
            if o[r] < 2: u[r, h + 11, h, 0] = k
    w = layers(rng)
    for i in [0, 8, 9, 10, 11, 12, 13, 14, 15]:
        w[:, :, i] = 0
        w[:, :, :, :, :, i] = 0
    return {"x": x.reshape(N, 128, 4 * C).astype(BF), "u": u.reshape(N, 128, 512), "v": d["v"], "nb": np.stack([gtable(nb[r].reshape(8, 2 * C)) for r in range(N)]), **weights(rng, w)}
def setup_inputs_huge(rng):
    d = numbers_of(rng)
    c = rng.choice([-1.0, 1.0], (N, 1, C, 1))
    c[rng.permutation(N)[:N // 2]] = -1.0
    x = 2.0 ** 30 * (0.6 + 0.2 * rng.random((N, 128, C, 4))) * c
    u = d["u"].reshape(N, 128, 128, 4)
    u[:, :, ::16] = (2.0 ** 30 * (1.0 - 0.1 * rng.random((N, 128, 8, 4)))).astype(np.float32).astype(BF)
    w = np.zeros((N, 128, 4, 128, 4), np.float32)
    i = np.arange(128)
    for b in range(4): w[:, i, b, i, b] = -2
    return {"x": x.astype(np.float32).reshape(N, 128, 4 * C).astype(BF), "u": u.reshape(N, 128, 512), "v": d["v"], "nb": links_of(rng), **weights(rng, w.astype(BF))}
def setup_inputs_forms(rng):
    d = numbers_of(rng)
    x = d["x"].astype(np.float32).reshape(N, 8, 16, C, 4)
    a = (1.0 + (2 * rng.integers(0, 64, (N, 8, 8, C, 4)) + 1) * 2.0 ** -7) * np.exp2(-rng.integers(8, 14, (N, 8, 8, C, 4)).astype(np.float64))
    x[:, :, :8] = a * rng.choice([-1.0, 1.0], a.shape)
    x[:, :, 0, :, 0] = rng.choice([1.875, 1.96875], (N, 8, C))
    x[:, :, 1, :, 0] = rng.integers(8, 10, (N, 8, C)) * rng.choice([-1.0, 1.0], (N, 8, C)) * 2.0 ** -16
    u = d["u"].reshape(N, 128, 128, 4)
    u[:, :, ::16] = 0
    for h in range(0, 128, 16): u[:, h + 1, h, 0] = 1
    nb = np.stack([some_links(rng) for r in range(N)])
    o = rng.permutation(N) % 4
    for r in range(N):
        count = rng.permutation([M, M, M, M - 1, M + 1, 1, 0, C])
        for g in range(8):
            if o[r] == 0: nb[r, g, 1] = nb[r, g, 0]
            if o[r] in (1, 2):
                n = rng.integers(0, 2 * L - 1, C)
                n[:2 * L - 2] = np.arange(1, 2 * L - 1)
                n[2 * L - 2] = 2 * L - 2
                if o[r] == 1: n[L - 2] = 2 * L - 2
                else: n[2 * L - 3] = 0
                m = n.copy()
                e = 2 * L - 1 + np.arange(min(int(count[g]), C - 2 * L + 1))
                if o[r] == 1: n[e] = rng.integers(0, 2, len(e)) * (L - 1)
                else: n[e] = rng.integers(0, 2 * L - 2, len(e))
                m[e] = (n[e] + L - 1) % (2 * L - 2)
                k = rng.permutation(C)
                nb[r, g, 0, k], nb[r, g, 1, k] = k[n], k[m]
    return {"x": x.reshape(N, 128, 4 * C).astype(BF), "u": u.reshape(N, 128, 512), "v": d["v"], "nb": np.stack([gtable(nb[r].reshape(8, 2 * C)) for r in range(N)]), **weights(rng, layers(rng))}
def setup_inputs_spread(rng):
    d = setup_inputs(rng)
    d["x"] = big(wide(rng, N, 128, 4 * C, cols=6))
    return d
def check_inputs(d):
    b = []
    for k in ("x", "u", "v"):
        a = np.abs(d[k].astype(np.float32))
        if not (np.isfinite(a).all() and ((a == 0) | (a >= 2.0 ** -30) & (a <= 2.0 ** 30)).all()): b.append("a value of " + k)
    if not ((d["nb"] >= 0) & (d["nb"] < C)).all(): b.append("an entry of nb")
    none, least, most = [emit(mx_ref.quantize(np.full((128, 16), k, np.float32).astype(BF)))[1][0, 0] for k in (0.0, 2.0 ** -30, 2.0 ** 30)]
    for r in range(N):
        if ((d["wc"][r] == 0x7F) | (d["wc"][r] == 0xFF)).any(): b.append("wc: a code that is no number")
        s = mx_ref.live(d["ws"][r])
        if ((s != none) & ((s < least) | (s > most))).any(): b.append("ws: a scale out of range")
    return b
def bubbles(a, s):
    at = lambda t, e: np.take_along_axis(t, e, axis=1)
    c = np.where(s > 0, a[:, C:], a[:, :C])
    p, q = [a[:, :C]], [a[:, C:]]
    for k in range(1, L):
        p.append(at(c, p[-1]))
        q.append(at(c, q[-1]))
    i, j = np.full((8, C), -1), np.full((8, C), -1)
    for n in reversed(range(2 * L - 1)):
        for k in reversed(range(max(0, n - L + 1), min(n, L - 1) + 1)):
            met = p[k] == q[n - k]
            i[met], j[met] = k, n - k
    is_bubble = (i >= 0) & (p[0] != q[0])
    o = np.lexsort((-s, ~is_bubble))[:, :M]
    filled = at(is_bubble, o)
    g, k = np.arange(8)[:, None, None], np.arange(L)
    np0 = np.stack(p, axis=2)[g, o[:, :, None], np.minimum(k, at(i, o)[:, :, None])]
    nq0 = np.stack(q, axis=2)[g, o[:, :, None], np.minimum(k, at(j, o)[:, :, None])]
    one = at(s, at(q[0], o)) > at(s, at(p[0], o))
    new = a.copy()
    h, m = np.nonzero(filled)
    new[h, (o + C * ~one)[h, m]] = np0[h, m, L - 1]
    slots = [np.where(filled[:, :, None], t, -1).reshape(8, L * M) for t in (np0, nq0, np.where(one[:, :, None], nq0, np0))]
    e = np.full((8, C), -1)
    for n in reversed(range(L * M)):
        h = np.flatnonzero(slots[2][:, n] >= 0)
        e[h, slots[2][h, n]] = n
    return slots[0], slots[1], e, new
def reference(x, u, v, nb, wc, ws):
    qu = [mx_ref.quantize(u[r]) for r in range(N)]
    lay = [pk(wc[r], ws[r]) for r in range(N)]
    now = [x[r] for r in range(N)]
    links = [gentries(nb[r]).astype(np.int64) for r in range(N)]
    for t in range(R):
        own, sent, place = [], [], []
        for r in range(N):
            q = mx_ref.quantize(now[r])
            own.append(decode(q))
            s = mx_ref.matmul(qu[r], q)[::16] + np.float32(0.0)
            a, b, e, links[r] = bubbles(links[r], s)
            place.append(e)
            w = own[r].astype(BF)
            sent.append(mx_ref.quantize(((gcols(w, a).astype(np.float32) + gcols(w, b).astype(np.float32)) * np.float32(0.5)).astype(BF)))
        for r in range(N):
            came, made = sent[(r - 1) % N], []
            for b in range(4):
                h = mx_ref.matmul(pick(lay[r], np.arange(128 * b, 128 * b + 128)), came) * np.float32(0.03125)
                made.append(gpick(np.concatenate([h, np.zeros((128, 1), np.float32)], axis=1), place[r]) + own[r][:, b::4])
            now[r] = tile(made)
    y, ol = np.zeros((N, 128, C), np.float32), np.zeros((N, 8, 2 * C), np.float32)
    oc, osc = np.zeros((N, 128, 4 * C), np.uint8), np.zeros((N, 16, C), np.uint8)
    for r in range(N):
        q = mx_ref.quantize(now[r])
        y[r] = mx_ref.matmul(mx_ref.quantize(v[r]), q)
        ol[r] = links[r]
        oc[r], osc[r] = emit(q)
    return {"y": y, "ol": ol, "oc": oc, "osc": osc}

@@ -1,0 +1,377 @@
+import numpy as np
+from concourse.mybir import dt, AluOpType, ActivationFunctionType, AxisListType
+
+N = 8
+R = 3
+C = 256
+NS = 11
+BIG = 131072.0
+F32, BF, I32, U16, U8, X4 = "float32", "bfloat16", "int32", "uint16", "uint8", "float8_e4m3fn_x4"
+
+
+def _sb(n, d):
+    return ("sbuf", [128, n], d)
+
+
+SCRATCH = {
+    "xt": _sb(1024, BF), "xs": _sb(1024, BF), "ut": _sb(512, BF), "vt": _sb(512, BF), "et": _sb(2048, BF),
+    "eye": _sb(128, BF), "one": _sb(128, BF),
+    "xq": _sb(256, X4), "xp": _sb(256, U8), "uq": _sb(128, X4), "up": _sb(128, U8), "uq2": _sb(128, X4),
+    "up2": _sb(128, U8), "vq": _sb(128, X4), "vp": _sb(128, U8), "eq": _sb(512, X4), "ep": _sb(512, U8),
+    "wq": _sb(512, X4), "wp": _sb(512, U8),
+    "zt": _sb(768, BF), "zq": _sb(192, X4), "zp": _sb(192, U8),
+    "pi": _sb(4, I32), "pf": _sb(4, F32), "sm": _sb(64, F32), "idw": _sb(512, F32), "rp": _sb(256, F32), "nmask": _sb(256, F32),
+    "sc0": _sb(256, F32), "nw": _sb(16, F32), "nT": _sb(256, F32), "nTi": _sb(256, F32), "kk": _sb(192, F32), "rv": _sb(24, F32),
+    "scab": _sb(24, F32), "exl": _sb(16, U16), "upl": _sb(8, U16), "w256": _sb(512, F32), "w2048": _sb(272, F32),
+    "w512": _sb(272, F32), "n512": _sb(16, F32), "nm": _sb(2, F32), "md": _sb(576, F32), "gm": _sb(64, F32),
+    "cl": _sb(160, F32), "cl2": _sb(160, F32), "cl16": _sb(10, U16),
+    "v0": _sb(256, F32), "a1": _sb(256, F32), "a2": _sb(256, F32), "a3": _sb(256, F32), "a4": _sb(256, F32),
+    "asc": _sb(256, F32),
+    "ms": _sb(256, F32), "sc": _sb(256, F32), "ssb": _sb(256, F32), "cf": _sb(48, F32),
+    "wc16": _sb(16, U16), "va": _sb(256, F32), "vb": _sb(256, F32), "pq": _sb(1280, F32),
+    "t3": ("sbuf", [128, 32, 16], F32), "e3": ("sbuf", [128, 16, 36], BF), "e2": _sb(576, BF), "so": _sb(576, F32),
+    "ne": _sb(32, F32), "yv": _sb(16, F32), "ex": _sb(256, F32),
+    "ur": _sb(256, F32), "jk": _sb(4096, BF), "acc": _sb(16, F32), "acc2": _sb(16, F32),
+    "a16": _sb(16, U16), "nB": _sb(32, F32), "kap": _sb(256, F32), "r16": _sb(16, U16),
+    "qq": _sb(256, F32), "xk0": _sb(264, F32), "xk1": _sb(264, F32), "kv": _sb(2, F32), "kw": _sb(32, I32),
+    "kn": _sb(16, I32), "off": _sb(4, U16), "g2": _sb(128, F32), "t2": ("sbuf", [128, 8, 16], F32),
+    "w2": ("sbuf", [128, 4, 20], F32), "ij": _sb(24, I32),
+    "ff": _sb(24, F32), "dd": _sb(24, F32), "d2": _sb(24, F32), "ab": _sb(24, F32),
+    "ab16": _sb(32, U16), "br": _sb(2, F32), "dba": _sb(16, F32), "bt": _sb(16, F32), "bt16": _sb(16, U16),
+    "ke": _sb(192, F32), "abd": ("sbuf", [128, 16, 200], F32), "ev": _sb(16, F32), "ei": _sb(64, I32), "e16": _sb(16, U16),
+    "li": _sb(12, I32), "ln16": _sb(2, U16), "mt": _sb(32, I32), "lt": _sb(560, I32), "lw": _sb(32, I32),
+    "lw16": _sb(32, U16), "dl": _sb(16, F32), "olr": _sb(512, F32), "ysb": _sb(256, F32),
+    "at": _sb(768, BF), "f2": _sb(1088, BF), "fw": _sb(1024, BF), "hb": _sb(896, F32),
+}
+PS = ["ps1", "ps2", "pd0", "pd1", "pd2", "pd3", "ph0", "ph1"]
+for _t in range(R):
+    SCRATCH["yq%d" % _t] = _sb(192, X4)
+    SCRATCH["yp%d" % _t] = _sb(192, U8)
+for _n in PS:
+    SCRATCH[_n] = ("psum", [128, 512], F32)
+
+DMAS = ["dx", "du", "dv", "dwc", "dws", "dn0", "dn1", "dlt", "das", "dl0", "dl1", "oy", "ool", "ooc", "os0", "os1", "os2", "os3"]
+SEMAPHORES = ["sv", "ss", "sp", "sg", "lc"] + ["ar%d" % t for t in range(R)] + DMAS
+
+
+def rank_program(g, core, T, topo):
+    rank = T.rank_of(core)
+    if rank is None:
+        return
+    A = AluOpType
+    ACT = ActivationFunctionType
+    XAX = AxisListType.X
+    queues = {"v": g.vector, "s": g.scalar, "p": g.tensor, "g": g, "y": g.sync}
+    total, waited, wr, rd = {}, {q: {} for q in queues}, {}, {}
+
+    def need(q, deps):
+        best = {}
+        for s, n in deps:
+            best[s] = max(best.get(s, 0), n)
+        for s in sorted(best):
+            if waited[q].get(s, 0) < best[s]:
+                queues[q].wait_ge(T.sem[s], best[s])
+                waited[q][s] = best[s]
+
+    def before(q, reads, writes):
+        deps = []
+        for k in reads:
+            if k in wr:
+                deps.append(wr[k][1:])
+            if k in PS:
+                deps += [r[1:] for r in rd.get(k, []) if r[0] != q]
+        for k in writes:
+            if k in wr:
+                deps.append(wr[k][1:])
+            deps += [r[1:] for r in rd.get(k, [])]
+        need(q, deps)
+
+    def after(q, sem, inc, reads, writes):
+        total[sem] = total.get(sem, 0) + inc
+        tok = (q, sem, total[sem])
+        for k in writes:
+            wr[k] = tok
+            rd[k] = []
+        for k in reads:
+            if k not in writes:
+                rd[k] = [r for r in rd.get(k, []) if r[1] != sem] + [tok]
+
+    def op(q, reads, writes, name, *args, **kw):
+        before(q, reads, writes)
+        fns = {"memset": g.vector.memset, "tt": g.vector.tensor_tensor, "ts": g.vector.tensor_scalar,
+               "cp": g.vector.tensor_copy, "red": g.vector.tensor_reduce, "scan": g.vector.tensor_tensor_scan,
+               "tr": g.vector.transpose, "qz": g.vector.quantize_mx, "act": g.scalar.activation,
+               "mm": g.tensor.matmul_mx, "iota": g.iota, "asel": g.affine_select}
+        fns[name](*args, **kw).then_inc(T.sem["s" + q], 1)
+        after(q, "s" + q, 1, reads, writes)
+
+    def dma(q, sem, reads, writes, out, in_):
+        before(q, reads, writes)
+        queues[q].dma_start(out, in_).then_inc(T.sem[sem], 16)
+        after(q, sem, 16, reads, writes)
+
+    def V(name, writes, reads, *args, **kw):
+        op("v", reads.split(), writes.split(), name, *args, **kw)
+
+    def S(writes, reads, out, in_, func, **kw):
+        op("s", reads.split(), writes.split(), "act", out, in_, func, **kw)
+
+    dma("y", "dx", [], ["xt"], T.xt[:], T.x[:])
+    dma("s", "du", [], ["ut"], T.ut[:], T.u[:])
+    dma("y", "dn0", [], ["lw", "lwb"], T.lw[:], T.nb[:])
+    dma("y", "dn1", [], ["lt0"], T.lt[0:128:16, 0:256], T.nb[:, 0:16])
+    dma("y", "dlt", [], ["lt1"], T.lt[0:128:16, 256:512], T.nb[:, 16:32])
+    dma("y", "dwc", [], ["wq"], T.wq[:, 0:512].bitcast(dt.uint8), T.wc[:])
+    dma("y", "dws", [], ["wp"], T.wp[:, 0:512], T.ws[:])
+    dma("y", "dv", [], ["vt"], T.vt[:], T.v[:])
+
+    def iota(key, out, pattern, base, cm=0):
+        kw = {} if key == "pi" else {"allow_small_or_imprecise_dtypes": True}
+        op("g", [], [key], "iota", out, pattern, base, cm, **kw)
+    V("memset", "one", "", T.one[:], 1.0)
+    V("memset", "et", "", T.et[:], 0.0)
+    iota("pi", T.pi[:, 0:1], [[0, 1]], 0, 1)
+    iota("sm1", T.sm[:, 8:14], [[-1, 6]], 5)
+    iota("sm2", T.sm[:, 16:22], [[1, 6]], 8)
+    iota("sm0", T.sm[:, 0:8], [[16, 8]], 0)
+    op("g", ["one"], ["eye"], "asel", T.eye[:], T.one[:], [[-1, 128]], A.is_equal, 0.0, 0, 1)
+    iota("idw", T.idw[:], [[1, 512]], 0)
+    iota("rp", T.rp[:], [[0, 16], [1, 16]], 0)
+    iota("nw0", T.sm[:, 32:48], [[16, 16]], 0)
+    iota("exl0", T.sm[:, 48:64], [[1, 16]], 0)
+    pairs = [(i, s - i) for s in range(10, 0, -1) for i in range(min(5, s), max(0, s - 5) - 1, -1)]
+    worth = [8 * (i + j) + i for i, j in pairs] + [0]
+    iota("md", T.md[:], [[0, 576]], -1)
+    iota("md", T.md[:, 0:576:36], [[0, 16]], -(2 ** 24 - 1))
+    for k in range(len(pairs)):
+        d = worth[k] - worth[k + 1]
+        if d != 1:
+            iota("md", T.md[:, k + 1:576:36], [[0, 16]], -d)
+    iota("nTi", T.nTi[:], [[32, 8], [0, 32]], 1)
+    iota("w256", T.w256[:], [[256, 512]], -65280)
+    iota("w2048", T.w2048[:], [[2048, 272]], 0)
+    iota("sm3", T.sm[:, 24:26], [[16, 2]], 0)
+    iota("xk0", T.xk0[:, 256:264], [[0, 8]], 527)
+    iota("xk1", T.xk1[:, 256:264], [[0, 8]], 783)
+    iota("rv", T.rv[:], [[0, 4], [1, 6]], 0)
+    iota("gm", T.gm[:], [[0, 2], [1, 2], [0, 16]], 0)
+    iota("cl", T.cl[:], [[0, 160]], 0)
+    iota("cl", T.cl[:, 0:16], [[0, 4], [1, 2], [0, 2]], 0)
+    iota("cl", T.cl[:, 32:56], [[0, 2], [1, 2], [0, 6]], 0)
+    iota("cl", T.cl[:, 64:88], [[12, 2], [1, 6], [6, 2]], 0)
+    iota("cl", T.cl[:, 96:108], [[1, 2], [0, 6]], 0)
+    iota("cl", T.cl[:, 128:140], [[1, 6], [6, 2]], 0)
+    iota("pqz", T.pq[:, 512:1280], [[0, 768]], 256)
+    for b in range(4):
+        iota("f2z", T.f2[:, 272 * b + 256:272 * b + 272], [[0, 16]], 0)
+    iota("dbz", T.dba[:, 12:16], [[0, 4]], 0)
+    iota("kk", T.kk[:], [[1, 6], [8, 32]], 0)
+    iota("w512", T.w512[:], [[512, 272]], 0)
+    for b in range(4):
+        iota("hbz", T.hb[:, 224 * b + 192:224 * b + 224], [[0, 32]], 0)
+
+    V("ts", "pi1", "pi", T.pi[:, 1:2], T.pi[:, 0:1], 15, None, A.bitwise_and)
+    V("ts", "pi2", "pi", T.pi[:, 2:3], T.pi[:, 0:1], 31, None, A.bitwise_and)
+    V("ts", "pi3", "pi", T.pi[:, 3:4], T.pi[:, 0:1], 4, 1, A.arith_shift_right, A.bitwise_and)
+    V("cp", "pf", "pi1 pi2 pi3", T.pf[:, 0:3], T.pi[:, 1:4])
+    r16, p32 = T.pf[:, 0:1], T.pf[:, 1:2]
+    V("ts", "sm1", "sm1 pf", T.sm[:, 8:14], T.sm[:, 8:14], r16, None, A.is_equal)
+    V("ts", "sm2", "sm2 pf", T.sm[:, 16:22], T.sm[:, 16:22], r16, None, A.is_equal)
+    V("cp", "upl", "sm0", T.upl[:], T.sm[:, 0:8])
+    V("tt", "sm1", "sm1 sm2", T.sm[:, 8:14], T.sm[:, 8:14], T.sm[:, 16:22], A.add)
+    for b in range(4):
+        S("et", "eye", T.et[:, 512 * b + b:512 * b + 512:4], T.eye[:], ACT.Copy)
+    V("qz", "uq up", "ut", T.uq[:, 0:128], T.up[:, 0:128], T.ut[:, 0:512])
+    V("cp", "uq2", "uq upl", T.uq2[:, 0:128].bitcast(dt.uint32), T.uq[:, 0:128].bitcast(dt.uint32).indirect(T.upl[:, 0:8]))
+    V("cp", "up2", "up upl", T.up2[:, 0:128], T.up[:, 0:128].indirect(T.upl[:, 0:8]))
+    V("qz", "xq xp", "xt", T.xq[:, 0:256], T.xp[:, 0:256], T.xt[:, 0:1024])
+    V("ts", "nmask", "rp pf", T.nmask[:], T.rp[:], r16, -1.0, A.is_equal, A.mult)
+    V("ts", "sc0", "rp", T.sc0[:], T.rp[:], 0.0, None, A.not_equal)
+    for t, k in enumerate(["v0", "a1", "a2", "a3", "a4", "asc"]):
+        S(k, "idw sm1", T[k][:], T.idw[:, 0:256], ACT.Copy, scale=T.sm[:, 8 + t:9 + t])
+
+    def lists():
+        V("cp", "lw16", "lw lwb", T.lw16[:], T.lw[:])
+        V("tt", "dl", "lw lwb", T.dl[:], T.lw[:, 16:32], T.lw[:, 0:16], A.subtract)
+    lists()
+
+    def mm(out, st, stk, sc, mv, mvk, mp, n):
+        op("p", stk.split() + mvk.split(), [out], "mm", T[out][:, 0:n], st, sc, mv, mp, True, True)
+
+    dst = T.cores[(rank + 1) % N]
+    prv = T.cores[(rank - 1) % N]
+
+    def engs(a, b):
+        e = topo.engines(a, b)
+        return e[::len(e) // 8]
+    emask = sum(1 << k for k in engs(core, dst))
+    rid, pid = topo.addr(dst)[:2]
+
+    def send(t):
+        before("g", ["zq", "zp"], [])
+        n = len(engs(core, dst))
+        g.remote_dma(T["yq%d" % t][:, 0:192].bitcast(dt.uint8), T.zq[:, 0:192].bitcast(dt.uint8), T.sem["ar%d" % t], T.sem.lc, pid, rid, emask)
+        g.remote_dma(T["yp%d" % t][:, 0:192], T.zp[:, 0:192], T.sem["ar%d" % t], T.sem.lc, pid, rid, emask)
+        after("g", "lc", 2 * n, ["zq", "zp"], [])
+        m = 2 * len(engs(prv, core))
+        total["ar%d" % t] = m
+        wr["y%d" % t] = ("r", "ar%d" % t, m)
+
+    def late_constants():
+        S("md", "md", T.md[:], T.md[:], ACT.Copy, scale=1.0 / 128)
+        S("nT", "nTi pf", T.nT[:], T.nTi[:], ACT.Identity, bias=p32, scale=1.0)
+        S("nw", "nw0 pf", T.nw[:], T.sm[:, 32:48], ACT.Identity, bias=r16, scale=1.0)
+        S("n512", "nw", T.n512[:], T.nw[:], ACT.Copy, scale=-512.0)
+        S("sm3", "sm3 pf", T.sm[:, 24:26], T.sm[:, 24:26], ACT.Identity, bias=r16, scale=1.0)
+        S("nm", "sm3", T.nm[:], T.sm[:, 24:26], ACT.Copy, scale=-2048.0)
+        S("sm4", "pf", T.sm[:, 28:29], r16, ACT.Copy, scale=16.0)
+        for k in ("xk0", "xk1"):
+            S(k, k + " sm4", T[k][:, 256:264], T[k][:, 256:264], ACT.Identity, bias=T.sm[:, 28:29], scale=1.0)
+        V("cp", "exl", "exl0", T.exl[:], T.sm[:, 48:64])
+
+    def later_constants():
+        V("ts", "scab", "rv", T.scab[:], T.rv[:], 0.0, None, A.not_equal)
+        V("ts", "gm", "gm pf", T.gm[:], T.gm[:], T.pf[:, 2:3], None, A.is_equal)
+        V("tt", "cl2", "cl nmask", T.cl2[:], T.cl[:], T.nmask[:, 0:160], A.mult)
+        V("scan", "cl", "cl2 sc0", T.cl[:], T.sc0[:, 0:160], T.cl2[:], 0.0, A.mult, A.add)
+        V("ts", "cl16", "cl", T.cl16[:], T.cl[:, 15:160:16], -1.0, None, A.mult)
+        V("memset", "w2z", "", T.w2[:, :, 0], 0.0)
+        V("memset", "abz", "", T.abd[:, :, 192:200], 254.0)
+    V("memset", "e3", "", T.e3[:, :, 0], 0.0)
+
+    for t in range(R):
+        xq, xp = T.xq[:, 0:256], T.xp[:, 0:256]
+        for k in ("ps1", "ps2"):
+            mm(k, T.uq2[:, 0:128], "uq2 up2", T.up2[:, 0:128], xq, "xq xp", xp, 256)
+        if t == 0:
+            V("qz", "eq ep", "et", T.eq[:, 0:512], T.ep[:, 0:512], T.et[:, 0:2048])
+        for b in range(4):
+            mm("pd%d" % b, T.eq[:, 128 * b:128 * b + 128], "eq ep", T.ep[:, 128 * b:128 * b + 128], xq, "xq xp", xp, 256)
+        V("tt", "ms", "ps1 nmask", T.ms[:], T.ps1[:, 0:256], T.nmask[:], A.mult)
+        S("ssb", "ps2", T.ssb[:], T.ps2[:, 0:256], ACT.Copy)
+        dma("y", "das", ["ssb"], ["asc"], T.asc[15:128:16, :], T.ssb[15:128:16, :])
+        V("scan", "sc", "ms sc0", T.sc[:], T.sc0[:], T.ms[:], 0.0, A.mult, A.add)
+        V("ts", "cf", "sc", T.cf[:, 0:16], T.sc[:, 15:256:16], 0.0, None, A.is_lt)
+        V("tt", "c1", "cf dl", T.cf[:, 16:32], T.cf[:, 0:16], T.dl[:], A.mult)
+        V("tt", "c2", "c1 lw lwb", T.cf[:, 32:48], T.cf[:, 16:32], T.lw[:, 0:16], A.add)
+        V("cp", "wc16", "c2", T.wc16[:], T.cf[:, 32:48])
+
+        def order(lo, hi):
+            for c in range(lo, hi):
+                S("jk%d acc%d" % (c, c), "ssb sc", T.jk[:, 256 * c:256 * c + 256], T.ssb[:], ACT.Sign, bias=T.sc[:, 16 * c + 15:16 * c + 16], scale=1.0, accum_out=T.acc[:, c:c + 1])
+        order(0, 11)
+        cur = "v0"
+        for k, add in enumerate(["a1", "a2", "a3", "a4", "asc"]):
+            nxt = "va" if k % 2 == 0 else "vb"
+            V("tt", nxt, cur + " wc16 " + add, T[nxt][:], T[cur][:, 0:256].indirect(T.wc16[:, 0:16]), T[add][:], A.add)
+            cur = nxt
+        V("cp", "pq0", cur + " lw16", T.pq[:, 0:256], T[cur][:, 0:256].indirect(T.lw16[:, 0:16]))
+        S("pq1", cur + " lw16", T.pq[:, 256:512], T[cur][:, 0:256].indirect(T.lw16[:, 16:32]), ACT.Copy)
+        order(11, 16)
+        V("tr", "t3", "pq0 pq1", T.t3[:], T.pq[:, 0:512])
+        if t == 0:
+            late_constants()
+        k = 1
+        for s in range(10, 0, -1):
+            hi, lo = min(5, s), max(0, s - 5)
+            n = hi - lo + 1
+            V("tt", "e3_%d" % s, "t3 e3", T.e3[:, :, k:k + n], T.t3[:, 0:16, 13 - hi:14 - lo], T.t3[:, 16:32, s - hi:s - lo + 1], A.is_equal)
+            k += n
+        V("tt", "ne", "t3", T.ne[:, 0:16], T.t3[:, 0:16, 0], T.t3[:, 16:32, 0], A.is_equal)
+        V("ts", "e2", "e3 " + " ".join("e3_%d" % s for s in range(1, 11)), T.e2[:], T.e3[:], BIG, 1.0 - BIG, A.mult, A.add)
+        V("ts", "neb", "ne", T.ne[:, 16:32], T.ne[:, 0:16], BIG, None, A.mult)
+        V("scan", "so", "e2 md", T.so[:], T.e2[:], T.md[:], -BIG, A.max, A.add)
+        accs = " ".join("acc%d" % c for c in range(16))
+        V("tt", "yv", "neb so", T.yv[:], T.ne[:, 16:32], T.so[:, 35:576:36], A.subtract)
+        V("tt", "ex", "yv exl nT", T.ex[:], T.yv[:, 0:16].indirect(T.exl[:, 0:16]), T.nT[:], A.add)
+        V("tr", "ur", "ex", T.ur[:], T.ex[:])
+        V("ts", "a16", accs, T.a16[:], T.acc[:], 255.0, None, A.add)
+        V("ts", "nb0", accs, T.nB[:, 16:32], T.acc[:], -256.0, None, A.mult)
+        V("tt", "kap", "a16 w256 ur", T.kap[:], T.w256[:, 0:512].indirect(T.a16[:, 0:16]), T.ur[:], A.add)
+        V("tt", "nB", "nb0 nw", T.nB[:, 0:16], T.nB[:, 16:32], T.nw[:], A.subtract)
+        for c in range(NS):
+            S("jk%d rk%d" % (c, c), "kap nB", T.jk[:, 256 * c:256 * c + 256], T.kap[:], ACT.Sign, bias=T.nB[:, c:c + 1], scale=1.0, accum_out=T.acc2[:, c:c + 1])
+        for c in range(NS, 16):
+            V("ts", "jk%d" % c, "kap nB", T.jk[:, 256 * c:256 * c + 256], T.kap[:], T.nB[:, c:c + 1], 0.0, A.add, A.is_lt)
+        for c in range(NS, 16):
+            V("red", "rk%d" % c, "jk%d" % c, T.acc2[:, c:c + 1], T.jk[:, 256 * c:256 * c + 256], XAX, A.add)
+        V("cp", "r16b", " ".join("rk%d" % c for c in range(NS, 16)), T.r16[:, NS:16], T.acc2[:, NS:16])
+        if t == 0:
+            later_constants()
+        V("ts", "r16a", " ".join("rk%d" % c for c in range(NS)), T.r16[:, 0:NS], T.acc2[:, 0:NS], -0.5, 128.0, A.mult, A.add)
+        V("tt", "qq", "r16a r16b w2048 ur", T.qq[:], T.w2048[:, 0:272].indirect(T.r16[:, 0:16]), T.ur[:], A.add)
+        S("xk1a", "qq nm", T.xk1[:, 0:256], T.qq[:], ACT.Identity, bias=T.nm[:, 1:2], scale=1.0)
+        V("ts", "xk0a", "qq nm", T.xk0[:, 0:256], T.qq[:], T.nm[:, 0:1], None, A.add)
+        V("red", "kv0", "xk0 xk0a", T.kv[:, 0:1], T.xk0[:, 0:264], XAX, A.min, apply_absolute_value=True)
+        V("red", "kv1", "xk1 xk1a", T.kv[:, 1:2], T.xk1[:, 0:264], XAX, A.min, apply_absolute_value=True)
+        for b in range(4):
+            S("f2_%d" % b, "pd%d f2z" % b, T.f2[:, 272 * b:272 * b + 256], T["pd%d" % b][:, 0:256], ACT.Copy, scale=0.5)
+        for b in range(4):
+            S("fw%d" % b, "pd%d" % b, T.fw[:, 256 * b:256 * b + 256], T["pd%d" % b][:, 0:256], ACT.Copy)
+        V("ts", "kn", "kv0 kv1 cl16", T.kn[:], T.kv[:, 0:2].indirect(T.cl16[:, 0:1]), -0.34, None, A.add)
+        V("ts", "kw", "kv0 kv1 cl16", T.kw[:], T.kv[:, 0:2].indirect(T.cl16[:, 2:4]), 128.0, None, A.mult)
+        V("cp", "off", "kn", T.off[:], T.kn[:, 0:4])
+        V("ts", "ij", "kw", T.ij[:], T.kw[:, 0:24], 7, None, A.bitwise_and)
+        for kind in range(2):
+            V("tt", "g2_%d" % kind, "pqz pq0 pq1 off gm", T.g2[:, 64 * kind:64 * kind + 64], T.pq[:, 256 * kind:256 * kind + 1024].indirect(T.off[:, 0:4]), T.gm[:], A.mult)
+        V("ts", "ei ek", "kw", T.ei[:, 0:24], T.kw[:, 0:24], 3, 15, A.arith_shift_right, A.bitwise_and)
+        V("tr", "t2", "g2_0 g2_1", T.t2[:], T.g2[:])
+        V("tt", "ij", "ei ij", T.ij[:, 12:24], T.ei[:, 12:24], T.ij[:, 12:24], A.subtract)
+        V("tt", "w2", "t2", T.w2[:, :, 1:17], T.t2[:, 0:8:2, :], T.t2[:, 1:8:2, :], A.add)
+        V("tt", "ff", "rv ij", T.ff[:], T.ij[:], T.rv[:], A.is_ge)
+        V("tt", "dd", "w2 w2z", T.dd[:], T.w2[:, :, 1:7], T.w2[:, :, 0:6], A.subtract)
+        V("tt", "d2", "dd ff", T.d2[:], T.dd[:], T.ff[:], A.mult)
+        V("scan", "ab", "d2 scab", T.ab[:], T.scab[:], T.d2[:], 0.0, A.mult, A.add)
+        V("cp", "ab16", "ab cl16", T.ab16[:], T.ab[:, 0:24].indirect(T.cl16[:, 4:6]))
+        V("tt", "br", "w2", T.br[:], T.w2[:, 2:4, 16], T.w2[:, 0:2, 16], A.is_gt)
+        V("tt", "dba", "ab", T.dba[:, 0:12], T.ab[:, 12:24], T.ab[:, 0:12], A.subtract)
+        V("tt", "bt", "dbz dba br cl16", T.bt[:], T.br[:, 0:2].indirect(T.cl16[:, 6:7]), T.dba[:], A.mult)
+        for b in range(4):
+            S("at%d" % b, "f2z f2_%d ab16" % b, T.at[:, 192 * b:192 * b + 192], T.f2[:, 272 * b:272 * b + 272].indirect(T.ab16[:, 0:12]), ACT.Copy)
+            V("tt", "zt%d" % b, "f2z f2_%d ab16 at%d" % (b, b), T.zt[:, b:768:4], T.f2[:, 272 * b:272 * b + 272].indirect(T.ab16[:, 12:24]), T.at[:, 192 * b:192 * b + 192], A.add)
+        V("qz", "zq zp", "zt0 zt1 zt2 zt3", T.zq[:, 0:192], T.zp[:, 0:192], T.zt[:, 0:768])
+        send(t)
+        V("tt", "d2", "bt ab", T.d2[:, 0:12], T.bt[:, 0:12], T.ab[:, 0:12], A.add)
+        V("cp", "bt16", "d2 cl16", T.bt16[:], T.d2[:, 0:12].indirect(T.cl16[:, 8:9]))
+        V("tt", "ke", "bt16 w512 kk", T.ke[:], T.w512[:, 0:272].indirect(T.bt16[:, 0:12]), T.kk[:], A.add)
+        for c in range(16):
+            S("abd%d" % c, "ke n512 abz", T.abd[:, c, 0:192], T.ke[:], ACT.Abs, bias=T.n512[:, c:c + 1], scale=1.0)
+        V("ts", "li0", "kn", T.li[:, 0:2], T.kn[:, 0:4:2], 15, None, A.bitwise_and)
+        V("ts", "li1", "kn", T.li[:, 2:4], T.kn[:, 0:4:2], 4, None, A.arith_shift_right)
+        V("ts", "li2", "br", T.li[:, 4:6], T.br[:], -256.0, 256.0, A.mult, A.add)
+        V("ts", "li0", "li0", T.li[:, 0:2], T.li[:, 0:2], 16.0, None, A.mult)
+        V("tt", "li1", "li1 li2", T.li[:, 6:8], T.li[:, 2:4], T.li[:, 4:6], A.add)
+        V("cp", "mt", "idw ab16", T.mt[:], T.idw[:, 0:272].indirect(T.ab16[:, 10:12]))
+        V("tt", "li3", "li0 li1", T.li[:, 8:10], T.li[:, 0:2], T.li[:, 6:8], A.add)
+        V("cp", "ln16", "li3", T.ln16[:], T.li[:, 8:10])
+        V("cp", "lt0 lt1", "mt ln16", T.lt[:, 0:560].indirect(T.ln16[:, 0:2]), T.mt[:])
+        dma("y", "dl0", ["lt0"], ["lw"], T.lw[:, 0:16], T.lt[0:128:16, 0:256])
+        dma("y", "dl1", ["lt1"], ["lwb"], T.lw[:, 16:32], T.lt[0:128:16, 256:512])
+        if t == 0:
+            V("qz", "vq vp", "vt", T.vq[:, 0:128], T.vp[:, 0:128], T.vt[:, 0:512])
+        for c in range(16):
+            V("red", "ev%d" % c, "abz abd%d" % c, T.ev[:, c:c + 1], T.abd[:, c, 0:193], XAX, A.min)
+        V("ts", "ei", " ".join("ev%d" % c for c in range(16)), T.ei[:, 0:16], T.ev[:], 32.0, None, A.mult)
+        V("ts", "ek", "ei", T.ei[:, 16:32], T.ei[:, 0:16], 255, None, A.bitwise_and)
+        V("ts", "em", "ei", T.ei[:, 32:48], T.ei[:, 0:16], 8, None, A.arith_shift_right)
+        V("tt", "ex2", "ek em", T.ei[:, 48:64], T.ei[:, 16:32], T.ei[:, 32:48], A.add)
+        V("cp", "e16", "ex2", T.e16[:], T.ei[:, 48:64])
+        if t == R - 1:
+            V("cp", "lw16", "lw lwb", T.lw16[:], T.lw[:])
+        ph = ["ph0", "ph1", "ps1", "ps2"]
+        for b in range(4):
+            mm(ph[b], T.wq[:, 128 * b:128 * b + 128], "wq wp", T.wp[:, 128 * b:128 * b + 128], T["yq%d" % t][:, 0:192], "y%d" % t, T["yp%d" % t][:, 0:192], 192)
+            S("hb%d" % b, ph[b] + " hbz", T.hb[:, 224 * b:224 * b + 192], T[ph[b]][:, 0:192], ACT.Copy, scale=0.03125)
+            V("tt", "xs%d" % b, "hbz hb%d e16 fw%d" % (b, b), T.xs[:, b:1024:4], T.hb[:, 224 * b:224 * b + 224].indirect(T.e16[:, 0:16]), T.fw[:, 256 * b:256 * b + 256], A.add)
+        V("qz", "xq xp", "xs0 xs1 xs2 xs3", T.xq[:, 0:256], T.xp[:, 0:256], T.xs[:, 0:1024])
+        if t < R - 1:
+            lists()
+    S("olr", "idw lw16", T.olr[:], T.idw[:, 0:256].indirect(T.lw16[:, 0:32]), ACT.Copy)
+    dma("y", "ool", ["olr"], [], T.ol[:], T.olr[0:128:16, :])
+    mm("ps1", T.vq[:, 0:128], "vq vp", T.vp[:, 0:128], T.xq[:, 0:256], "xq xp", T.xp[:, 0:256], 256)
+    dma("y", "ooc", ["xq"], [], T.oc[:, 0:1024], T.xq[:, 0:256].bitcast(dt.uint8))
+    for k in range(4):
+        dma("y", "os%d" % k, ["xp"], [], T.osc[4 * k:4 * k + 4, 0:256], T.xp[32 * k:32 * k + 4, 0:256])
+    S("ysb", "ps1", T.ysb[:], T.ps1[:, 0:256], ACT.Copy)
+    dma("s", "oy", ["ysb"], [], T.y[:], T.ysb[:])
+    need("g", [(s, n) for s, n in total.items()])

@@ -4,8 +4,9 @@ from concourse.mybir import dt, AluOpType, ActivationFunctionType, AxisListType
 N = 8
 R = 3
 C = 256
-NS = 11
-BIG = 131072.0
+NS = 9
+NE = 8
+U = 2.0 ** -18
 F32, BF, I32, U16, U8, X4 = "float32", "bfloat16", "int32", "uint16", "uint8", "float8_e4m3fn_x4"
 
 
@@ -14,44 +15,45 @@ def _sb(n, d):
 
 
 SCRATCH = {
-    "xt": _sb(1024, BF), "xs": _sb(1024, BF), "ut": _sb(512, BF), "vt": _sb(512, BF), "et": _sb(2048, BF),
-    "eye": _sb(128, BF), "one": _sb(128, BF),
-    "xq": _sb(256, X4), "xp": _sb(256, U8), "uq": _sb(128, X4), "up": _sb(128, U8), "uq2": _sb(128, X4),
+    "xt": _sb(1024, BF), "xs": _sb(1024, BF), "ut": _sb(512, BF), "vt": _sb(512, BF), "et": _sb(520, BF),
+    "one": _sb(520, BF), "rl16": _sb(32, U16),
+    "uq": _sb(128, X4), "up": _sb(128, U8), "uq2": _sb(128, X4),
     "up2": _sb(128, U8), "vq": _sb(128, X4), "vp": _sb(128, U8), "eq": _sb(512, X4), "ep": _sb(512, U8),
     "wq": _sb(512, X4), "wp": _sb(512, U8),
     "zt": _sb(768, BF), "zq": _sb(192, X4), "zp": _sb(192, U8),
-    "pi": _sb(4, I32), "pf": _sb(4, F32), "sm": _sb(64, F32), "idw": _sb(512, F32), "rp": _sb(256, F32), "nmask": _sb(256, F32),
-    "sc0": _sb(256, F32), "nw": _sb(16, F32), "nT": _sb(256, F32), "nTi": _sb(256, F32), "kk": _sb(192, F32), "rv": _sb(24, F32),
-    "scab": _sb(24, F32), "exl": _sb(16, U16), "upl": _sb(8, U16), "w256": _sb(512, F32), "w2048": _sb(272, F32),
-    "w512": _sb(272, F32), "n512": _sb(16, F32), "nm": _sb(2, F32), "md": _sb(576, F32), "gm": _sb(64, F32),
-    "cl": _sb(160, F32), "cl2": _sb(160, F32), "cl16": _sb(10, U16),
+    "pi": _sb(4, I32), "pf": _sb(16, F32), "sm": _sb(96, F32), "idw": _sb(272, F32), "idb": _sb(272, BF), "rp": _sb(256, F32),
+    "nmask": _sb(256, F32), "sc0": _sb(256, F32), "nw": _sb(64, F32), "nT": _sb(96, F32),
+    "scab": _sb(24, F32), "upl": _sb(8, U16), "w256": _sb(512, F32), "tsel": _sb(272, F32),
+    "dg": _sb(512, BF), "dg1": _sb(80, BF), "cl": _sb(784, BF), "clo": _sb(784, BF),
+    "cl16": _sb(50, U16), "wt": _sb(176, F32), "md": _sb(176, BF), "de": _sb(200, BF), "cm": _sb(2, F32),
     "v0": _sb(256, F32), "a1": _sb(256, F32), "a2": _sb(256, F32), "a3": _sb(256, F32), "a4": _sb(256, F32),
     "asc": _sb(256, F32),
-    "ms": _sb(256, F32), "sc": _sb(256, F32), "ssb": _sb(256, F32), "cf": _sb(48, F32),
-    "wc16": _sb(16, U16), "va": _sb(256, F32), "vb": _sb(256, F32), "pq": _sb(1280, F32),
-    "t3": ("sbuf", [128, 32, 16], F32), "e3": ("sbuf", [128, 16, 36], BF), "e2": _sb(576, BF), "so": _sb(576, F32),
-    "ne": _sb(32, F32), "yv": _sb(16, F32), "ex": _sb(256, F32),
-    "ur": _sb(256, F32), "jk": _sb(4096, BF), "acc": _sb(16, F32), "acc2": _sb(16, F32),
+    "ms": _sb(256, F32), "sc": _sb(256, F32), "ssb": _sb(256, F32), "c0": _sb(32, F32), "c1": _sb(32, F32), "c2": _sb(32, F32),
+    "wc16": _sb(16, U16), "va": _sb(256, F32), "vb": _sb(256, F32), "qp": _sb(256, F32), "pq": _sb(264, F32),
+    "t3": _sb(256, F32), "ab": _sb(72, U16), "la": _sb(72, U16),
+    "f0": _sb(256, BF), "f1": _sb(256, BF), "fo": _sb(256, BF), "scb": _sb(256, BF),
+    "wr": _sb(256, BF), "ur": _sb(256, BF), "jk": _sb(4096, BF), "jo": _sb(4096, BF), "acc": _sb(16, F32), "acc2": _sb(16, F32),
     "a16": _sb(16, U16), "nB": _sb(32, F32), "kap": _sb(256, F32), "r16": _sb(16, U16),
-    "qq": _sb(256, F32), "xk0": _sb(264, F32), "xk1": _sb(264, F32), "kv": _sb(2, F32), "kw": _sb(32, I32),
-    "kn": _sb(16, I32), "off": _sb(4, U16), "g2": _sb(128, F32), "t2": ("sbuf", [128, 8, 16], F32),
-    "w2": ("sbuf", [128, 4, 20], F32), "ij": _sb(24, I32),
-    "ff": _sb(24, F32), "dd": _sb(24, F32), "d2": _sb(24, F32), "ab": _sb(24, F32),
-    "ab16": _sb(32, U16), "br": _sb(2, F32), "dba": _sb(16, F32), "bt": _sb(16, F32), "bt16": _sb(16, U16),
-    "ke": _sb(192, F32), "abd": ("sbuf", [128, 16, 200], F32), "ev": _sb(16, F32), "ei": _sb(64, I32), "e16": _sb(16, U16),
-    "li": _sb(12, I32), "ln16": _sb(2, U16), "mt": _sb(32, I32), "lt": _sb(560, I32), "lw": _sb(32, I32),
-    "lw16": _sb(32, U16), "dl": _sb(16, F32), "olr": _sb(512, F32), "ysb": _sb(256, F32),
-    "at": _sb(768, BF), "f2": _sb(1088, BF), "fw": _sb(1024, BF), "hb": _sb(896, F32),
+    "qq": _sb(256, F32), "qj": _sb(256, F32), "kv": _sb(2, F32), "off": _sb(16, U16), "g2": _sb(64, F32), "t2": _sb(96, F32),
+    "gp": _sb(224, F32), "ee": _sb(176, BF), "so": _sb(224, BF), "nd": _sb(32, F32), "ff": _sb(32, F32), "d2": _sb(24, F32),
+    "abi": _sb(48, F32), "b0": _sb(24, F32), "bti": _sb(24, F32), "bt16": _sb(12, U16),
+    "btv": _sb(192, BF), "btr": _sb(192, BF), "abd": ("sbuf", [128, 16, 200], BF), "abo": ("sbuf", [128, 16, 200], BF),
+    "ei": _sb(64, I32), "e16": _sb(16, U16),
+    "li": _sb(12, F32), "ln16": _sb(2, U16), "m16": _sb(2, U16), "mt": _sb(32, BF), "lt": _sb(544, BF), "lo": _sb(512, BF),
+    "lw": _sb(32, I32), "lw16": _sb(32, U16), "olr": _sb(512, F32),
+    "at": _sb(768, BF), "f2": _sb(1088, BF), "fw": _sb(1024, BF), "hb": _sb(832, F32),
 }
 PS = ["ps1", "ps2", "pd0", "pd1", "pd2", "pd3", "ph0", "ph1"]
-for _t in range(R):
-    SCRATCH["yq%d" % _t] = _sb(192, X4)
-    SCRATCH["yp%d" % _t] = _sb(192, U8)
+for _t in range(R + 1):
+    SCRATCH["xq%d" % _t] = _sb(512, X4)
+    SCRATCH["xp%d" % _t] = _sb(512, U8)
 for _n in PS:
     SCRATCH[_n] = ("psum", [128, 512], F32)
 
-DMAS = ["dx", "du", "dv", "dwc", "dws", "dn0", "dn1", "dlt", "das", "dl0", "dl1", "oy", "ool", "ooc", "os0", "os1", "os2", "os3"]
-SEMAPHORES = ["sv", "ss", "sp", "sg", "lc"] + ["ar%d" % t for t in range(R)] + DMAS
+DMAS = ["dx", "du", "dv", "dwc", "dws", "dn0", "das", "dat", "oy", "ool", "ooc", "os0", "os1", "os2", "os3"]
+SEMAPHORES = ["sv", "ss", "sp", "sg", "lc"] + ["ax%d" % t for t in range(R)] + ["al%d" % t for t in range(R)] + DMAS
+
+LN, LM, LS, LP, LQ, LV, LX, LE = 0, 256, 288, 320, 544, 736, 768, 784
 
 
 def rank_program(g, core, T, topo):
@@ -116,11 +118,12 @@ def rank_program(g, core, T, topo):
     def S(writes, reads, out, in_, func, **kw):
         op("s", reads.split(), writes.split(), "act", out, in_, func, **kw)
 
+    def names(stem, lo, hi):
+        return " ".join(stem + str(c) for c in range(lo, hi))
+
     dma("y", "dx", [], ["xt"], T.xt[:], T.x[:])
     dma("s", "du", [], ["ut"], T.ut[:], T.u[:])
-    dma("y", "dn0", [], ["lw", "lwb"], T.lw[:], T.nb[:])
-    dma("y", "dn1", [], ["lt0"], T.lt[0:128:16, 0:256], T.nb[:, 0:16])
-    dma("y", "dlt", [], ["lt1"], T.lt[0:128:16, 256:512], T.nb[:, 16:32])
+    dma("y", "dn0", [], ["lw"], T.lw[:], T.nb[:])
     dma("y", "dwc", [], ["wq"], T.wq[:, 0:512].bitcast(dt.uint8), T.wc[:])
     dma("y", "dws", [], ["wp"], T.wp[:, 0:512], T.ws[:])
     dma("y", "dv", [], ["vt"], T.vt[:], T.v[:])
@@ -128,72 +131,59 @@ def rank_program(g, core, T, topo):
     def iota(key, out, pattern, base, cm=0):
         kw = {} if key == "pi" else {"allow_small_or_imprecise_dtypes": True}
         op("g", [], [key], "iota", out, pattern, base, cm, **kw)
-    V("memset", "one", "", T.one[:], 1.0)
-    V("memset", "et", "", T.et[:], 0.0)
     iota("pi", T.pi[:, 0:1], [[0, 1]], 0, 1)
-    iota("sm1", T.sm[:, 8:14], [[-1, 6]], 5)
-    iota("sm2", T.sm[:, 16:22], [[1, 6]], 8)
+    iota("sm1", T.sm[:, 8:20], [[8, 2], [-1, 6]], 7)
+    iota("idw", T.idw[:], [[1, 272]], 0)
     iota("sm0", T.sm[:, 0:8], [[16, 8]], 0)
-    op("g", ["one"], ["eye"], "asel", T.eye[:], T.one[:], [[-1, 128]], A.is_equal, 0.0, 0, 1)
-    iota("idw", T.idw[:], [[1, 512]], 0)
     iota("rp", T.rp[:], [[0, 16], [1, 16]], 0)
-    iota("nw0", T.sm[:, 32:48], [[16, 16]], 0)
-    iota("exl0", T.sm[:, 48:64], [[1, 16]], 0)
-    pairs = [(i, s - i) for s in range(10, 0, -1) for i in range(min(5, s), max(0, s - 5) - 1, -1)]
-    worth = [8 * (i + j) + i for i, j in pairs] + [0]
-    iota("md", T.md[:], [[0, 576]], -1)
-    iota("md", T.md[:, 0:576:36], [[0, 16]], -(2 ** 24 - 1))
-    for k in range(len(pairs)):
-        d = worth[k] - worth[k + 1]
-        if d != 1:
-            iota("md", T.md[:, k + 1:576:36], [[0, 16]], -d)
-    iota("nTi", T.nTi[:], [[32, 8], [0, 32]], 1)
-    iota("w256", T.w256[:], [[256, 512]], -65280)
-    iota("w2048", T.w2048[:], [[2048, 272]], 0)
-    iota("sm3", T.sm[:, 24:26], [[16, 2]], 0)
-    iota("xk0", T.xk0[:, 256:264], [[0, 8]], 527)
-    iota("xk1", T.xk1[:, 256:264], [[0, 8]], 783)
-    iota("rv", T.rv[:], [[0, 4], [1, 6]], 0)
-    iota("gm", T.gm[:], [[0, 2], [1, 2], [0, 16]], 0)
-    iota("cl", T.cl[:], [[0, 160]], 0)
-    iota("cl", T.cl[:, 0:16], [[0, 4], [1, 2], [0, 2]], 0)
-    iota("cl", T.cl[:, 32:56], [[0, 2], [1, 2], [0, 6]], 0)
-    iota("cl", T.cl[:, 64:88], [[12, 2], [1, 6], [6, 2]], 0)
-    iota("cl", T.cl[:, 96:108], [[1, 2], [0, 6]], 0)
-    iota("cl", T.cl[:, 128:140], [[1, 6], [6, 2]], 0)
-    iota("pqz", T.pq[:, 512:1280], [[0, 768]], 256)
-    for b in range(4):
-        iota("f2z", T.f2[:, 272 * b + 256:272 * b + 272], [[0, 16]], 0)
-    iota("dbz", T.dba[:, 12:16], [[0, 4]], 0)
-    iota("kk", T.kk[:], [[1, 6], [8, 32]], 0)
-    iota("w512", T.w512[:], [[512, 272]], 0)
-    for b in range(4):
-        iota("hbz", T.hb[:, 224 * b + 192:224 * b + 224], [[0, 32]], 0)
-
+    V("memset", "f0", "", T.f0[:], 0.0)
     V("ts", "pi1", "pi", T.pi[:, 1:2], T.pi[:, 0:1], 15, None, A.bitwise_and)
     V("ts", "pi2", "pi", T.pi[:, 2:3], T.pi[:, 0:1], 31, None, A.bitwise_and)
-    V("ts", "pi3", "pi", T.pi[:, 3:4], T.pi[:, 0:1], 4, 1, A.arith_shift_right, A.bitwise_and)
+    V("ts", "pi3", "pi", T.pi[:, 3:4], T.pi[:, 0:1], 16, None, A.bitwise_and)
     V("cp", "pf", "pi1 pi2 pi3", T.pf[:, 0:3], T.pi[:, 1:4])
-    r16, p32 = T.pf[:, 0:1], T.pf[:, 1:2]
-    V("ts", "sm1", "sm1 pf", T.sm[:, 8:14], T.sm[:, 8:14], r16, None, A.is_equal)
-    V("ts", "sm2", "sm2 pf", T.sm[:, 16:22], T.sm[:, 16:22], r16, None, A.is_equal)
+    r16, p32, odd16 = T.pf[:, 0:1], T.pf[:, 1:2], T.pf[:, 2:3]
+    V("ts", "sm1", "sm1 pf", T.sm[:, 8:20], T.sm[:, 8:20], r16, None, A.is_equal)
+    V("tt", "smS", "sm1", T.sm[:, 24:30], T.sm[:, 8:14], T.sm[:, 14:20], A.add)
+    V("ts", "smB", "sm1", T.sm[:, 32:38], T.sm[:, 8:14], 256.0, None, A.mult)
+    V("memset", "one", "", T.one[:], 1.0)
+    V("memset", "cl", "", T.cl[:, LM:LE], 0.0)
+    V("memset", "c0", "", T.c0[:], 0.0)
     V("cp", "upl", "sm0", T.upl[:], T.sm[:, 0:8])
-    V("tt", "sm1", "sm1 sm2", T.sm[:, 8:14], T.sm[:, 8:14], T.sm[:, 16:22], A.add)
-    for b in range(4):
-        S("et", "eye", T.et[:, 512 * b + b:512 * b + 512:4], T.eye[:], ACT.Copy)
+    for t, k in enumerate(["v0", "a1", "a2", "a3", "a4", "asc"]):
+        S(k + (" asd" if k == "asc" else ""), "idw smS smB", T[k][:], T.idw[:, 0:256], ACT.Identity, scale=T.sm[:, 24 + t:25 + t], bias=T.sm[:, 32 + t:33 + t])
+    V("ts", "pfa", "pf", T.pf[:, 10:11], r16, 8.0, None, A.is_ge)
+    V("ts", "pf5", "pf", T.pf[:, 5:6], r16, 10.0, 256.0, A.is_ge, A.mult)
+    V("ts", "pf3", "pf pfa", T.pf[:, 3:4], r16, 1.0, T.pf[:, 10:11], A.is_equal, A.add)
+    V("ts", "pf6", "pf3", T.pf[:, 6:7], T.pf[:, 3:4], -1.0, 1e29, A.add, A.mult)
+    V("ts", "pf7", "pf", T.pf[:, 7:8], r16, 15.0, 256.0, A.is_lt, A.mult)
+    V("ts", "pf8", "pf", T.pf[:, 8:9], r16, 2.0, 1.0, A.mult, A.add)
+    V("ts", "pf9", "pf", T.pf[:, 9:10], p32, U, None, A.mult)
+    V("tt", "pf4", "pf5 pf6", T.pf[:, 4:5], T.pf[:, 5:6], T.pf[:, 6:7], A.add)
+    fix = T.pf[:, 7:8]
+    V("ts", "dg2", "idw pf", T.dg1[:, 16:33], T.idw[:, 0:17], r16, 1024.0, A.is_equal, A.mult)
+    V("ts", "rl16", "idw pf", T.rl16[:], T.idw[:, 0:32], 0.0, r16, A.mult, A.add)
+    V("ts", "dg3", "dg2", T.dg1[:, 49:64], T.dg1[:, 16:31], -0.25, None, A.mult)
+    V("memset", "dg4", "", T.dg1[:, 48:49], 0.0)
+    V("tt", "dgs", "dg2 dg3 dg4", T.dg1[:, 64:80], T.dg1[:, 16:32], T.dg1[:, 48:64], A.add)
+    S("dg", "dgs rl16", T.dg[:, 0:512], T.dg1[:, 64:80].indirect(T.rl16[:, 0:32]), ACT.Copy)
+    V("ts", "nmask", "rp pf", T.nmask[:], T.rp[:], r16, -1.0, A.is_equal, A.mult)
+    V("ts", "sc0", "rp", T.sc0[:], T.rp[:], 0.0, None, A.not_equal)
     V("qz", "uq up", "ut", T.uq[:, 0:128], T.up[:, 0:128], T.ut[:, 0:512])
     V("cp", "uq2", "uq upl", T.uq2[:, 0:128].bitcast(dt.uint32), T.uq[:, 0:128].bitcast(dt.uint32).indirect(T.upl[:, 0:8]))
     V("cp", "up2", "up upl", T.up2[:, 0:128], T.up[:, 0:128].indirect(T.upl[:, 0:8]))
-    V("qz", "xq xp", "xt", T.xq[:, 0:256], T.xp[:, 0:256], T.xt[:, 0:1024])
-    V("ts", "nmask", "rp pf", T.nmask[:], T.rp[:], r16, -1.0, A.is_equal, A.mult)
-    V("ts", "sc0", "rp", T.sc0[:], T.rp[:], 0.0, None, A.not_equal)
-    for t, k in enumerate(["v0", "a1", "a2", "a3", "a4", "asc"]):
-        S(k, "idw sm1", T[k][:], T.idw[:, 0:256], ACT.Copy, scale=T.sm[:, 8 + t:9 + t])
+    V("qz", "xq0", "xt", T.xq0[:, 0:256], T.xp0[:, 0:256], T.xt[:, 0:1024])
+    V("cp", "lw16", "lw", T.lw16[:], T.lw[:])
+    V("tt", "c0", "lw", T.c0[:, 1:32:2], T.lw[:, 16:32], T.lw[:, 0:16], A.subtract)
+    V("cp", "c1o", "lw", T.c1[:, 1:32:2], T.lw[:, 0:16])
 
-    def lists():
-        V("cp", "lw16", "lw lwb", T.lw16[:], T.lw[:])
-        V("tt", "dl", "lw lwb", T.dl[:], T.lw[:, 16:32], T.lw[:, 0:16], A.subtract)
-    lists()
+    def cli(lo, hi, pattern, base, step=1):
+        iota("cl", T.cl[:, lo:hi:step], pattern, base)
+    iota("cla", T.cl[:, LN:LN + 256], [[2, 16], [-1, 2], [0, 8]], 1)
+    iota("nT", T.nT[:, 0:16], [[32, 8], [0, 2]], 0)
+    iota("f1", T.f1[:], [[0, 256]], 0)
+    iota("f1", T.f1[:, 0:256:16], [[0, 16]], 1)
+    iota("f1", T.f1[:, 1:256:16], [[0, 16]], 1)
+    iota("nw0", T.nw[:, 0:16], [[16, 16]], 0)
 
     def mm(out, st, stk, sc, mv, mvk, mp, n):
         op("p", stk.split() + mvk.split(), [out], "mm", T[out][:, 0:n], st, sc, mv, mp, True, True)
@@ -206,172 +196,230 @@ def rank_program(g, core, T, topo):
         return e[::len(e) // 8]
     emask = sum(1 << k for k in engs(core, dst))
     rid, pid = topo.addr(dst)[:2]
+    nout, nin = len(engs(core, dst)), len(engs(prv, core))
 
-    def send(t):
-        before("g", ["zq", "zp"], [])
-        n = len(engs(core, dst))
-        g.remote_dma(T["yq%d" % t][:, 0:192].bitcast(dt.uint8), T.zq[:, 0:192].bitcast(dt.uint8), T.sem["ar%d" % t], T.sem.lc, pid, rid, emask)
-        g.remote_dma(T["yp%d" % t][:, 0:192], T.zp[:, 0:192], T.sem["ar%d" % t], T.sem.lc, pid, rid, emask)
-        after("g", "lc", 2 * n, ["zq", "zp"], [])
-        m = 2 * len(engs(prv, core))
-        total["ar%d" % t] = m
-        wr["y%d" % t] = ("r", "ar%d" % t, m)
+    def send_x(t):
+        before("g", ["xq%d" % t], [])
+        q, p = T["xq%d" % t], T["xp%d" % t]
+        g.remote_dma(q[:, 256:512].bitcast(dt.uint8), q[:, 0:256].bitcast(dt.uint8), T.sem["ax%d" % t], T.sem.lc, pid, rid, emask)
+        g.remote_dma(p[:, 256:512], p[:, 0:256], T.sem["ax%d" % t], T.sem.lc, pid, rid, emask)
+        total["lc"] = total.get("lc", 0) + 2 * nout
+        total["ax%d" % t] = 2 * nin
+        wr["xn%d" % t] = ("r", "ax%d" % t, 2 * nin)
+
+    def send_lists(t):
+        before("g", ["ab%d" % t], [])
+        g.remote_dma(T.la[:, 24 * t:24 * t + 24], T.ab[:, 24 * t:24 * t + 24], T.sem["al%d" % t], T.sem.lc, pid, rid, emask)
+        total["lc"] = total.get("lc", 0) + nout
+        total["al%d" % t] = nin
+        wr["la%d" % t] = ("r", "al%d" % t, nin)
+
+    def wrap_lists(lo, hi, key):
+        V("scan", "clo" + key, "cla dg" if key == "a" else "cl dg", T.clo[:, lo:hi], T.dg[:, 0:hi - lo], T.cl[:, lo:hi], 0.0, A.add, A.min)
+
+    def more_iotas():
+        cli(LM, LM + 24, [[1, 4], [0, 6]], 0)
+        cli(LM, LM + 24, [[0, 4]], 4, 6)
+        iota("m5c", T.nT[:, 84:88], [[0, 4]], 2)
+        cli(LS, LS + 16, [[0, 4], [1, 2], [0, 2]], 0)
+        cli(LP, LP + 84, [[32, 2], [1, 6], [0, 7]], 2)
+        cli(LP + 84, LP + 168, [[32, 2], [0, 6], [1, 7]], 1)
+        cli(LP + 169, LP + 193, [[8, 2], [32, 2], [1, 6]], 2)
+        cli(LP + 193, LP + 205, [[32, 2], [0, 6]], 0)
+        cli(LQ, LQ + 84, [[32, 2], [0, 6], [1, 7]], 9)
+        cli(LQ + 84, LQ + 168, [[32, 2], [1, 6], [0, 7]], 10)
+        cli(LQ, LQ + 169, [[0, 25]], 65, 7)
+        cli(LV, LV + 24, [[8, 2], [32, 2], [1, 6]], 1)
+        cli(LV, LV + 24, [[0, 4]], 64, 6)
+        cli(LX, LX + 12, [[32, 2], [0, 6]], 1)
+        cli(LP, LP + 169, [[0, 25]], 64, 7)
+        iota("tsz", T.tsel[:, 32:272], [[0, 240]], 0)
+        iota("wt", T.wt[:, 0:168], [[1, 2], [0, 84]], 8)
+        iota("wt", T.wt[:, 1:84:7], [[0, 2], [9, 6]], 0)
+        iota("wt", T.wt[:, 85:168:7], [[0, 2], [8, 6]], 0)
+        iota("wt", T.wt[:, 7:85:7], [[0, 2], [-9, 6]], -40)
+        iota("wt", T.wt[:, 91:169:7], [[0, 2], [-8, 6]], -45)
+        iota("wt", T.wt[:, 1:169:42], [[0, 4]], -256)
+        iota("scab", T.scab[:], [[0, 24]], 1)
+        iota("scab", T.scab[:, 0:24:6], [[0, 4]], 0)
+        op("g", ["one"], ["et"], "asel", T.et[:], T.one[:], [[-1, 520]], A.is_equal, 0.0, 3, 4)
+        iota("t2c", T.t2[:, 64:96], [[0, 2], [0, 16]], 256)
+        iota("t2c", T.t2[:, 65:96:16], [[0, 2]], -5)
+        iota("pqz", T.pq[:, 256:264], [[0, 8]], 512)
+        iota("gpz", T.gp[:, 208:224], [[0, 16]], 0)
+        iota("so", T.so[:, 168:224], [[0, 56]], 2)
+        iota("de", T.de[:], [[0, 200]], -16)
+        iota("de", T.de[:, 16:192:16], [[0, 11]], 239)
+        iota("de", T.de[:, 0:193:192], [[251, 2]], 0)
+        iota("cm", T.cm[:], [[1, 2]], -1)
+        iota("b0", T.b0[:], [[0, 24]], 0)
+        iota("ltz", T.lt[:, 512:544], [[0, 32]], 0)
+        iota("abz", T.abd[:, :, 192], [[0, 16]], 1024)
+        for b in range(4):
+            iota("f2z", T.f2[:, 272 * b + 256:272 * b + 272], [[0, 16]], 0)
+        for b in range(4):
+            iota("hbz", T.hb[:, 208 * b + 192:208 * b + 208], [[0, 16]], 0)
+
+    def mid_constants():
+        S("nT", "nT pf9", T.nT[:, 0:16], T.nT[:, 0:16], ACT.Identity, bias=T.pf[:, 9:10], scale=U)
+        S("scb", "sc0", T.scb[:], T.sc0[:], ACT.Copy)
+        S("w256", "idw", T.w256[:, 0:256], T.idw[:, 0:256], ACT.Identity, scale=256 * U, bias=-255 * 256 * U)
+        S("w256", "idw", T.w256[:, 256:512], T.idw[:, 0:256], ACT.Identity, scale=256 * U, bias=256 * U)
+        S("nw1", "nw0 pf", T.nw[:, 16:32], T.nw[:, 0:16], ACT.Identity, bias=r16, scale=1.0)
+        S("nw2", "nw1", T.nw[:, 32:48], T.nw[:, 16:32], ACT.Identity, bias=-0.5 * U, scale=U)
+    mid_constants()
 
     def late_constants():
-        S("md", "md", T.md[:], T.md[:], ACT.Copy, scale=1.0 / 128)
-        S("nT", "nTi pf", T.nT[:], T.nTi[:], ACT.Identity, bias=p32, scale=1.0)
-        S("nw", "nw0 pf", T.nw[:], T.sm[:, 32:48], ACT.Identity, bias=r16, scale=1.0)
-        S("n512", "nw", T.n512[:], T.nw[:], ACT.Copy, scale=-512.0)
-        S("sm3", "sm3 pf", T.sm[:, 24:26], T.sm[:, 24:26], ACT.Identity, bias=r16, scale=1.0)
-        S("nm", "sm3", T.nm[:], T.sm[:, 24:26], ACT.Copy, scale=-2048.0)
-        S("sm4", "pf", T.sm[:, 28:29], r16, ACT.Copy, scale=16.0)
-        for k in ("xk0", "xk1"):
-            S(k, k + " sm4", T[k][:, 256:264], T[k][:, 256:264], ACT.Identity, bias=T.sm[:, 28:29], scale=1.0)
-        V("cp", "exl", "exl0", T.exl[:], T.sm[:, 48:64])
+        V("ts", "ts2", "idw pf8", T.sm[:, 40:73], T.idw[:, 0:33], T.pf[:, 8:9], -1.0 / U, A.is_equal, A.mult)
+        wrap_lists(LM, LQ, "b")
+        wrap_lists(LQ, LE, "c")
+        V("tt", "tsel", "ts2", T.tsel[:, 0:32], T.sm[:, 41:73], T.sm[:, 40:72], A.subtract)
+        V("ts", "cl16b", "clob pf7", T.cl16[:, LM // 16:LP // 16], T.clo[:, LM + 15:LP:16], fix, None, A.add)
+        V("ts", "cl16c", "clob cloc pf7 pf", T.cl16[:, LP // 16:LE // 16], T.clo[:, LP + 15:LE:16], fix, odd16, A.add, A.add)
 
-    def later_constants():
-        V("ts", "scab", "rv", T.scab[:], T.rv[:], 0.0, None, A.not_equal)
-        V("ts", "gm", "gm pf", T.gm[:], T.gm[:], T.pf[:, 2:3], None, A.is_equal)
-        V("tt", "cl2", "cl nmask", T.cl2[:], T.cl[:], T.nmask[:, 0:160], A.mult)
-        V("scan", "cl", "cl2 sc0", T.cl[:], T.sc0[:, 0:160], T.cl2[:], 0.0, A.mult, A.add)
-        V("ts", "cl16", "cl", T.cl16[:], T.cl[:, 15:160:16], -1.0, None, A.mult)
-        V("memset", "w2z", "", T.w2[:, :, 0], 0.0)
-        V("memset", "abz", "", T.abd[:, :, 192:200], 254.0)
-    V("memset", "e3", "", T.e3[:, :, 0], 0.0)
+    def lst(lo, n):
+        return T.cl16[:, lo // 16:(lo + n) // 16]
 
     for t in range(R):
-        xq, xp = T.xq[:, 0:256], T.xp[:, 0:256]
+        xk = "xq%d" % t
+        xq, xp = T[xk], T["xp%d" % t]
         for k in ("ps1", "ps2"):
-            mm(k, T.uq2[:, 0:128], "uq2 up2", T.up2[:, 0:128], xq, "xq xp", xp, 256)
+            mm(k, T.uq2[:, 0:128], "uq2 up2", T.up2[:, 0:128], xq[:, 0:256], xk, xp[:, 0:256], 256)
+        send_x(t)
         if t == 0:
-            V("qz", "eq ep", "et", T.eq[:, 0:512], T.ep[:, 0:512], T.et[:, 0:2048])
-        for b in range(4):
-            mm("pd%d" % b, T.eq[:, 128 * b:128 * b + 128], "eq ep", T.ep[:, 128 * b:128 * b + 128], xq, "xq xp", xp, 256)
+            more_iotas()
         V("tt", "ms", "ps1 nmask", T.ms[:], T.ps1[:, 0:256], T.nmask[:], A.mult)
         S("ssb", "ps2", T.ssb[:], T.ps2[:, 0:256], ACT.Copy)
-        dma("y", "das", ["ssb"], ["asc"], T.asc[15:128:16, :], T.ssb[15:128:16, :])
+        dma("y", "das", ["ssb"], ["asc"], T.asc[0:128:16, :], T.ssb[0:128:16, :])
+        dma("y", "dat", ["ssb"], ["asd"], T.asc[1:128:16, :], T.ssb[1:128:16, :])
         V("scan", "sc", "ms sc0", T.sc[:], T.sc0[:], T.ms[:], 0.0, A.mult, A.add)
-        V("ts", "cf", "sc", T.cf[:, 0:16], T.sc[:, 15:256:16], 0.0, None, A.is_lt)
-        V("tt", "c1", "cf dl", T.cf[:, 16:32], T.cf[:, 0:16], T.dl[:], A.mult)
-        V("tt", "c2", "c1 lw lwb", T.cf[:, 32:48], T.cf[:, 16:32], T.lw[:, 0:16], A.add)
-        V("cp", "wc16", "c2", T.wc16[:], T.cf[:, 32:48])
-
-        def order(lo, hi):
-            for c in range(lo, hi):
-                S("jk%d acc%d" % (c, c), "ssb sc", T.jk[:, 256 * c:256 * c + 256], T.ssb[:], ACT.Sign, bias=T.sc[:, 16 * c + 15:16 * c + 16], scale=1.0, accum_out=T.acc[:, c:c + 1])
-        order(0, 11)
+        V("ts", "c1e", "sc", T.c1[:, 0:32:2], T.sc[:, 15:256:16], 0.0, None, A.is_lt)
+        V("scan", "c2", "c0 c1e c1o", T.c2[:], T.c0[:], T.c1[:], 0.0, A.mult, A.add)
+        V("cp", "wc16", "c2", T.wc16[:], T.c2[:, 1:32:2])
+        for c in range(16):
+            S("jk%d acc%d" % (c, c), "ssb sc", T.jk[:, 256 * c:256 * c + 256], T.ssb[:], ACT.Sign, bias=T.sc[:, 16 * c + 15:16 * c + 16], scale=1.0, accum_out=T.acc[:, c:c + 1])
         cur = "v0"
         for k, add in enumerate(["a1", "a2", "a3", "a4", "asc"]):
             nxt = "va" if k % 2 == 0 else "vb"
-            V("tt", nxt, cur + " wc16 " + add, T[nxt][:], T[cur][:, 0:256].indirect(T.wc16[:, 0:16]), T[add][:], A.add)
+            V("tt", nxt, cur + " wc16 asd " + add if k == 4 else cur + " wc16 " + add, T[nxt][:], T[cur][:, 0:256].indirect(T.wc16[:, 0:16]), T[add][:], A.add)
             cur = nxt
-        V("cp", "pq0", cur + " lw16", T.pq[:, 0:256], T[cur][:, 0:256].indirect(T.lw16[:, 0:16]))
-        S("pq1", cur + " lw16", T.pq[:, 256:512], T[cur][:, 0:256].indirect(T.lw16[:, 16:32]), ACT.Copy)
-        order(11, 16)
-        V("tr", "t3", "pq0 pq1", T.t3[:], T.pq[:, 0:512])
-        if t == 0:
-            late_constants()
-        k = 1
-        for s in range(10, 0, -1):
-            hi, lo = min(5, s), max(0, s - 5)
-            n = hi - lo + 1
-            V("tt", "e3_%d" % s, "t3 e3", T.e3[:, :, k:k + n], T.t3[:, 0:16, 13 - hi:14 - lo], T.t3[:, 16:32, s - hi:s - lo + 1], A.is_equal)
-            k += n
-        V("tt", "ne", "t3", T.ne[:, 0:16], T.t3[:, 0:16, 0], T.t3[:, 16:32, 0], A.is_equal)
-        V("ts", "e2", "e3 " + " ".join("e3_%d" % s for s in range(1, 11)), T.e2[:], T.e3[:], BIG, 1.0 - BIG, A.mult, A.add)
-        V("ts", "neb", "ne", T.ne[:, 16:32], T.ne[:, 0:16], BIG, None, A.mult)
-        V("scan", "so", "e2 md", T.so[:], T.e2[:], T.md[:], -BIG, A.max, A.add)
-        accs = " ".join("acc%d" % c for c in range(16))
-        V("tt", "yv", "neb so", T.yv[:], T.ne[:, 16:32], T.so[:, 35:576:36], A.subtract)
-        V("tt", "ex", "yv exl nT", T.ex[:], T.yv[:, 0:16].indirect(T.exl[:, 0:16]), T.nT[:], A.add)
-        V("tr", "ur", "ex", T.ur[:], T.ex[:])
+            if t == 0 and k == 3:
+                wrap_lists(LN, LM, "a")
+                V("ts", "cl16a", "cloa pf7", T.cl16[:, 0:LM // 16], T.clo[:, 15:LM:16], fix, None, A.add)
+        V("ts", "qp", cur + " lw16 pf3 pf4", T.qp[:], T[cur][:, 0:256].indirect(T.lw16[:, 16:32]), T.pf[:, 3:4], T.pf[:, 4:5], A.mult, A.add)
+        V("tt", "pq", cur + " lw16 qp", T.pq[:, 0:256], T[cur][:, 0:256].indirect(T.lw16[:, 0:16]), T.qp[:], A.max)
+        V("tr", "t3", "pq", T.t3[:], T.pq[:, 0:256])
+        V("cp", "t5", "t3", T.nT[:, 48:80], T.t3[:, 7:256:8])
+        V("tt", "f1k", "t3", T.nT[:, 16:32], T.t3[:, 2:256:16], T.t3[:, 10:256:16], A.is_equal)
+        V("tt", "ur", "t3 t5 cl16a", T.ur[:], T.nT[:, 48:80].indirect(lst(LN, 256)), T.t3[:], A.not_equal)
+        V("scan", "wr", "ur f1", T.wr[:], T.ur[:], T.f1[:], 1.0, A.min, A.max)
+        V("tt", "f1m", "f1k nT", T.nT[:, 32:48], T.nT[:, 16:32], T.nT[:, 0:16], A.max)
+        V("tt", "f0", "wr f1m", T.f0[:, 0:256:16], T.wr[:, 15:256:16], T.nT[:, 32:48], A.max)
+        V("scan", "fo", "f0 scb", T.fo[:], T.scb[:], T.f0[:], 0.0, A.mult, A.add)
+        V("tr", "wr", "fo", T.wr[:], T.fo[:])
+        accs = names("acc", 0, 16)
         V("ts", "a16", accs, T.a16[:], T.acc[:], 255.0, None, A.add)
-        V("ts", "nb0", accs, T.nB[:, 16:32], T.acc[:], -256.0, None, A.mult)
-        V("tt", "kap", "a16 w256 ur", T.kap[:], T.w256[:, 0:512].indirect(T.a16[:, 0:16]), T.ur[:], A.add)
-        V("tt", "nB", "nb0 nw", T.nB[:, 0:16], T.nB[:, 16:32], T.nw[:], A.subtract)
+        V("ts", "nb0", accs, T.nB[:, 16:32], T.acc[:], -256.0 * U, None, A.mult)
+        V("tt", "kap", "a16 w256 wr", T.kap[:], T.w256[:, 0:512].indirect(T.a16[:, 0:16]), T.wr[:], A.add)
+        V("tt", "nB", "nb0 nw2", T.nB[:, 0:16], T.nB[:, 16:32], T.nw[:, 32:48], A.subtract)
         for c in range(NS):
             S("jk%d rk%d" % (c, c), "kap nB", T.jk[:, 256 * c:256 * c + 256], T.kap[:], ACT.Sign, bias=T.nB[:, c:c + 1], scale=1.0, accum_out=T.acc2[:, c:c + 1])
         for c in range(NS, 16):
             V("ts", "jk%d" % c, "kap nB", T.jk[:, 256 * c:256 * c + 256], T.kap[:], T.nB[:, c:c + 1], 0.0, A.add, A.is_lt)
         for c in range(NS, 16):
-            V("red", "rk%d" % c, "jk%d" % c, T.acc2[:, c:c + 1], T.jk[:, 256 * c:256 * c + 256], XAX, A.add)
-        V("cp", "r16b", " ".join("rk%d" % c for c in range(NS, 16)), T.r16[:, NS:16], T.acc2[:, NS:16])
+            j = T.jk[:, 256 * c:256 * c + 256]
+            V("scan", "rk%d" % c, "jk%d" % c, T.jo[:, 256 * c:256 * c + 256], j, j, 0.0, A.add, A.max)
+        V("ts", "ur", "wr", T.ur[:], T.wr[:], 256 * U, 256 * U, A.min, A.subtract)
+        V("cp", "r16b", names("rk", NS, 16), T.r16[:, NS:16], T.jo[:, 256 * NS + 255:4096:256])
         if t == 0:
-            later_constants()
-        V("ts", "r16a", " ".join("rk%d" % c for c in range(NS)), T.r16[:, 0:NS], T.acc2[:, 0:NS], -0.5, 128.0, A.mult, A.add)
-        V("tt", "qq", "r16a r16b w2048 ur", T.qq[:], T.w2048[:, 0:272].indirect(T.r16[:, 0:16]), T.ur[:], A.add)
-        S("xk1a", "qq nm", T.xk1[:, 0:256], T.qq[:], ACT.Identity, bias=T.nm[:, 1:2], scale=1.0)
-        V("ts", "xk0a", "qq nm", T.xk0[:, 0:256], T.qq[:], T.nm[:, 0:1], None, A.add)
-        V("red", "kv0", "xk0 xk0a", T.kv[:, 0:1], T.xk0[:, 0:264], XAX, A.min, apply_absolute_value=True)
-        V("red", "kv1", "xk1 xk1a", T.kv[:, 1:2], T.xk1[:, 0:264], XAX, A.min, apply_absolute_value=True)
+            late_constants()
+            for b in range(4):
+                V("qz", "eq%d" % b, "et", T.eq[:, 128 * b:128 * b + 128], T.ep[:, 128 * b:128 * b + 128], T.et[:, 3 - b:515 - b])
         for b in range(4):
-            S("f2_%d" % b, "pd%d f2z" % b, T.f2[:, 272 * b:272 * b + 256], T["pd%d" % b][:, 0:256], ACT.Copy, scale=0.5)
+            mm("pd%d" % b, T.eq[:, 128 * b:128 * b + 128], "eq%d" % b, T.ep[:, 128 * b:128 * b + 128], xq[:, 0:512], xk + " xn%d" % t, xp[:, 0:512], 512)
+        V("ts", "r16a", names("rk", 0, NS), T.r16[:, 0:NS], T.acc2[:, 0:NS], -0.5, 128.0, A.mult, A.add)
+        V("tt", "qq", "r16a r16b tsel tsz ur", T.qq[:], T.tsel[:, 0:272].indirect(T.r16[:, 0:16]), T.ur[:], A.mult)
+        if t == 0:
+            S("md", "wt", T.md[:, 0:169], T.wt[:, 0:169], ACT.Copy, scale=1.0 / 128)
+            S("idb", "idw", T.idb[:], T.idw[:], ACT.Copy)
+            S("cm", "cm pf8", T.cm[:], T.cm[:], ACT.Identity, bias=T.pf[:, 8:9], scale=1.0)
+            S("nw3", "nw1", T.nw[:, 48:64], T.nw[:, 16:32], ACT.Copy, scale=-1024.0)
+            S("lt", "idb lw16", T.lt[:, 0:512], T.idb[:, 0:272].indirect(T.lw16[:, 0:32]), ACT.Copy)
+        S("kv1", "qq", T.qj[:], T.qq[:], ACT.Relu, scale=-1.0, accum_out=T.kv[:, 1:2])
+        V("red", "kv0", "qq", T.kv[:, 0:1], T.qq[:], XAX, A.max)
+        S("li0", "kv0 kv1", T.li[:, 0:2], T.kv[:], ACT.Identity, bias=512.0, scale=-1.0)
+        S("li1", "kv0 kv1", T.li[:, 2:4], T.kv[:], ACT.Relu, bias=1.0, scale=-1.0)
+        for h in range(2):
+            S("li2%d" % h, "li0 li1 cm", T.li[:, 4 + h:5 + h], T.li[:, 2 + h:3 + h], ACT.Identity, bias=T.li[:, h:h + 1], scale=T.cm[:, h:h + 1])
+        V("ts", "off", "kv0 kv1 cl16b", T.off[:], T.kv[:, 0:2].indirect(lst(LS, 16)), -1.0, 256.0, A.mult, A.add)
+        V("cp", "g2", "pqz pq off", T.g2[:], T.pq[:, 0:264].indirect(T.off[:, 0:4]))
+        V("tr", "t2", "g2", T.t2[:, 0:64], T.g2[:])
+        t2 = T.t2[:, 0:96]
+        V("cp", "gp", "t2 t2c cl16c", T.gp[:, 0:208], t2.indirect(lst(LP, 208)))
+        V("tt", "ee", "t2 t2c cl16c gp", T.ee[:], t2.indirect(lst(LQ, 176)), T.gp[:, 0:176], A.is_equal)
+        V("tt", "nd", "t2 t2c cl16c gp", T.nd[:], t2.indirect(lst(LV, 32)), T.gp[:, 169:201], A.subtract)
+        V("scan", "so", "ee md", T.so[:, 0:169], T.md[:, 0:169], T.ee[:, 0:169], 0.0, A.add, A.max)
+        V("tt", "br", "t2 t2c cl16c gp gpz abo_", T.abi[:, 0:32:2], t2.indirect(lst(LX, 16)), T.gp[:, 193:209], A.is_gt)
+        V("cp", "m5", "so", T.nT[:, 80:84], T.so[:, 42:169:42])
+        V("tt", "ff", "so m5 m5c cl16b", T.ff[:], T.nT[:, 80:88].indirect(lst(LM, 32)), T.so[:, 0:224:7], A.is_gt)
+        V("tt", "d2", "nd ff", T.d2[:], T.nd[:, 0:24], T.ff[:, 0:24], A.mult)
+        V("scan", "ab", "d2 scab br", T.abi[:, 1:48:2], T.scab[:], T.d2[:], 0.0, A.mult, A.subtract)
+        V("cp", "ab%d" % t, "ab", T.ab[:, 24 * t:24 * t + 24], T.abi[:, 1:48:2])
+        send_lists(t)
+        for b in range(4):
+            S("f2_%d" % b, "pd%d f2z" % b, T.f2[:, 272 * b:272 * b + 256], T["pd%d" % b][:, 256:512], ACT.Copy, scale=0.5)
+        V("tt", "b0", "ab b0", T.b0[:, 1:24:2], T.abi[:, 25:48:2], T.abi[:, 1:24:2], A.subtract)
+        V("cp", "m16", "ab", T.m16[:], T.abi[:, 11:24:12])
+        V("scan", "bti", "b0 ab br", T.bti[:], T.b0[:], T.abi[:, 0:24], 0.0, A.mult, A.add)
+        V("cp", "bt16", "bti", T.bt16[:], T.bti[:, 1:24:2])
+        S("btr", "idb bt16", T.btr[:], T.idb[:, 0:272].indirect(T.bt16[:, 0:12]), ACT.Copy)
+        V("cp", "btv", "idb bt16", T.btv[:], T.idb[:, 0:272].indirect(T.bt16[:, 0:12]))
+        for c in range(NE):
+            S("abd%d" % c, "btr nw3", T.abd[:, c, 0:192], T.btr[:], ACT.Abs, bias=T.nw[:, 48 + c:49 + c], scale=1024.0)
+        for c in range(NE, 16):
+            V("ts", "abd%d" % c, "btv nw1", T.abd[:, c, 0:192], T.btv[:], T.nw[:, 16 + c:17 + c], 1024.0, A.not_equal, A.mult)
+        for c in list(range(NE, 16)) + list(range(NE)):
+            V("scan", "ev%d" % c, "abz de abd%d" % c, T.abo[:, c, 0:193], T.de[:, 0:193], T.abd[:, c, 0:193], 252.0, A.add, A.min)
+        for b in range(4):
+            w = T.f2[:, 272 * b:272 * b + 272]
+            S("at%d" % b, "f2z f2_%d la%d" % (b, t), T.at[:, 192 * b:192 * b + 192], w.indirect(T.la[:, 24 * t:24 * t + 12]), ACT.Copy)
+        V("ts", "ei", names("ev", 0, 16), T.ei[:, 0:16], T.abo[:, :, 192], 16.0, None, A.mult)
+        for b in range(4):
+            w = T.f2[:, 272 * b:272 * b + 272]
+            V("tt", "zt%d" % b, "f2z f2_%d la%d at%d" % (b, t, b), T.zt[:, b:768:4], w.indirect(T.la[:, 24 * t + 12:24 * t + 24]), T.at[:, 192 * b:192 * b + 192], A.add)
+        for h in range(2):
+            S("li3%d" % h, "br li2%d" % h, T.li[:, 6 + h:7 + h], T.abi[:, 12 * h:12 * h + 1], ACT.Identity, bias=T.li[:, 4 + h:5 + h], scale=-256.0)
+        S("mt", "idb m16", T.mt[:], T.idb[:, 0:272].indirect(T.m16[:, 0:2]), ACT.Copy)
         for b in range(4):
             S("fw%d" % b, "pd%d" % b, T.fw[:, 256 * b:256 * b + 256], T["pd%d" % b][:, 0:256], ACT.Copy)
-        V("ts", "kn", "kv0 kv1 cl16", T.kn[:], T.kv[:, 0:2].indirect(T.cl16[:, 0:1]), -0.34, None, A.add)
-        V("ts", "kw", "kv0 kv1 cl16", T.kw[:], T.kv[:, 0:2].indirect(T.cl16[:, 2:4]), 128.0, None, A.mult)
-        V("cp", "off", "kn", T.off[:], T.kn[:, 0:4])
-        V("ts", "ij", "kw", T.ij[:], T.kw[:, 0:24], 7, None, A.bitwise_and)
-        for kind in range(2):
-            V("tt", "g2_%d" % kind, "pqz pq0 pq1 off gm", T.g2[:, 64 * kind:64 * kind + 64], T.pq[:, 256 * kind:256 * kind + 1024].indirect(T.off[:, 0:4]), T.gm[:], A.mult)
-        V("ts", "ei ek", "kw", T.ei[:, 0:24], T.kw[:, 0:24], 3, 15, A.arith_shift_right, A.bitwise_and)
-        V("tr", "t2", "g2_0 g2_1", T.t2[:], T.g2[:])
-        V("tt", "ij", "ei ij", T.ij[:, 12:24], T.ei[:, 12:24], T.ij[:, 12:24], A.subtract)
-        V("tt", "w2", "t2", T.w2[:, :, 1:17], T.t2[:, 0:8:2, :], T.t2[:, 1:8:2, :], A.add)
-        V("tt", "ff", "rv ij", T.ff[:], T.ij[:], T.rv[:], A.is_ge)
-        V("tt", "dd", "w2 w2z", T.dd[:], T.w2[:, :, 1:7], T.w2[:, :, 0:6], A.subtract)
-        V("tt", "d2", "dd ff", T.d2[:], T.dd[:], T.ff[:], A.mult)
-        V("scan", "ab", "d2 scab", T.ab[:], T.scab[:], T.d2[:], 0.0, A.mult, A.add)
-        V("cp", "ab16", "ab cl16", T.ab16[:], T.ab[:, 0:24].indirect(T.cl16[:, 4:6]))
-        V("tt", "br", "w2", T.br[:], T.w2[:, 2:4, 16], T.w2[:, 0:2, 16], A.is_gt)
-        V("tt", "dba", "ab", T.dba[:, 0:12], T.ab[:, 12:24], T.ab[:, 0:12], A.subtract)
-        V("tt", "bt", "dbz dba br cl16", T.bt[:], T.br[:, 0:2].indirect(T.cl16[:, 6:7]), T.dba[:], A.mult)
-        for b in range(4):
-            S("at%d" % b, "f2z f2_%d ab16" % b, T.at[:, 192 * b:192 * b + 192], T.f2[:, 272 * b:272 * b + 272].indirect(T.ab16[:, 0:12]), ACT.Copy)
-            V("tt", "zt%d" % b, "f2z f2_%d ab16 at%d" % (b, b), T.zt[:, b:768:4], T.f2[:, 272 * b:272 * b + 272].indirect(T.ab16[:, 12:24]), T.at[:, 192 * b:192 * b + 192], A.add)
         V("qz", "zq zp", "zt0 zt1 zt2 zt3", T.zq[:, 0:192], T.zp[:, 0:192], T.zt[:, 0:768])
-        send(t)
-        V("tt", "d2", "bt ab", T.d2[:, 0:12], T.bt[:, 0:12], T.ab[:, 0:12], A.add)
-        V("cp", "bt16", "d2 cl16", T.bt16[:], T.d2[:, 0:12].indirect(T.cl16[:, 8:9]))
-        V("tt", "ke", "bt16 w512 kk", T.ke[:], T.w512[:, 0:272].indirect(T.bt16[:, 0:12]), T.kk[:], A.add)
-        for c in range(16):
-            S("abd%d" % c, "ke n512 abz", T.abd[:, c, 0:192], T.ke[:], ACT.Abs, bias=T.n512[:, c:c + 1], scale=1.0)
-        V("ts", "li0", "kn", T.li[:, 0:2], T.kn[:, 0:4:2], 15, None, A.bitwise_and)
-        V("ts", "li1", "kn", T.li[:, 2:4], T.kn[:, 0:4:2], 4, None, A.arith_shift_right)
-        V("ts", "li2", "br", T.li[:, 4:6], T.br[:], -256.0, 256.0, A.mult, A.add)
-        V("ts", "li0", "li0", T.li[:, 0:2], T.li[:, 0:2], 16.0, None, A.mult)
-        V("tt", "li1", "li1 li2", T.li[:, 6:8], T.li[:, 2:4], T.li[:, 4:6], A.add)
-        V("cp", "mt", "idw ab16", T.mt[:], T.idw[:, 0:272].indirect(T.ab16[:, 10:12]))
-        V("tt", "li3", "li0 li1", T.li[:, 8:10], T.li[:, 0:2], T.li[:, 6:8], A.add)
-        V("cp", "ln16", "li3", T.ln16[:], T.li[:, 8:10])
-        V("cp", "lt0 lt1", "mt ln16", T.lt[:, 0:560].indirect(T.ln16[:, 0:2]), T.mt[:])
-        dma("y", "dl0", ["lt0"], ["lw"], T.lw[:, 0:16], T.lt[0:128:16, 0:256])
-        dma("y", "dl1", ["lt1"], ["lwb"], T.lw[:, 16:32], T.lt[0:128:16, 256:512])
-        if t == 0:
-            V("qz", "vq vp", "vt", T.vq[:, 0:128], T.vp[:, 0:128], T.vt[:, 0:512])
-        for c in range(16):
-            V("red", "ev%d" % c, "abz abd%d" % c, T.ev[:, c:c + 1], T.abd[:, c, 0:193], XAX, A.min)
-        V("ts", "ei", " ".join("ev%d" % c for c in range(16)), T.ei[:, 0:16], T.ev[:], 32.0, None, A.mult)
         V("ts", "ek", "ei", T.ei[:, 16:32], T.ei[:, 0:16], 255, None, A.bitwise_and)
         V("ts", "em", "ei", T.ei[:, 32:48], T.ei[:, 0:16], 8, None, A.arith_shift_right)
+        V("cp", "ln16", "li30 li31", T.ln16[:], T.li[:, 6:8])
         V("tt", "ex2", "ek em", T.ei[:, 48:64], T.ei[:, 16:32], T.ei[:, 32:48], A.add)
+        V("cp", "lt", "mt ln16 ltz", T.lt[:, 0:544].indirect(T.ln16[:, 0:2]), T.mt[:])
         V("cp", "e16", "ex2", T.e16[:], T.ei[:, 48:64])
-        if t == R - 1:
-            V("cp", "lw16", "lw lwb", T.lw16[:], T.lw[:])
         ph = ["ph0", "ph1", "ps1", "ps2"]
         for b in range(4):
-            mm(ph[b], T.wq[:, 128 * b:128 * b + 128], "wq wp", T.wp[:, 128 * b:128 * b + 128], T["yq%d" % t][:, 0:192], "y%d" % t, T["yp%d" % t][:, 0:192], 192)
-            S("hb%d" % b, ph[b] + " hbz", T.hb[:, 224 * b:224 * b + 192], T[ph[b]][:, 0:192], ACT.Copy, scale=0.03125)
-            V("tt", "xs%d" % b, "hbz hb%d e16 fw%d" % (b, b), T.xs[:, b:1024:4], T.hb[:, 224 * b:224 * b + 224].indirect(T.e16[:, 0:16]), T.fw[:, 256 * b:256 * b + 256], A.add)
-        V("qz", "xq xp", "xs0 xs1 xs2 xs3", T.xq[:, 0:256], T.xp[:, 0:256], T.xs[:, 0:1024])
+            mm(ph[b], T.wq[:, 128 * b:128 * b + 128], "wq wp", T.wp[:, 128 * b:128 * b + 128], T.zq[:, 0:192], "zq zp", T.zp[:, 0:192], 192)
+            S("hb%d" % b, ph[b] + " hbz", T.hb[:, 208 * b:208 * b + 192], T[ph[b]][:, 0:192], ACT.Copy, scale=0.03125)
+            V("tt", "xs%d" % b, "hbz hb%d e16 fw%d" % (b, b), T.xs[:, b:1024:4], T.hb[:, 208 * b:208 * b + 208].indirect(T.e16[:, 0:16]), T.fw[:, 256 * b:256 * b + 256], A.add)
+        V("qz", "xq%d" % (t + 1), "xs0 xs1 xs2 xs3", T["xq%d" % (t + 1)][:, 0:256], T["xp%d" % (t + 1)][:, 0:256], T.xs[:, 0:1024])
         if t < R - 1:
-            lists()
-    S("olr", "idw lw16", T.olr[:], T.idw[:, 0:256].indirect(T.lw16[:, 0:32]), ACT.Copy)
+            V("scan", "lo", "lt dg", T.lo[:], T.dg[:, 0:512], T.lt[:, 0:512], 0.0, A.add, A.min)
+            V("ts", "lw16", "lo pf7", T.lw16[:], T.lo[:, 15:512:16], fix, None, A.add)
+            V("ts", "c1o", "lo pf7", T.c1[:, 1:32:2], T.lo[:, 15:256:16], fix, None, A.add)
+            V("tt", "c0", "lo", T.c0[:, 1:32:2], T.lo[:, 271:512:16], T.lo[:, 15:256:16], A.subtract)
+        if t == 0:
+            V("qz", "vq vp", "vt", T.vq[:, 0:128], T.vp[:, 0:128], T.vt[:, 0:512])
+    xk = "xq%d" % R
+    xq, xp = T[xk], T["xp%d" % R]
+    S("olr", "lt", T.olr[:], T.lt[:, 0:512], ACT.Copy)
     dma("y", "ool", ["olr"], [], T.ol[:], T.olr[0:128:16, :])
-    mm("ps1", T.vq[:, 0:128], "vq vp", T.vp[:, 0:128], T.xq[:, 0:256], "xq xp", T.xp[:, 0:256], 256)
-    dma("y", "ooc", ["xq"], [], T.oc[:, 0:1024], T.xq[:, 0:256].bitcast(dt.uint8))
+    mm("ps1", T.vq[:, 0:128], "vq vp", T.vp[:, 0:128], xq[:, 0:256], xk, xp[:, 0:256], 256)
+    dma("y", "ooc", [xk], [], T.oc[:, 0:1024], xq[:, 0:256].bitcast(dt.uint8))
     for k in range(4):
-        dma("y", "os%d" % k, ["xp"], [], T.osc[4 * k:4 * k + 4, 0:256], T.xp[32 * k:32 * k + 4, 0:256])
-    S("ysb", "ps1", T.ysb[:], T.ps1[:, 0:256], ACT.Copy)
-    dma("s", "oy", ["ysb"], [], T.y[:], T.ysb[:])
+        dma("y", "os%d" % k, [xk], [], T.osc[4 * k:4 * k + 4, 0:256], xp[32 * k:32 * k + 4, 0:256])
+    S("kv1", "ps1", T.qj[:], T.ps1[:, 0:256], ACT.Copy)
+    dma("s", "oy", ["kv1"], [], T.y[:], T.qj[:])
     need("g", [(s, n) for s, n in total.items()])

@@ -7,6 +7,7 @@ C = 256
 NS = 9
 NE = 8
 U = 2.0 ** -18
+CYC, LAT, DMA, NEAR, FAR, SLACK = 0.9, 200.0, 2100.0, 2200.0, 3500.0, 100.0
 F32, BF, I32, U16, U8, X4 = "float32", "bfloat16", "int32", "uint16", "uint8", "float8_e4m3fn_x4"
 
 
@@ -22,22 +23,21 @@ SCRATCH = {
     "wq": _sb(512, X4), "wp": _sb(512, U8),
     "zt": _sb(768, BF), "zq": _sb(192, X4), "zp": _sb(192, U8),
     "pi": _sb(4, I32), "pf": _sb(16, F32), "sm": _sb(96, F32), "idw": _sb(272, F32), "idb": _sb(272, BF), "rp": _sb(256, F32),
-    "nmask": _sb(256, F32), "sc0": _sb(256, F32), "nw": _sb(64, F32), "nT": _sb(96, F32),
+    "nmask": _sb(256, F32), "thr": _sb(256, F32), "sc0": _sb(256, F32), "nw": _sb(64, F32), "nT": _sb(96, F32),
     "scab": _sb(24, F32), "upl": _sb(8, U16), "w256": _sb(512, F32), "tsel": _sb(272, F32),
     "dg": _sb(512, BF), "dg1": _sb(80, BF), "cl": _sb(784, BF), "clo": _sb(784, BF),
     "cl16": _sb(50, U16), "wt": _sb(176, F32), "md": _sb(176, BF), "de": _sb(200, BF), "cm": _sb(2, F32),
-    "v0": _sb(256, F32), "a1": _sb(256, F32), "a2": _sb(256, F32), "a3": _sb(256, F32), "a4": _sb(256, F32),
-    "asc": _sb(256, F32),
-    "ms": _sb(256, F32), "sc": _sb(256, F32), "ssb": _sb(256, F32), "c0": _sb(32, F32), "c1": _sb(32, F32), "c2": _sb(32, F32),
+    "aa": _sb(1280, F32), "asc": _sb(256, F32),
+    "ms": _sb(256, F32), "sc": _sb(256, F32), "ssb": _sb(256, F32), "c0": _sb(512, BF), "c1": _sb(512, BF), "c2": _sb(512, BF),
     "wc16": _sb(16, U16), "va": _sb(256, F32), "vb": _sb(256, F32), "qp": _sb(256, F32), "pq": _sb(264, F32),
     "t3": _sb(256, F32), "ab": _sb(72, U16), "la": _sb(72, U16),
     "f0": _sb(256, BF), "f1": _sb(256, BF), "fo": _sb(256, BF), "scb": _sb(256, BF),
     "wr": _sb(256, BF), "ur": _sb(256, BF), "jk": _sb(4096, BF), "jo": _sb(4096, BF), "acc": _sb(16, F32), "acc2": _sb(16, F32),
     "a16": _sb(16, U16), "nB": _sb(32, F32), "kap": _sb(256, F32), "r16": _sb(16, U16),
     "qq": _sb(256, F32), "qj": _sb(256, F32), "kv": _sb(2, F32), "off": _sb(16, U16), "g2": _sb(64, F32), "t2": _sb(96, F32),
-    "gp": _sb(224, F32), "ee": _sb(176, BF), "so": _sb(224, BF), "nd": _sb(32, F32), "ff": _sb(32, F32), "d2": _sb(24, F32),
+    "gp": _sb(224, F32), "ee": _sb(176, BF), "so": _sb(176, BF), "nd": _sb(32, F32), "ff": _sb(24, F32), "d2": _sb(24, F32),
     "abi": _sb(48, F32), "b0": _sb(24, F32), "bti": _sb(24, F32), "bt16": _sb(12, U16),
-    "btv": _sb(192, BF), "btr": _sb(192, BF), "abd": ("sbuf", [128, 16, 200], BF), "abo": ("sbuf", [128, 16, 200], BF),
+    "btv": _sb(192, BF), "abd": ("sbuf", [128, 16, 200], BF), "abo": ("sbuf", [128, 16, 200], BF),
     "ei": _sb(64, I32), "e16": _sb(16, U16),
     "li": _sb(12, F32), "ln16": _sb(2, U16), "m16": _sb(2, U16), "mt": _sb(32, BF), "lt": _sb(544, BF), "lo": _sb(512, BF),
     "lw": _sb(32, I32), "lw16": _sb(32, U16), "olr": _sb(512, F32),
@@ -53,7 +53,46 @@ for _n in PS:
 DMAS = ["dx", "du", "dv", "dwc", "dws", "dn0", "das", "dat", "oy", "ool", "ooc", "os0", "os1", "os2", "os3"]
 SEMAPHORES = ["sv", "ss", "sp", "sg", "lc"] + ["ax%d" % t for t in range(R)] + ["al%d" % t for t in range(R)] + DMAS
 
-LN, LM, LS, LP, LQ, LV, LX, LE = 0, 256, 288, 320, 544, 736, 768, 784
+LN, LS, LP, LQ, LV, LX, LE = 0, 256, 288, 512, 704, 736, 752
+
+
+def width(ap):
+    return int(np.prod([int(k) for k in ap.shape[1:]]))
+
+
+def in_order(calls):
+    n = len(calls)
+    after = [[] for _ in calls]
+    for i, c in enumerate(calls):
+        for d in c["deps"]:
+            after[d].append(i)
+    chain = [0.0] * n
+    for i in range(n - 1, -1, -1):
+        chain[i] = calls[i]["len"] + max([LAT + chain[k] for k in after[i]] + [0.0])
+    left = [len(c["deps"]) for c in calls]
+    ready = {i: 0.0 for i in range(n) if left[i] == 0}
+    free, order = {}, []
+    while ready:
+        start = {i: max(t, free.get(calls[i]["q"], 0.0)) for i, t in ready.items()}
+        first = min(start, key=lambda i: (start[i], i))
+        q = calls[first]["q"]
+        best = first
+        for i in ready:
+            if calls[i]["q"] == q and chain[i] > chain[best] and start[i] <= start[first] + max(0.0, min(calls[first]["hold"] - SLACK, chain[i] - chain[first])):
+                best = i
+        if q is None:
+            best = first
+        order.append(best)
+        t = start[best]
+        del ready[best]
+        if q is not None:
+            free[q] = t + calls[best]["hold"]
+        calls[best]["end"] = t + calls[best]["len"]
+        for k in after[best]:
+            left[k] -= 1
+            if left[k] == 0:
+                ready[k] = max(calls[d]["end"] + LAT for d in calls[k]["deps"])
+    return order
 
 
 def rank_program(g, core, T, topo):
@@ -64,53 +103,57 @@ def rank_program(g, core, T, topo):
     ACT = ActivationFunctionType
     XAX = AxisListType.X
     queues = {"v": g.vector, "s": g.scalar, "p": g.tensor, "g": g, "y": g.sync}
-    total, waited, wr, rd = {}, {q: {} for q in queues}, {}, {}
+    calls, wr, rd = [], {}, {}
 
-    def need(q, deps):
-        best = {}
-        for s, n in deps:
-            best[s] = max(best.get(s, 0), n)
-        for s in sorted(best):
-            if waited[q].get(s, 0) < best[s]:
-                queues[q].wait_ge(T.sem[s], best[s])
-                waited[q][s] = best[s]
-
-    def before(q, reads, writes):
-        deps = []
+    def note(q, reads, writes, sem, inc, issue, length, hold):
+        deps = set()
         for k in reads:
             if k in wr:
-                deps.append(wr[k][1:])
+                deps.add(wr[k])
             if k in PS:
-                deps += [r[1:] for r in rd.get(k, []) if r[0] != q]
+                deps.update(r for r in rd.get(k, []) if calls[r]["q"] != q)
         for k in writes:
             if k in wr:
-                deps.append(wr[k][1:])
-            deps += [r[1:] for r in rd.get(k, [])]
-        need(q, deps)
-
-    def after(q, sem, inc, reads, writes):
-        total[sem] = total.get(sem, 0) + inc
-        tok = (q, sem, total[sem])
+                deps.add(wr[k])
+            deps.update(rd.get(k, []))
+        i = len(calls)
+        calls.append({"q": q, "deps": sorted(deps), "sem": sem, "inc": inc, "issue": issue, "len": length, "hold": hold})
         for k in writes:
-            wr[k] = tok
+            wr[k] = i
             rd[k] = []
         for k in reads:
             if k not in writes:
-                rd[k] = [r for r in rd.get(k, []) if r[1] != sem] + [tok]
+                rd.setdefault(k, []).append(i)
+
+    fns = {"memset": g.vector.memset, "tt": g.vector.tensor_tensor, "ts": g.vector.tensor_scalar,
+           "cp": g.vector.tensor_copy, "red": g.vector.tensor_reduce, "scan": g.vector.tensor_tensor_scan,
+           "tr": g.vector.transpose, "qz": g.vector.quantize_mx, "act": g.scalar.activation,
+           "mm": g.tensor.matmul_mx, "iota": g.iota, "asel": g.affine_select}
 
     def op(q, reads, writes, name, *args, **kw):
-        before(q, reads, writes)
-        fns = {"memset": g.vector.memset, "tt": g.vector.tensor_tensor, "ts": g.vector.tensor_scalar,
-               "cp": g.vector.tensor_copy, "red": g.vector.tensor_reduce, "scan": g.vector.tensor_tensor_scan,
-               "tr": g.vector.transpose, "qz": g.vector.quantize_mx, "act": g.scalar.activation,
-               "mm": g.tensor.matmul_mx, "iota": g.iota, "asel": g.affine_select}
-        fns[name](*args, **kw).then_inc(T.sem["s" + q], 1)
-        after(q, "s" + q, 1, reads, writes)
+        picks = [k for k, a in enumerate(args[:2]) if isinstance(a, tuple)]
+        args = [a[0].indirect(a[1]) if isinstance(a, tuple) else a for a in args]
+        if picks:
+            n = width(args[1 - picks[0]])
+            length = 55.0 + (1.56 if picks[0] else 3.8) * CYC * n
+        elif name == "qz":
+            length = 12.0 + 0.22 * width(args[2])
+        elif name == "mm":
+            length = 1.2 * (width(args[0]) + 16)
+        elif name in ("iota", "asel"):
+            length = 140.0 + 2 * CYC * width(args[0])
+        elif name == "act":
+            length = 50.0 + CYC * max(64, width(args[0]))
+        else:
+            sides = {"memset": 1, "tt": 3, "scan": 3}.get(name, 2)
+            each = 0.5 if name != "red" and all("16" in str(a.dtype) for a in args[:sides]) else 1.0
+            if name == "tt":
+                each = 1.0 if any(k in PS for k in reads) else 2.0
+            length = CYC * max(64, each * width(args[sides - 1]))
+        note(q, reads, writes, "s" + q, 1, lambda: fns[name](*args, **kw).then_inc(T.sem["s" + q], 1), length, length)
 
-    def dma(q, sem, reads, writes, out, in_):
-        before(q, reads, writes)
-        queues[q].dma_start(out, in_).then_inc(T.sem[sem], 16)
-        after(q, sem, 16, reads, writes)
+    def dma(q, sem, reads, writes, out, in_, length=DMA):
+        note(q, reads, writes, sem, 16, lambda: queues[q].dma_start(out, in_).then_inc(T.sem[sem], 16), length, 60.0)
 
     def V(name, writes, reads, *args, **kw):
         op("v", reads.split(), writes.split(), name, *args, **kw)
@@ -118,19 +161,23 @@ def rank_program(g, core, T, topo):
     def S(writes, reads, out, in_, func, **kw):
         op("s", reads.split(), writes.split(), "act", out, in_, func, **kw)
 
+    def iota(key, out, pattern, base, cm=0, on=""):
+        kw = {} if key == "pi" else {"allow_small_or_imprecise_dtypes": True}
+        op("g", on.split(), [key], "iota", out, pattern, base, cm, **kw)
+
+    def mm(out, st, stk, sc, mv, mvk, mp, n):
+        op("p", stk.split() + mvk.split(), [out], "mm", T[out][:, 0:n], st, sc, mv, mp, True, True)
+
     def names(stem, lo, hi):
         return " ".join(stem + str(c) for c in range(lo, hi))
 
-    dma("y", "dx", [], ["xt"], T.xt[:], T.x[:])
-    dma("s", "du", [], ["ut"], T.ut[:], T.u[:])
-    dma("y", "dn0", [], ["lw"], T.lw[:], T.nb[:])
-    dma("y", "dwc", [], ["wq"], T.wq[:, 0:512].bitcast(dt.uint8), T.wc[:])
-    dma("y", "dws", [], ["wp"], T.wp[:, 0:512], T.ws[:])
-    dma("y", "dv", [], ["vt"], T.vt[:], T.v[:])
+    dma("y", "dx", [], ["xt"], T.xt[:], T.x[:], 3300.0)
+    dma("s", "du", [], ["ut"], T.ut[:], T.u[:], 2900.0)
+    dma("y", "dn0", [], ["lw"], T.lw[:], T.nb[:], 2500.0)
+    dma("y", "dwc", ["xt"], ["wq"], T.wq[:, 0:512].bitcast(dt.uint8), T.wc[:], 3300.0)
+    dma("y", "dws", ["xt"], ["wp"], T.wp[:, 0:512], T.ws[:], 2700.0)
+    dma("y", "dv", ["xt"], ["vt"], T.vt[:], T.v[:], 2900.0)
 
-    def iota(key, out, pattern, base, cm=0):
-        kw = {} if key == "pi" else {"allow_small_or_imprecise_dtypes": True}
-        op("g", [], [key], "iota", out, pattern, base, cm, **kw)
     iota("pi", T.pi[:, 0:1], [[0, 1]], 0, 1)
     iota("sm1", T.sm[:, 8:20], [[8, 2], [-1, 6]], 7)
     iota("idw", T.idw[:], [[1, 272]], 0)
@@ -146,11 +193,14 @@ def rank_program(g, core, T, topo):
     V("tt", "smS", "sm1", T.sm[:, 24:30], T.sm[:, 8:14], T.sm[:, 14:20], A.add)
     V("ts", "smB", "sm1", T.sm[:, 32:38], T.sm[:, 8:14], 256.0, None, A.mult)
     V("memset", "one", "", T.one[:], 1.0)
-    V("memset", "cl", "", T.cl[:, LM:LE], 0.0)
-    V("memset", "c0", "", T.c0[:], 0.0)
+    V("memset", "cl0", "", T.cl[:, LS:LE], 0.0)
+    V("memset", "c0", "", T.c0[:], 1.0)
+    V("memset", "c0z", "c0", T.c0[:, 0:512:32], 0.0)
+    V("memset", "c1z", "", T.c1[:], 0.0)
     V("cp", "upl", "sm0", T.upl[:], T.sm[:, 0:8])
-    for t, k in enumerate(["v0", "a1", "a2", "a3", "a4", "asc"]):
-        S(k + (" asd" if k == "asc" else ""), "idw smS smB", T[k][:], T.idw[:, 0:256], ACT.Identity, scale=T.sm[:, 24 + t:25 + t], bias=T.sm[:, 32 + t:33 + t])
+    adds = [T.aa[:, 256 * k:256 * k + 256] for k in range(5)] + [T.asc[:]]
+    for k in range(6):
+        S("asc asd" if k == 5 else "a%d" % k, "idw smS smB", adds[k], T.idw[:, 0:256], ACT.Identity, scale=T.sm[:, 24 + k:25 + k], bias=T.sm[:, 32 + k:33 + k])
     V("ts", "pfa", "pf", T.pf[:, 10:11], r16, 8.0, None, A.is_ge)
     V("ts", "pf5", "pf", T.pf[:, 5:6], r16, 10.0, 256.0, A.is_ge, A.mult)
     V("ts", "pf3", "pf pfa", T.pf[:, 3:4], r16, 1.0, T.pf[:, 10:11], A.is_equal, A.add)
@@ -165,28 +215,86 @@ def rank_program(g, core, T, topo):
     V("ts", "dg3", "dg2", T.dg1[:, 49:64], T.dg1[:, 16:31], -0.25, None, A.mult)
     V("memset", "dg4", "", T.dg1[:, 48:49], 0.0)
     V("tt", "dgs", "dg2 dg3 dg4", T.dg1[:, 64:80], T.dg1[:, 16:32], T.dg1[:, 48:64], A.add)
-    S("dg", "dgs rl16", T.dg[:, 0:512], T.dg1[:, 64:80].indirect(T.rl16[:, 0:32]), ACT.Copy)
+    S("dg", "dgs rl16", T.dg[:, 0:512], (T.dg1[:, 64:80], T.rl16[:, 0:32]), ACT.Copy)
     V("ts", "nmask", "rp pf", T.nmask[:], T.rp[:], r16, -1.0, A.is_equal, A.mult)
-    V("ts", "sc0", "rp", T.sc0[:], T.rp[:], 0.0, None, A.not_equal)
+    V("ts", "thr", "rp pf", T.thr[:], T.rp[:], r16, 1e29, A.not_equal, A.mult)
+    S("sc0", "rp", T.sc0[:], T.rp[:], ACT.Sign)
+    S("scb", "rp", T.scb[:], T.rp[:], ACT.Sign)
     V("qz", "uq up", "ut", T.uq[:, 0:128], T.up[:, 0:128], T.ut[:, 0:512])
-    V("cp", "uq2", "uq upl", T.uq2[:, 0:128].bitcast(dt.uint32), T.uq[:, 0:128].bitcast(dt.uint32).indirect(T.upl[:, 0:8]))
-    V("cp", "up2", "up upl", T.up2[:, 0:128], T.up[:, 0:128].indirect(T.upl[:, 0:8]))
+    V("cp", "uq2", "uq upl", T.uq2[:, 0:128].bitcast(dt.uint32), (T.uq[:, 0:128].bitcast(dt.uint32), T.upl[:, 0:8]))
+    S("up2", "up upl", T.up2[:, 0:128], (T.up[:, 0:128], T.upl[:, 0:8]), ACT.Copy)
     V("qz", "xq0", "xt", T.xq0[:, 0:256], T.xp0[:, 0:256], T.xt[:, 0:1024])
+    V("qz", "vq vp", "vt", T.vq[:, 0:128], T.vp[:, 0:128], T.vt[:, 0:512])
     V("cp", "lw16", "lw", T.lw16[:], T.lw[:])
-    V("tt", "c0", "lw", T.c0[:, 1:32:2], T.lw[:, 16:32], T.lw[:, 0:16], A.subtract)
-    V("cp", "c1o", "lw", T.c1[:, 1:32:2], T.lw[:, 0:16])
+    V("tt", "c0", "lw", T.c0[:, 31:512:32], T.lw[:, 16:32], T.lw[:, 0:16], A.subtract)
+    V("cp", "c1o", "lw c1z", T.c1[:, 31:512:32], T.lw[:, 0:16])
 
-    def cli(lo, hi, pattern, base, step=1):
-        iota("cl", T.cl[:, lo:hi:step], pattern, base)
     iota("cla", T.cl[:, LN:LN + 256], [[2, 16], [-1, 2], [0, 8]], 1)
+    parts = [(LS, 16, [[0, 4], [1, 2], [0, 2]], 0), (LP, 84, [[32, 2], [1, 6], [0, 7]], 2), (LP + 84, 84, [[32, 2], [0, 6], [1, 7]], 1),
+             (LP + 169, 24, [[8, 2], [32, 2], [1, 6]], 2), (LP + 193, 12, [[32, 2], [0, 6]], 0), (LQ, 84, [[32, 2], [0, 6], [1, 7]], 9),
+             (LQ + 84, 84, [[32, 2], [1, 6], [0, 7]], 10), (LV, 24, [[8, 2], [32, 2], [1, 6]], 1), (LX, 12, [[32, 2], [0, 6]], 1)]
+    for k, (lo, n, pattern, base) in enumerate(parts):
+        iota("cl%d" % (k + 1), T.cl[:, lo:lo + n], pattern, base, on="cl0")
+    iota("clx", T.cl[:, LP:LP + 169:7], [[0, 25]], 64, on="cl2 cl3")
+    iota("cly", T.cl[:, LQ:LQ + 169:7], [[0, 25]], 65, on="cl6 cl7")
+    iota("clz", T.cl[:, LV:LV + 24:6], [[0, 4]], 64, on="cl8")
+
+    def wrap(lo, hi, key, reads):
+        V("scan", key, reads + " dg", T.clo[:, lo:hi], T.dg[:, 0:hi - lo], T.cl[:, lo:hi], 0.0, A.add, A.min)
+    wrap(LN, LS, "cloa", "cla")
+    wrap(LS, LQ, "clob", "cl1 cl4 cl5 clx")
+    wrap(LQ, LE, "cloc", "cly clz cl9")
+    V("ts", "cl16a", "cloa pf7", T.cl16[:, 0:LS // 16], T.clo[:, 15:LS:16], fix, None, A.add)
+    V("ts", "cl16b", "clob pf7", T.cl16[:, LS // 16:LP // 16], T.clo[:, LS + 15:LP:16], fix, None, A.add)
+    V("ts", "cl16c", "clob cloc pf7 pf", T.cl16[:, LP // 16:LE // 16], T.clo[:, LP + 15:LE:16], fix, odd16, A.add, A.add)
+
+    def lst(lo, n):
+        return T.cl16[:, lo // 16:(lo + n) // 16]
+
     iota("nT", T.nT[:, 0:16], [[32, 8], [0, 2]], 0)
     iota("f1", T.f1[:], [[0, 256]], 0)
-    iota("f1", T.f1[:, 0:256:16], [[0, 16]], 1)
-    iota("f1", T.f1[:, 1:256:16], [[0, 16]], 1)
+    iota("f1a", T.f1[:, 0:256:16], [[0, 16]], 1, on="f1")
+    iota("f1b", T.f1[:, 1:256:16], [[0, 16]], 1, on="f1")
     iota("nw0", T.nw[:, 0:16], [[16, 16]], 0)
-
-    def mm(out, st, stk, sc, mv, mvk, mp, n):
-        op("p", stk.split() + mvk.split(), [out], "mm", T[out][:, 0:n], st, sc, mv, mp, True, True)
+    iota("tsz", T.tsel[:, 32:272], [[0, 240]], 0)
+    iota("wt0", T.wt[:, 0:168], [[1, 2], [0, 84]], 8)
+    iota("wt1", T.wt[:, 1:84:7], [[0, 2], [9, 6]], 0, on="wt0")
+    iota("wt2", T.wt[:, 85:168:7], [[0, 2], [8, 6]], 0, on="wt0")
+    iota("wt3", T.wt[:, 7:85:7], [[0, 2], [-9, 6]], -40, on="wt0")
+    iota("wt4", T.wt[:, 91:169:7], [[0, 2], [-8, 6]], -45, on="wt0")
+    iota("wt5", T.wt[:, 1:169:42], [[0, 4]], -256, on="wt1 wt2")
+    iota("scab", T.scab[:], [[0, 24]], 1)
+    iota("scab", T.scab[:, 0:24:6], [[0, 4]], 0)
+    iota("ffc", T.ff[:, 0:24:6], [[0, 4]], 1)
+    op("g", ["one"], ["et"], "asel", T.et[:], T.one[:], [[-1, 520]], A.is_equal, 0.0, 3, 4)
+    iota("t2c", T.t2[:, 64:96], [[0, 32]], 256)
+    iota("t2c", T.t2[:, 65:96:16], [[0, 2]], -5)
+    iota("pqz", T.pq[:, 256:264], [[0, 8]], 512)
+    iota("gpz", T.gp[:, 208:224], [[0, 16]], 0)
+    iota("de0", T.de[:], [[0, 200]], -16)
+    iota("de1", T.de[:, 16:192:16], [[0, 11]], 239, on="de0")
+    iota("de2", T.de[:, 0:193:192], [[251, 2]], 0, on="de0")
+    iota("cm", T.cm[:], [[1, 2]], -1)
+    iota("b0", T.b0[:], [[0, 24]], 0)
+    iota("ltz", T.lt[:, 512:544], [[0, 32]], 0)
+    iota("abz", T.abd[:, :, 192], [[0, 16]], 1024)
+    for b in range(4):
+        iota("f2z%d" % b, T.f2[:, 272 * b + 256:272 * b + 272], [[0, 16]], 0)
+        iota("hbz%d" % b, T.hb[:, 208 * b + 192:208 * b + 208], [[0, 16]], 0)
+    S("nT", "nT pf9", T.nT[:, 0:16], T.nT[:, 0:16], ACT.Identity, bias=T.pf[:, 9:10], scale=U)
+    S("w256a", "idw", T.w256[:, 0:256], T.idw[:, 0:256], ACT.Identity, scale=256 * U, bias=-255 * 256 * U)
+    S("w256b", "idw", T.w256[:, 256:512], T.idw[:, 0:256], ACT.Identity, scale=256 * U, bias=256 * U)
+    S("nw1", "nw0 pf", T.nw[:, 16:32], T.nw[:, 0:16], ACT.Identity, bias=r16, scale=1.0)
+    S("nw2", "nw1", T.nw[:, 32:48], T.nw[:, 16:32], ACT.Identity, bias=-0.5 * U, scale=U)
+    S("nw3", "nw1", T.nw[:, 48:64], T.nw[:, 16:32], ACT.Copy, scale=-1024.0)
+    S("md", "wt3 wt4 wt5", T.md[:, 0:169], T.wt[:, 0:169], ACT.Copy, scale=1.0 / 128)
+    S("idb", "idw", T.idb[:], T.idw[:], ACT.Copy)
+    S("cm", "cm pf8", T.cm[:], T.cm[:], ACT.Identity, bias=T.pf[:, 8:9], scale=1.0)
+    S("lt", "idb lw16", T.lt[:, 0:512], (T.idb[:, 0:272], T.lw16[:, 0:32]), ACT.Copy)
+    V("ts", "ts2", "idw pf8", T.sm[:, 40:73], T.idw[:, 0:33], T.pf[:, 8:9], -1.0 / U, A.is_equal, A.mult)
+    V("tt", "tsel", "ts2", T.tsel[:, 0:32], T.sm[:, 41:73], T.sm[:, 40:72], A.subtract)
+    for b in range(4):
+        V("qz", "eq%d" % b, "et", T.eq[:, 128 * b:128 * b + 128], T.ep[:, 128 * b:128 * b + 128], T.et[:, 3 - b:515 - b])
 
     dst = T.cores[(rank + 1) % N]
     prv = T.cores[(rank - 1) % N]
@@ -198,121 +306,45 @@ def rank_program(g, core, T, topo):
     rid, pid = topo.addr(dst)[:2]
     nout, nin = len(engs(core, dst)), len(engs(prv, core))
 
-    def send_x(t):
-        before("g", ["xq%d" % t], [])
-        q, p = T["xq%d" % t], T["xp%d" % t]
-        g.remote_dma(q[:, 256:512].bitcast(dt.uint8), q[:, 0:256].bitcast(dt.uint8), T.sem["ax%d" % t], T.sem.lc, pid, rid, emask)
-        g.remote_dma(p[:, 256:512], p[:, 0:256], T.sem["ax%d" % t], T.sem.lc, pid, rid, emask)
-        total["lc"] = total.get("lc", 0) + 2 * nout
-        total["ax%d" % t] = 2 * nin
-        wr["xn%d" % t] = ("r", "ax%d" % t, 2 * nin)
-
-    def send_lists(t):
-        before("g", ["ab%d" % t], [])
-        g.remote_dma(T.la[:, 24 * t:24 * t + 24], T.ab[:, 24 * t:24 * t + 24], T.sem["al%d" % t], T.sem.lc, pid, rid, emask)
-        total["lc"] = total.get("lc", 0) + nout
-        total["al%d" % t] = nin
-        wr["la%d" % t] = ("r", "al%d" % t, nin)
-
-    def wrap_lists(lo, hi, key):
-        V("scan", "clo" + key, "cla dg" if key == "a" else "cl dg", T.clo[:, lo:hi], T.dg[:, 0:hi - lo], T.cl[:, lo:hi], 0.0, A.add, A.min)
-
-    def more_iotas():
-        cli(LM, LM + 24, [[1, 4], [0, 6]], 0)
-        cli(LM, LM + 24, [[0, 4]], 4, 6)
-        iota("m5c", T.nT[:, 84:88], [[0, 4]], 2)
-        cli(LS, LS + 16, [[0, 4], [1, 2], [0, 2]], 0)
-        cli(LP, LP + 84, [[32, 2], [1, 6], [0, 7]], 2)
-        cli(LP + 84, LP + 168, [[32, 2], [0, 6], [1, 7]], 1)
-        cli(LP + 169, LP + 193, [[8, 2], [32, 2], [1, 6]], 2)
-        cli(LP + 193, LP + 205, [[32, 2], [0, 6]], 0)
-        cli(LQ, LQ + 84, [[32, 2], [0, 6], [1, 7]], 9)
-        cli(LQ + 84, LQ + 168, [[32, 2], [1, 6], [0, 7]], 10)
-        cli(LQ, LQ + 169, [[0, 25]], 65, 7)
-        cli(LV, LV + 24, [[8, 2], [32, 2], [1, 6]], 1)
-        cli(LV, LV + 24, [[0, 4]], 64, 6)
-        cli(LX, LX + 12, [[32, 2], [0, 6]], 1)
-        cli(LP, LP + 169, [[0, 25]], 64, 7)
-        iota("tsz", T.tsel[:, 32:272], [[0, 240]], 0)
-        iota("wt", T.wt[:, 0:168], [[1, 2], [0, 84]], 8)
-        iota("wt", T.wt[:, 1:84:7], [[0, 2], [9, 6]], 0)
-        iota("wt", T.wt[:, 85:168:7], [[0, 2], [8, 6]], 0)
-        iota("wt", T.wt[:, 7:85:7], [[0, 2], [-9, 6]], -40)
-        iota("wt", T.wt[:, 91:169:7], [[0, 2], [-8, 6]], -45)
-        iota("wt", T.wt[:, 1:169:42], [[0, 4]], -256)
-        iota("scab", T.scab[:], [[0, 24]], 1)
-        iota("scab", T.scab[:, 0:24:6], [[0, 4]], 0)
-        op("g", ["one"], ["et"], "asel", T.et[:], T.one[:], [[-1, 520]], A.is_equal, 0.0, 3, 4)
-        iota("t2c", T.t2[:, 64:96], [[0, 2], [0, 16]], 256)
-        iota("t2c", T.t2[:, 65:96:16], [[0, 2]], -5)
-        iota("pqz", T.pq[:, 256:264], [[0, 8]], 512)
-        iota("gpz", T.gp[:, 208:224], [[0, 16]], 0)
-        iota("so", T.so[:, 168:224], [[0, 56]], 2)
-        iota("de", T.de[:], [[0, 200]], -16)
-        iota("de", T.de[:, 16:192:16], [[0, 11]], 239)
-        iota("de", T.de[:, 0:193:192], [[251, 2]], 0)
-        iota("cm", T.cm[:], [[1, 2]], -1)
-        iota("b0", T.b0[:], [[0, 24]], 0)
-        iota("ltz", T.lt[:, 512:544], [[0, 32]], 0)
-        iota("abz", T.abd[:, :, 192], [[0, 16]], 1024)
-        for b in range(4):
-            iota("f2z", T.f2[:, 272 * b + 256:272 * b + 272], [[0, 16]], 0)
-        for b in range(4):
-            iota("hbz", T.hb[:, 208 * b + 192:208 * b + 208], [[0, 16]], 0)
-
-    def mid_constants():
-        S("nT", "nT pf9", T.nT[:, 0:16], T.nT[:, 0:16], ACT.Identity, bias=T.pf[:, 9:10], scale=U)
-        S("scb", "sc0", T.scb[:], T.sc0[:], ACT.Copy)
-        S("w256", "idw", T.w256[:, 0:256], T.idw[:, 0:256], ACT.Identity, scale=256 * U, bias=-255 * 256 * U)
-        S("w256", "idw", T.w256[:, 256:512], T.idw[:, 0:256], ACT.Identity, scale=256 * U, bias=256 * U)
-        S("nw1", "nw0 pf", T.nw[:, 16:32], T.nw[:, 0:16], ACT.Identity, bias=r16, scale=1.0)
-        S("nw2", "nw1", T.nw[:, 32:48], T.nw[:, 16:32], ACT.Identity, bias=-0.5 * U, scale=U)
-    mid_constants()
-
-    def late_constants():
-        V("ts", "ts2", "idw pf8", T.sm[:, 40:73], T.idw[:, 0:33], T.pf[:, 8:9], -1.0 / U, A.is_equal, A.mult)
-        wrap_lists(LM, LQ, "b")
-        wrap_lists(LQ, LE, "c")
-        V("tt", "tsel", "ts2", T.tsel[:, 0:32], T.sm[:, 41:73], T.sm[:, 40:72], A.subtract)
-        V("ts", "cl16b", "clob pf7", T.cl16[:, LM // 16:LP // 16], T.clo[:, LM + 15:LP:16], fix, None, A.add)
-        V("ts", "cl16c", "clob cloc pf7 pf", T.cl16[:, LP // 16:LE // 16], T.clo[:, LP + 15:LE:16], fix, odd16, A.add, A.add)
-
-    def lst(lo, n):
-        return T.cl16[:, lo // 16:(lo + n) // 16]
+    def send(key, sem, arrives, pairs, length):
+        def issue():
+            for out, in_ in pairs:
+                g.remote_dma(out, in_, T.sem[sem], T.sem.lc, pid, rid, emask)
+        note("g", [key], ["sent" + sem], "lc", nout * len(pairs), issue, 0.0, 300.0 * len(pairs))
+        note(None, ["sent" + sem], [arrives], sem, nin * len(pairs), None, length, 0.0)
 
     for t in range(R):
         xk = "xq%d" % t
         xq, xp = T[xk], T["xp%d" % t]
         for k in ("ps1", "ps2"):
             mm(k, T.uq2[:, 0:128], "uq2 up2", T.up2[:, 0:128], xq[:, 0:256], xk, xp[:, 0:256], 256)
-        send_x(t)
-        if t == 0:
-            more_iotas()
+        send(xk, "ax%d" % t, "xn%d" % t, [(xq[:, 256:512].bitcast(dt.uint8), xq[:, 0:256].bitcast(dt.uint8)), (xp[:, 256:512], xp[:, 0:256])], FAR)
+        for b in range(4):
+            mm("pd%d" % b, T.eq[:, 128 * b:128 * b + 128], "eq%d" % b, T.ep[:, 128 * b:128 * b + 128], xq[:, 0:512], xk + " xn%d" % t, xp[:, 0:512], 512)
+            S("f2_%d" % b, "pd%d" % b, T.f2[:, 272 * b:272 * b + 256], T["pd%d" % b][:, 256:512], ACT.Copy, scale=0.5)
+            S("fw%d" % b, "pd%d" % b, T.fw[:, 256 * b:256 * b + 256], T["pd%d" % b][:, 0:256], ACT.Copy)
+        V("tt", "c1e", "ps1 thr c1z", T.c1[:, 0:512:2], T.ps1[:, 0:256], T.thr[:], A.is_gt)
+        V("scan", "c2", "c0 c0z c1e c1o", T.c2[:], T.c0[:], T.c1[:], 0.0, A.mult, A.add)
+        V("cp", "wc16", "c2", T.wc16[:], T.c2[:, 31:512:32])
         V("tt", "ms", "ps1 nmask", T.ms[:], T.ps1[:, 0:256], T.nmask[:], A.mult)
         S("ssb", "ps2", T.ssb[:], T.ps2[:, 0:256], ACT.Copy)
         dma("y", "das", ["ssb"], ["asc"], T.asc[0:128:16, :], T.ssb[0:128:16, :])
         dma("y", "dat", ["ssb"], ["asd"], T.asc[1:128:16, :], T.ssb[1:128:16, :])
         V("scan", "sc", "ms sc0", T.sc[:], T.sc0[:], T.ms[:], 0.0, A.mult, A.add)
-        V("ts", "c1e", "sc", T.c1[:, 0:32:2], T.sc[:, 15:256:16], 0.0, None, A.is_lt)
-        V("scan", "c2", "c0 c1e c1o", T.c2[:], T.c0[:], T.c1[:], 0.0, A.mult, A.add)
-        V("cp", "wc16", "c2", T.wc16[:], T.c2[:, 1:32:2])
         for c in range(16):
             S("jk%d acc%d" % (c, c), "ssb sc", T.jk[:, 256 * c:256 * c + 256], T.ssb[:], ACT.Sign, bias=T.sc[:, 16 * c + 15:16 * c + 16], scale=1.0, accum_out=T.acc[:, c:c + 1])
-        cur = "v0"
-        for k, add in enumerate(["a1", "a2", "a3", "a4", "asc"]):
-            nxt = "va" if k % 2 == 0 else "vb"
-            V("tt", nxt, cur + " wc16 asd " + add if k == 4 else cur + " wc16 " + add, T[nxt][:], T[cur][:, 0:256].indirect(T.wc16[:, 0:16]), T[add][:], A.add)
-            cur = nxt
-            if t == 0 and k == 3:
-                wrap_lists(LN, LM, "a")
-                V("ts", "cl16a", "cloa pf7", T.cl16[:, 0:LM // 16], T.clo[:, 15:LM:16], fix, None, A.add)
-        V("ts", "qp", cur + " lw16 pf3 pf4", T.qp[:], T[cur][:, 0:256].indirect(T.lw16[:, 16:32]), T.pf[:, 3:4], T.pf[:, 4:5], A.mult, A.add)
-        V("tt", "pq", cur + " lw16 qp", T.pq[:, 0:256], T[cur][:, 0:256].indirect(T.lw16[:, 0:16]), T.qp[:], A.max)
+        cur, key = adds[0], "a0"
+        for k in range(1, 6):
+            nxt = "va" if k % 2 else "vb"
+            V("tt", nxt, key + (" wc16 asc asd" if k == 5 else " wc16 a%d" % k), T[nxt][:], (cur, T.wc16[:, 0:16]), adds[k], A.add)
+            cur, key = T[nxt][:, 0:256], nxt
+        V("ts", "qp", key + " lw16 pf3 pf4", T.qp[:], (cur, T.lw16[:, 16:32]), T.pf[:, 3:4], T.pf[:, 4:5], A.mult, A.add)
+        V("tt", "pq", key + " lw16 qp", T.pq[:, 0:256], (cur, T.lw16[:, 0:16]), T.qp[:], A.max)
         V("tr", "t3", "pq", T.t3[:], T.pq[:, 0:256])
         V("cp", "t5", "t3", T.nT[:, 48:80], T.t3[:, 7:256:8])
         V("tt", "f1k", "t3", T.nT[:, 16:32], T.t3[:, 2:256:16], T.t3[:, 10:256:16], A.is_equal)
-        V("tt", "ur", "t3 t5 cl16a", T.ur[:], T.nT[:, 48:80].indirect(lst(LN, 256)), T.t3[:], A.not_equal)
-        V("scan", "wr", "ur f1", T.wr[:], T.ur[:], T.f1[:], 1.0, A.min, A.max)
+        V("tt", "ur", "t3 t5 cl16a", T.ur[:], (T.nT[:, 48:80], lst(LN, 256)), T.t3[:], A.not_equal)
+        V("scan", "wr", "ur f1a f1b", T.wr[:], T.ur[:], T.f1[:], 1.0, A.min, A.max)
         V("tt", "f1m", "f1k nT", T.nT[:, 32:48], T.nT[:, 16:32], T.nT[:, 0:16], A.max)
         V("tt", "f0", "wr f1m", T.f0[:, 0:256:16], T.wr[:, 15:256:16], T.nT[:, 32:48], A.max)
         V("scan", "fo", "f0 scb", T.fo[:], T.scb[:], T.f0[:], 0.0, A.mult, A.add)
@@ -320,106 +352,100 @@ def rank_program(g, core, T, topo):
         accs = names("acc", 0, 16)
         V("ts", "a16", accs, T.a16[:], T.acc[:], 255.0, None, A.add)
         V("ts", "nb0", accs, T.nB[:, 16:32], T.acc[:], -256.0 * U, None, A.mult)
-        V("tt", "kap", "a16 w256 wr", T.kap[:], T.w256[:, 0:512].indirect(T.a16[:, 0:16]), T.wr[:], A.add)
+        V("tt", "kap", "a16 w256a w256b wr", T.kap[:], (T.w256[:, 0:512], T.a16[:, 0:16]), T.wr[:], A.add)
         V("tt", "nB", "nb0 nw2", T.nB[:, 0:16], T.nB[:, 16:32], T.nw[:, 32:48], A.subtract)
         for c in range(NS):
             S("jk%d rk%d" % (c, c), "kap nB", T.jk[:, 256 * c:256 * c + 256], T.kap[:], ACT.Sign, bias=T.nB[:, c:c + 1], scale=1.0, accum_out=T.acc2[:, c:c + 1])
         for c in range(NS, 16):
-            V("ts", "jk%d" % c, "kap nB", T.jk[:, 256 * c:256 * c + 256], T.kap[:], T.nB[:, c:c + 1], 0.0, A.add, A.is_lt)
-        for c in range(NS, 16):
             j = T.jk[:, 256 * c:256 * c + 256]
+            V("ts", "jk%d" % c, "kap nB", j, T.kap[:], T.nB[:, c:c + 1], 0.0, A.add, A.is_lt)
             V("scan", "rk%d" % c, "jk%d" % c, T.jo[:, 256 * c:256 * c + 256], j, j, 0.0, A.add, A.max)
         V("ts", "ur", "wr", T.ur[:], T.wr[:], 256 * U, 256 * U, A.min, A.subtract)
         V("cp", "r16b", names("rk", NS, 16), T.r16[:, NS:16], T.jo[:, 256 * NS + 255:4096:256])
-        if t == 0:
-            late_constants()
-            for b in range(4):
-                V("qz", "eq%d" % b, "et", T.eq[:, 128 * b:128 * b + 128], T.ep[:, 128 * b:128 * b + 128], T.et[:, 3 - b:515 - b])
-        for b in range(4):
-            mm("pd%d" % b, T.eq[:, 128 * b:128 * b + 128], "eq%d" % b, T.ep[:, 128 * b:128 * b + 128], xq[:, 0:512], xk + " xn%d" % t, xp[:, 0:512], 512)
         V("ts", "r16a", names("rk", 0, NS), T.r16[:, 0:NS], T.acc2[:, 0:NS], -0.5, 128.0, A.mult, A.add)
-        V("tt", "qq", "r16a r16b tsel tsz ur", T.qq[:], T.tsel[:, 0:272].indirect(T.r16[:, 0:16]), T.ur[:], A.mult)
-        if t == 0:
-            S("md", "wt", T.md[:, 0:169], T.wt[:, 0:169], ACT.Copy, scale=1.0 / 128)
-            S("idb", "idw", T.idb[:], T.idw[:], ACT.Copy)
-            S("cm", "cm pf8", T.cm[:], T.cm[:], ACT.Identity, bias=T.pf[:, 8:9], scale=1.0)
-            S("nw3", "nw1", T.nw[:, 48:64], T.nw[:, 16:32], ACT.Copy, scale=-1024.0)
-            S("lt", "idb lw16", T.lt[:, 0:512], T.idb[:, 0:272].indirect(T.lw16[:, 0:32]), ACT.Copy)
+        V("tt", "qq", "r16a r16b tsel tsz ur", T.qq[:], (T.tsel[:, 0:272], T.r16[:, 0:16]), T.ur[:], A.mult)
         S("kv1", "qq", T.qj[:], T.qq[:], ACT.Relu, scale=-1.0, accum_out=T.kv[:, 1:2])
         V("red", "kv0", "qq", T.kv[:, 0:1], T.qq[:], XAX, A.max)
+        V("ts", "off", "kv0 kv1 cl16b", T.off[:], (T.kv[:, 0:2], lst(LS, 16)), -1.0, 256.0, A.mult, A.add)
+        V("cp", "g2", "pqz pq off", T.g2[:], (T.pq[:, 0:264], T.off[:, 0:4]))
+        V("tr", "t2", "g2", T.t2[:, 0:64], T.g2[:])
+        t2 = T.t2[:, 0:96]
+        V("cp", "gp", "t2 t2c cl16c", T.gp[:, 0:208], (t2, lst(LP, 208)))
+        V("tt", "ee", "t2 t2c cl16c gp", T.ee[:], (t2, lst(LQ, 176)), T.gp[:, 0:176], A.is_equal)
+        V("tt", "nd", "t2 t2c cl16c gp", T.nd[:], (t2, lst(LV, 32)), T.gp[:, 169:201], A.subtract)
+        V("scan", "so", "ee md", T.so[:, 0:169], T.md[:, 0:169], T.ee[:, 0:169], 0.0, A.add, A.max)
+        V("tt", "br", "t2 t2c cl16c gp gpz", T.abi[:, 0:32:2], (t2, lst(LX, 16)), T.gp[:, 193:209], A.is_gt)
+        for s in range(4):
+            V("ts", "ff%d" % s, "so", T.ff[:, 6 * s + 1:6 * s + 6], T.so[:, 42 * s + 7:42 * s + 42:7], T.so[:, 42 * s + 42:42 * s + 43], None, A.is_lt)
+        V("tt", "d2", "nd ffc ff0 ff1 ff2 ff3", T.d2[:], T.nd[:, 0:24], T.ff[:], A.mult)
+        V("scan", "ab", "d2 scab", T.abi[:, 1:48:2], T.scab[:], T.d2[:], 0.0, A.mult, A.subtract)
+        V("cp", "ab%d" % t, "ab", T.ab[:, 24 * t:24 * t + 24], T.abi[:, 1:48:2])
+        send("ab%d" % t, "al%d" % t, "la%d" % t, [(T.la[:, 24 * t:24 * t + 24], T.ab[:, 24 * t:24 * t + 24])], NEAR)
+        V("tt", "b0", "ab b0", T.b0[:, 1:24:2], T.abi[:, 25:48:2], T.abi[:, 1:24:2], A.subtract)
+        V("scan", "bti", "b0 ab br", T.bti[:], T.b0[:], T.abi[:, 0:24], 0.0, A.mult, A.add)
+        V("cp", "bt16", "bti", T.bt16[:], T.bti[:, 1:24:2])
+        V("cp", "btv", "idb bt16", T.btv[:], (T.idb[:, 0:272], T.bt16[:, 0:12]))
+        for c in range(16):
+            if c < NE:
+                S("abd%d" % c, "btv nw3", T.abd[:, c, 0:192], T.btv[:], ACT.Abs, bias=T.nw[:, 48 + c:49 + c], scale=1024.0)
+            else:
+                V("ts", "abd%d" % c, "btv nw1", T.abd[:, c, 0:192], T.btv[:], T.nw[:, 16 + c:17 + c], 1024.0, A.not_equal, A.mult)
+            V("scan", "ev%d" % c, "abz de1 de2 abd%d" % c, T.abo[:, c, 0:193], T.de[:, 0:193], T.abd[:, c, 0:193], 252.0, A.add, A.min)
+        V("ts", "ei", names("ev", 0, 16), T.ei[:, 0:16], T.abo[:, :, 192], 16.0, None, A.mult)
+        V("ts", "ek", "ei", T.ei[:, 16:32], T.ei[:, 0:16], 255, None, A.bitwise_and)
+        V("ts", "em", "ei", T.ei[:, 32:48], T.ei[:, 0:16], 8, None, A.arith_shift_right)
+        V("tt", "ex2", "ek em", T.ei[:, 48:64], T.ei[:, 16:32], T.ei[:, 32:48], A.add)
+        V("cp", "e16", "ex2", T.e16[:], T.ei[:, 48:64])
+        for b in range(4):
+            w = T.f2[:, 272 * b:272 * b + 272]
+            S("at%d" % b, "f2z%d f2_%d la%d" % (b, b, t), T.at[:, 192 * b:192 * b + 192], (w, T.la[:, 24 * t:24 * t + 12]), ACT.Copy)
+            V("tt", "zt%d" % b, "f2z%d f2_%d la%d at%d" % (b, b, t, b), T.zt[:, b:768:4], (w, T.la[:, 24 * t + 12:24 * t + 24]), T.at[:, 192 * b:192 * b + 192], A.add)
+        V("qz", "zq zp", "zt0 zt1 zt2 zt3", T.zq[:, 0:192], T.zp[:, 0:192], T.zt[:, 0:768])
         S("li0", "kv0 kv1", T.li[:, 0:2], T.kv[:], ACT.Identity, bias=512.0, scale=-1.0)
         S("li1", "kv0 kv1", T.li[:, 2:4], T.kv[:], ACT.Relu, bias=1.0, scale=-1.0)
         for h in range(2):
             S("li2%d" % h, "li0 li1 cm", T.li[:, 4 + h:5 + h], T.li[:, 2 + h:3 + h], ACT.Identity, bias=T.li[:, h:h + 1], scale=T.cm[:, h:h + 1])
-        V("ts", "off", "kv0 kv1 cl16b", T.off[:], T.kv[:, 0:2].indirect(lst(LS, 16)), -1.0, 256.0, A.mult, A.add)
-        V("cp", "g2", "pqz pq off", T.g2[:], T.pq[:, 0:264].indirect(T.off[:, 0:4]))
-        V("tr", "t2", "g2", T.t2[:, 0:64], T.g2[:])
-        t2 = T.t2[:, 0:96]
-        V("cp", "gp", "t2 t2c cl16c", T.gp[:, 0:208], t2.indirect(lst(LP, 208)))
-        V("tt", "ee", "t2 t2c cl16c gp", T.ee[:], t2.indirect(lst(LQ, 176)), T.gp[:, 0:176], A.is_equal)
-        V("tt", "nd", "t2 t2c cl16c gp", T.nd[:], t2.indirect(lst(LV, 32)), T.gp[:, 169:201], A.subtract)
-        V("scan", "so", "ee md", T.so[:, 0:169], T.md[:, 0:169], T.ee[:, 0:169], 0.0, A.add, A.max)
-        V("tt", "br", "t2 t2c cl16c gp gpz abo_", T.abi[:, 0:32:2], t2.indirect(lst(LX, 16)), T.gp[:, 193:209], A.is_gt)
-        V("cp", "m5", "so", T.nT[:, 80:84], T.so[:, 42:169:42])
-        V("tt", "ff", "so m5 m5c cl16b", T.ff[:], T.nT[:, 80:88].indirect(lst(LM, 32)), T.so[:, 0:224:7], A.is_gt)
-        V("tt", "d2", "nd ff", T.d2[:], T.nd[:, 0:24], T.ff[:, 0:24], A.mult)
-        V("scan", "ab", "d2 scab br", T.abi[:, 1:48:2], T.scab[:], T.d2[:], 0.0, A.mult, A.subtract)
-        V("cp", "ab%d" % t, "ab", T.ab[:, 24 * t:24 * t + 24], T.abi[:, 1:48:2])
-        send_lists(t)
-        for b in range(4):
-            S("f2_%d" % b, "pd%d f2z" % b, T.f2[:, 272 * b:272 * b + 256], T["pd%d" % b][:, 256:512], ACT.Copy, scale=0.5)
-        V("tt", "b0", "ab b0", T.b0[:, 1:24:2], T.abi[:, 25:48:2], T.abi[:, 1:24:2], A.subtract)
-        V("cp", "m16", "ab", T.m16[:], T.abi[:, 11:24:12])
-        V("scan", "bti", "b0 ab br", T.bti[:], T.b0[:], T.abi[:, 0:24], 0.0, A.mult, A.add)
-        V("cp", "bt16", "bti", T.bt16[:], T.bti[:, 1:24:2])
-        S("btr", "idb bt16", T.btr[:], T.idb[:, 0:272].indirect(T.bt16[:, 0:12]), ACT.Copy)
-        V("cp", "btv", "idb bt16", T.btv[:], T.idb[:, 0:272].indirect(T.bt16[:, 0:12]))
-        for c in range(NE):
-            S("abd%d" % c, "btr nw3", T.abd[:, c, 0:192], T.btr[:], ACT.Abs, bias=T.nw[:, 48 + c:49 + c], scale=1024.0)
-        for c in range(NE, 16):
-            V("ts", "abd%d" % c, "btv nw1", T.abd[:, c, 0:192], T.btv[:], T.nw[:, 16 + c:17 + c], 1024.0, A.not_equal, A.mult)
-        for c in list(range(NE, 16)) + list(range(NE)):
-            V("scan", "ev%d" % c, "abz de abd%d" % c, T.abo[:, c, 0:193], T.de[:, 0:193], T.abd[:, c, 0:193], 252.0, A.add, A.min)
-        for b in range(4):
-            w = T.f2[:, 272 * b:272 * b + 272]
-            S("at%d" % b, "f2z f2_%d la%d" % (b, t), T.at[:, 192 * b:192 * b + 192], w.indirect(T.la[:, 24 * t:24 * t + 12]), ACT.Copy)
-        V("ts", "ei", names("ev", 0, 16), T.ei[:, 0:16], T.abo[:, :, 192], 16.0, None, A.mult)
-        for b in range(4):
-            w = T.f2[:, 272 * b:272 * b + 272]
-            V("tt", "zt%d" % b, "f2z f2_%d la%d at%d" % (b, t, b), T.zt[:, b:768:4], w.indirect(T.la[:, 24 * t + 12:24 * t + 24]), T.at[:, 192 * b:192 * b + 192], A.add)
-        for h in range(2):
             S("li3%d" % h, "br li2%d" % h, T.li[:, 6 + h:7 + h], T.abi[:, 12 * h:12 * h + 1], ACT.Identity, bias=T.li[:, 4 + h:5 + h], scale=-256.0)
-        S("mt", "idb m16", T.mt[:], T.idb[:, 0:272].indirect(T.m16[:, 0:2]), ACT.Copy)
-        for b in range(4):
-            S("fw%d" % b, "pd%d" % b, T.fw[:, 256 * b:256 * b + 256], T["pd%d" % b][:, 0:256], ACT.Copy)
-        V("qz", "zq zp", "zt0 zt1 zt2 zt3", T.zq[:, 0:192], T.zp[:, 0:192], T.zt[:, 0:768])
-        V("ts", "ek", "ei", T.ei[:, 16:32], T.ei[:, 0:16], 255, None, A.bitwise_and)
-        V("ts", "em", "ei", T.ei[:, 32:48], T.ei[:, 0:16], 8, None, A.arith_shift_right)
+        V("cp", "m16", "ab", T.m16[:], T.abi[:, 11:24:12])
+        S("mt", "idb m16", T.mt[:], (T.idb[:, 0:272], T.m16[:, 0:2]), ACT.Copy)
         V("cp", "ln16", "li30 li31", T.ln16[:], T.li[:, 6:8])
-        V("tt", "ex2", "ek em", T.ei[:, 48:64], T.ei[:, 16:32], T.ei[:, 32:48], A.add)
-        V("cp", "lt", "mt ln16 ltz", T.lt[:, 0:544].indirect(T.ln16[:, 0:2]), T.mt[:])
-        V("cp", "e16", "ex2", T.e16[:], T.ei[:, 48:64])
-        ph = ["ph0", "ph1", "ps1", "ps2"]
-        for b in range(4):
-            mm(ph[b], T.wq[:, 128 * b:128 * b + 128], "wq wp", T.wp[:, 128 * b:128 * b + 128], T.zq[:, 0:192], "zq zp", T.zp[:, 0:192], 192)
-            S("hb%d" % b, ph[b] + " hbz", T.hb[:, 208 * b:208 * b + 192], T[ph[b]][:, 0:192], ACT.Copy, scale=0.03125)
-            V("tt", "xs%d" % b, "hbz hb%d e16 fw%d" % (b, b), T.xs[:, b:1024:4], T.hb[:, 208 * b:208 * b + 208].indirect(T.e16[:, 0:16]), T.fw[:, 256 * b:256 * b + 256], A.add)
-        V("qz", "xq%d" % (t + 1), "xs0 xs1 xs2 xs3", T["xq%d" % (t + 1)][:, 0:256], T["xp%d" % (t + 1)][:, 0:256], T.xs[:, 0:1024])
+        V("cp", "lt", "mt ln16 ltz", (T.lt[:, 0:544], T.ln16[:, 0:2]), T.mt[:])
         if t < R - 1:
             V("scan", "lo", "lt dg", T.lo[:], T.dg[:, 0:512], T.lt[:, 0:512], 0.0, A.add, A.min)
             V("ts", "lw16", "lo pf7", T.lw16[:], T.lo[:, 15:512:16], fix, None, A.add)
-            V("ts", "c1o", "lo pf7", T.c1[:, 1:32:2], T.lo[:, 15:256:16], fix, None, A.add)
-            V("tt", "c0", "lo", T.c0[:, 1:32:2], T.lo[:, 271:512:16], T.lo[:, 15:256:16], A.subtract)
-        if t == 0:
-            V("qz", "vq vp", "vt", T.vq[:, 0:128], T.vp[:, 0:128], T.vt[:, 0:512])
+            V("ts", "c1o", "lo pf7", T.c1[:, 31:512:32], T.lo[:, 15:256:16], fix, None, A.add)
+            V("tt", "c0", "lo", T.c0[:, 31:512:32], T.lo[:, 271:512:16], T.lo[:, 15:256:16], A.subtract)
+        ph = ["ph0", "ph1", "ps1", "ps2"]
+        for b in range(4):
+            mm(ph[b], T.wq[:, 128 * b:128 * b + 128], "wq wp", T.wp[:, 128 * b:128 * b + 128], T.zq[:, 0:192], "zq zp", T.zp[:, 0:192], 192)
+            S("hb%d" % b, ph[b], T.hb[:, 208 * b:208 * b + 192], T[ph[b]][:, 0:192], ACT.Copy, scale=0.03125)
+            V("tt", "xs%d" % b, "hbz%d hb%d e16 fw%d" % (b, b, b), T.xs[:, b:1024:4], (T.hb[:, 208 * b:208 * b + 208], T.e16[:, 0:16]), T.fw[:, 256 * b:256 * b + 256], A.add)
+        V("qz", "xq%d" % (t + 1), "xs0 xs1 xs2 xs3", T["xq%d" % (t + 1)][:, 0:256], T["xp%d" % (t + 1)][:, 0:256], T.xs[:, 0:1024])
     xk = "xq%d" % R
     xq, xp = T[xk], T["xp%d" % R]
     S("olr", "lt", T.olr[:], T.lt[:, 0:512], ACT.Copy)
     dma("y", "ool", ["olr"], [], T.ol[:], T.olr[0:128:16, :])
     mm("ps1", T.vq[:, 0:128], "vq vp", T.vp[:, 0:128], xq[:, 0:256], xk, xp[:, 0:256], 256)
-    dma("y", "ooc", [xk], [], T.oc[:, 0:1024], xq[:, 0:256].bitcast(dt.uint8))
+    dma("y", "ooc", [xk], [], T.oc[:, 0:1024], xq[:, 0:256].bitcast(dt.uint8), 2800.0)
     for k in range(4):
-        dma("y", "os%d" % k, [xk], [], T.osc[4 * k:4 * k + 4, 0:256], xp[32 * k:32 * k + 4, 0:256])
+        dma("ys"[k % 2], "os%d" % k, [xk], [], T.osc[4 * k:4 * k + 4, 0:256], xp[32 * k:32 * k + 4, 0:256])
     S("kv1", "ps1", T.qj[:], T.ps1[:, 0:256], ACT.Copy)
-    dma("s", "oy", ["kv1"], [], T.y[:], T.qj[:])
-    need("g", [(s, n) for s, n in total.items()])
+    dma("s", "oy", ["kv1"], [], T.y[:], T.qj[:], 2800.0)
+
+    total, waited = {}, {q: {} for q in queues}
+    for i in in_order(calls):
+        c = calls[i]
+        if c["q"] is not None:
+            best = {}
+            for d in c["deps"]:
+                s, n = calls[d]["done"]
+                best[s] = max(best.get(s, 0), n)
+            for s in sorted(best):
+                if waited[c["q"]].get(s, 0) < best[s]:
+                    queues[c["q"]].wait_ge(T.sem[s], best[s])
+                    waited[c["q"]][s] = best[s]
+            c["issue"]()
+        total[c["sem"]] = total.get(c["sem"], 0) + c["inc"]
+        c["done"] = (c["sem"], total[c["sem"]])
+    for s in sorted(total):
+        g.wait_ge(T.sem[s], total[s])

@@ -5,9 +5,11 @@ N = 8
 R = 3
 C = 256
 NS = 9
-NE = 8
+NE = 7
 U = 2.0 ** -18
-CYC, LAT, DMA, NEAR, FAR, SLACK = 0.9, 200.0, 2100.0, 2200.0, 3500.0, 100.0
+CYC, LAT, DMA, NEAR, FAR, SLACK = 0.85, 220.0, 2100.0, 2200.0, 3500.0, 100.0
+SEED, SPREAD, STEPS, GIVE, SOONER = 1, 0.0, 3000, 150.0, 700.0
+ORDER = {}
 F32, BF, I32, U16, U8, X4 = "float32", "bfloat16", "int32", "uint16", "uint8", "float8_e4m3fn_x4"
 
 
@@ -23,18 +25,18 @@ SCRATCH = {
     "wq": _sb(512, X4), "wp": _sb(512, U8),
     "zt": _sb(768, BF), "zq": _sb(192, X4), "zp": _sb(192, U8),
     "pi": _sb(4, I32), "pf": _sb(16, F32), "sm": _sb(96, F32), "idw": _sb(272, F32), "idb": _sb(272, BF), "rp": _sb(256, F32),
-    "nmask": _sb(256, F32), "thr": _sb(256, F32), "sc0": _sb(256, F32), "nw": _sb(64, F32), "nT": _sb(96, F32),
+    "nmask": _sb(128, F32), "thr": _sb(128, F32), "sc0": _sb(128, F32), "nw": _sb(64, F32), "nwb": _sb(16, BF), "nT": _sb(96, F32),
     "scab": _sb(24, F32), "upl": _sb(8, U16), "w256": _sb(512, F32), "tsel": _sb(272, F32),
     "dg": _sb(512, BF), "dg1": _sb(80, BF), "cl": _sb(784, BF), "clo": _sb(784, BF),
     "cl16": _sb(50, U16), "wt": _sb(176, F32), "md": _sb(176, BF), "de": _sb(200, BF), "cm": _sb(2, F32),
     "aa": _sb(1280, F32), "asc": _sb(256, F32),
     "ms": _sb(256, F32), "sc": _sb(256, F32), "ssb": _sb(256, F32), "c0": _sb(512, BF), "c1": _sb(512, BF), "c2": _sb(512, BF),
-    "wc16": _sb(16, U16), "va": _sb(256, F32), "vb": _sb(256, F32), "qp": _sb(256, F32), "pq": _sb(264, F32),
-    "t3": _sb(256, F32), "ab": _sb(72, U16), "la": _sb(72, U16),
-    "f0": _sb(256, BF), "f1": _sb(256, BF), "fo": _sb(256, BF), "scb": _sb(256, BF),
+    "wc16": _sb(16, U16), "va": _sb(256, F32), "vb": _sb(256, F32), "pq": _sb(528, F32),
+    "t3": ("sbuf", [128, 32, 16], F32), "ab": _sb(72, U16), "la": _sb(72, U16),
+    "f0": _sb(256, BF), "f1": _sb(192, BF), "ne": _sb(192, BF), "no": _sb(192, BF), "fo": _sb(256, BF), "scb": _sb(256, BF),
     "wr": _sb(256, BF), "ur": _sb(256, BF), "jk": _sb(4096, BF), "jo": _sb(4096, BF), "acc": _sb(16, F32), "acc2": _sb(16, F32),
     "a16": _sb(16, U16), "nB": _sb(32, F32), "kap": _sb(256, F32), "r16": _sb(16, U16),
-    "qq": _sb(256, F32), "qj": _sb(256, F32), "kv": _sb(2, F32), "off": _sb(16, U16), "g2": _sb(64, F32), "t2": _sb(96, F32),
+    "qq": _sb(256, F32), "qj": _sb(256, F32), "kv": _sb(2, F32), "off": _sb(16, U16), "g2": _sb(128, F32), "t2": _sb(160, F32),
     "gp": _sb(224, F32), "ee": _sb(176, BF), "so": _sb(176, BF), "nd": _sb(32, F32), "ff": _sb(24, F32), "d2": _sb(24, F32),
     "abi": _sb(48, F32), "b0": _sb(24, F32), "bti": _sb(24, F32), "bt16": _sb(12, U16),
     "btv": _sb(192, BF), "abd": ("sbuf", [128, 16, 200], BF), "abo": ("sbuf", [128, 16, 200], BF),
@@ -50,10 +52,10 @@ for _t in range(R + 1):
 for _n in PS:
     SCRATCH[_n] = ("psum", [128, 512], F32)
 
-DMAS = ["dx", "du", "dv", "dwc", "dws", "dn0", "das", "dat", "oy", "ool", "ooc", "os0", "os1", "os2", "os3"]
+DMAS = ["dx0", "dx1", "du", "dv", "dwc", "dws", "dn0", "das", "oy0", "oy1", "ool", "oc0", "oc1", "os0", "os1", "os2", "os3"]
 SEMAPHORES = ["sv", "ss", "sp", "sg", "lc"] + ["ax%d" % t for t in range(R)] + ["al%d" % t for t in range(R)] + DMAS
 
-LN, LS, LP, LQ, LV, LX, LE = 0, 256, 288, 512, 704, 736, 752
+LS, LP, LQ, LV, LX, LE = 0, 32, 256, 448, 480, 496
 
 
 def width(ap):
@@ -69,6 +71,10 @@ def in_order(calls):
     chain = [0.0] * n
     for i in range(n - 1, -1, -1):
         chain[i] = calls[i]["len"] + max([LAT + chain[k] for k in after[i]] + [0.0])
+    x = SEED
+    for i in range(n):
+        x = (x * 1103515245 + 12345) % 2147483648
+        chain[i] += SPREAD * x / 2147483648 + calls[i]["lift"]
     left = [len(c["deps"]) for c in calls]
     ready = {i: 0.0 for i in range(n) if left[i] == 0}
     free, order = {}, []
@@ -92,7 +98,71 @@ def in_order(calls):
             left[k] -= 1
             if left[k] == 0:
                 ready[k] = max(calls[d]["end"] + LAT for d in calls[k]["deps"])
-    return order
+    return improved(calls, after, order)
+
+
+def improved(calls, after, order):
+    n = len(calls)
+    qs, deps, hold = [c["q"] for c in calls], [c["deps"] for c in calls], [c["hold"] for c in calls]
+    lens = [[c["len"] - (less if c["len"] == NEAR else 0.0) for c in calls] for less in (0.0, SOONER)]
+
+    def run(order, length):
+        end, cause, free, last = [0.0] * n, [-1] * n, {}, {}
+        for i in order:
+            t, why = 0.0, -1
+            for d in deps[i]:
+                if end[d] + LAT > t:
+                    t, why = end[d] + LAT, d
+            q = qs[i]
+            if q is not None:
+                if free.get(q, 0.0) > t:
+                    t, why = free[q], -2 - last[q]
+                free[q], last[q] = t + hold[i], i
+            end[i], cause[i] = t + length[i], why
+        return end, cause
+
+    def judge(order):
+        total, pairs = 0.0, []
+        for length in lens:
+            end, cause = run(order, length)
+            i = max(range(n), key=lambda k: end[k])
+            total += end[i]
+            while cause[i] != -1:
+                if cause[i] < -1:
+                    pairs.append((-2 - cause[i], i))
+                    i = -2 - cause[i]
+                else:
+                    i = cause[i]
+        return total, pairs
+    best, pairs = judge(order)
+    top, kept, x = best, order, SEED
+    for step in range(STEPS):
+        x = (x * 1103515245 + 12345) % 2147483648
+        a, b = pairs[(x >> 8) % len(pairs)]
+        pa, pb = order.index(a), order.index(b)
+        mid = order[pa + 1:pb]
+        if x & 64:
+            need = {b}
+            for k in reversed(mid):
+                if any(s in need for s in after[k]):
+                    need.add(k)
+            if any(s in need for s in after[a]):
+                continue
+            new = order[:pa] + [k for k in mid if k in need] + [b, a] + [k for k in mid if k not in need] + order[pb + 1:]
+        else:
+            need = {a}
+            for k in mid:
+                if any(d in need for d in deps[k]):
+                    need.add(k)
+            if any(d in need for d in deps[b]):
+                continue
+            new = order[:pa] + [k for k in mid if k not in need] + [b, a] + [k for k in mid if k in need] + order[pb + 1:]
+        total, p = judge(new)
+        if total <= best + GIVE * (1.0 - step / STEPS) * ((x >> 4) % 64) / 64:
+            order, best, pairs = new, total, p
+            if total < top:
+                top, kept = total, new
+    return kept
 
 
 def rank_program(g, core, T, topo):
@@ -103,7 +173,7 @@ def rank_program(g, core, T, topo):
     ACT = ActivationFunctionType
     XAX = AxisListType.X
     queues = {"v": g.vector, "s": g.scalar, "p": g.tensor, "g": g, "y": g.sync}
-    calls, wr, rd = [], {}, {}
+    calls, wr, rd, lift = [], {}, {}, [0.0]
 
     def note(q, reads, writes, sem, inc, issue, length, hold):
         deps = set()
@@ -117,7 +187,7 @@ def rank_program(g, core, T, topo):
                 deps.add(wr[k])
             deps.update(rd.get(k, []))
         i = len(calls)
-        calls.append({"q": q, "deps": sorted(deps), "sem": sem, "inc": inc, "issue": issue, "len": length, "hold": hold})
+        calls.append({"q": q, "deps": sorted(deps), "sem": sem, "inc": inc, "issue": issue, "len": length, "hold": hold, "lift": lift[0]})
         for k in writes:
             wr[k] = i
             rd[k] = []
@@ -171,15 +241,16 @@ def rank_program(g, core, T, topo):
     def names(stem, lo, hi):
         return " ".join(stem + str(c) for c in range(lo, hi))
 
-    dma("y", "dx", [], ["xt"], T.xt[:], T.x[:], 3300.0)
+    dma("y", "dx0", [], ["xta"], T.xt[:, 0:512], T.x[:, 0:512], 3000.0)
     dma("s", "du", [], ["ut"], T.ut[:], T.u[:], 2900.0)
-    dma("y", "dn0", [], ["lw"], T.lw[:], T.nb[:], 2500.0)
+    dma("y", "dx1", [], ["xt"], T.xt[:, 512:1024], T.x[:, 512:1024], 3300.0)
+    dma("s", "dn0", [], ["lw"], T.lw[:], T.nb[:], 2500.0)
     dma("y", "dwc", ["xt"], ["wq"], T.wq[:, 0:512].bitcast(dt.uint8), T.wc[:], 3300.0)
     dma("y", "dws", ["xt"], ["wp"], T.wp[:, 0:512], T.ws[:], 2700.0)
     dma("y", "dv", ["xt"], ["vt"], T.vt[:], T.v[:], 2900.0)
 
     iota("pi", T.pi[:, 0:1], [[0, 1]], 0, 1)
-    iota("sm1", T.sm[:, 8:20], [[8, 2], [-1, 6]], 7)
+    iota("sm1", T.sm[:, 8:14], [[-1, 6]], 7)
     iota("idw", T.idw[:], [[1, 272]], 0)
     iota("sm0", T.sm[:, 0:8], [[16, 8]], 0)
     iota("rp", T.rp[:], [[0, 16], [1, 16]], 0)
@@ -189,9 +260,8 @@ def rank_program(g, core, T, topo):
     V("ts", "pi3", "pi", T.pi[:, 3:4], T.pi[:, 0:1], 16, None, A.bitwise_and)
     V("cp", "pf", "pi1 pi2 pi3", T.pf[:, 0:3], T.pi[:, 1:4])
     r16, p32, odd16 = T.pf[:, 0:1], T.pf[:, 1:2], T.pf[:, 2:3]
-    V("ts", "sm1", "sm1 pf", T.sm[:, 8:20], T.sm[:, 8:20], r16, None, A.is_equal)
-    V("tt", "smS", "sm1", T.sm[:, 24:30], T.sm[:, 8:14], T.sm[:, 14:20], A.add)
-    V("ts", "smB", "sm1", T.sm[:, 32:38], T.sm[:, 8:14], 256.0, None, A.mult)
+    V("ts", "smS", "sm1 pf", T.sm[:, 25:30], T.sm[:, 9:14], r16, None, A.is_equal)
+    V("ts", "smT", "pf", T.sm[:, 24:25], r16, 7.0, None, A.is_ge)
     V("memset", "one", "", T.one[:], 1.0)
     V("memset", "cl0", "", T.cl[:, LS:LE], 0.0)
     V("memset", "c0", "", T.c0[:], 1.0)
@@ -200,15 +270,10 @@ def rank_program(g, core, T, topo):
     V("cp", "upl", "sm0", T.upl[:], T.sm[:, 0:8])
     adds = [T.aa[:, 256 * k:256 * k + 256] for k in range(5)] + [T.asc[:]]
     for k in range(6):
-        S("asc asd" if k == 5 else "a%d" % k, "idw smS smB", adds[k], T.idw[:, 0:256], ACT.Identity, scale=T.sm[:, 24 + k:25 + k], bias=T.sm[:, 32 + k:33 + k])
-    V("ts", "pfa", "pf", T.pf[:, 10:11], r16, 8.0, None, A.is_ge)
-    V("ts", "pf5", "pf", T.pf[:, 5:6], r16, 10.0, 256.0, A.is_ge, A.mult)
-    V("ts", "pf3", "pf pfa", T.pf[:, 3:4], r16, 1.0, T.pf[:, 10:11], A.is_equal, A.add)
-    V("ts", "pf6", "pf3", T.pf[:, 6:7], T.pf[:, 3:4], -1.0, 1e29, A.add, A.mult)
+        S("asc" if k == 5 else "a%d" % k, "idw smS" if k else "idw smT", adds[k], T.idw[:, 0:256], ACT.Copy, scale=T.sm[:, 24 + k:25 + k])
     V("ts", "pf7", "pf", T.pf[:, 7:8], r16, 15.0, 256.0, A.is_lt, A.mult)
     V("ts", "pf8", "pf", T.pf[:, 8:9], r16, 2.0, 1.0, A.mult, A.add)
     V("ts", "pf9", "pf", T.pf[:, 9:10], p32, U, None, A.mult)
-    V("tt", "pf4", "pf5 pf6", T.pf[:, 4:5], T.pf[:, 5:6], T.pf[:, 6:7], A.add)
     fix = T.pf[:, 7:8]
     V("ts", "dg2", "idw pf", T.dg1[:, 16:33], T.idw[:, 0:17], r16, 1024.0, A.is_equal, A.mult)
     V("ts", "rl16", "idw pf", T.rl16[:], T.idw[:, 0:32], 0.0, r16, A.mult, A.add)
@@ -216,35 +281,33 @@ def rank_program(g, core, T, topo):
     V("memset", "dg4", "", T.dg1[:, 48:49], 0.0)
     V("tt", "dgs", "dg2 dg3 dg4", T.dg1[:, 64:80], T.dg1[:, 16:32], T.dg1[:, 48:64], A.add)
     S("dg", "dgs rl16", T.dg[:, 0:512], (T.dg1[:, 64:80], T.rl16[:, 0:32]), ACT.Copy)
-    V("ts", "nmask", "rp pf", T.nmask[:], T.rp[:], r16, -1.0, A.is_equal, A.mult)
-    V("ts", "thr", "rp pf", T.thr[:], T.rp[:], r16, 1e29, A.not_equal, A.mult)
-    S("sc0", "rp", T.sc0[:], T.rp[:], ACT.Sign)
+    V("ts", "nmask", "rp pf", T.nmask[:], T.rp[:, 0:128], r16, -1.0, A.is_equal, A.mult)
+    V("ts", "thr", "rp pf", T.thr[:], T.rp[:, 0:128], r16, 1e29, A.not_equal, A.mult)
+    S("sc0_", "rp", T.sc0[:], T.rp[:, 0:128], ACT.Sign)
     S("scb", "rp", T.scb[:], T.rp[:], ACT.Sign)
     V("qz", "uq up", "ut", T.uq[:, 0:128], T.up[:, 0:128], T.ut[:, 0:512])
     V("cp", "uq2", "uq upl", T.uq2[:, 0:128].bitcast(dt.uint32), (T.uq[:, 0:128].bitcast(dt.uint32), T.upl[:, 0:8]))
     S("up2", "up upl", T.up2[:, 0:128], (T.up[:, 0:128], T.upl[:, 0:8]), ACT.Copy)
-    V("qz", "xq0", "xt", T.xq0[:, 0:256], T.xp0[:, 0:256], T.xt[:, 0:1024])
+    V("qz", "xq0a", "xta", T.xq0[:, 0:128], T.xp0[:, 0:128], T.xt[:, 0:512])
+    V("qz", "xq0b", "xt", T.xq0[:, 128:256], T.xp0[:, 128:256], T.xt[:, 512:1024])
     V("qz", "vq vp", "vt", T.vq[:, 0:128], T.vp[:, 0:128], T.vt[:, 0:512])
     V("cp", "lw16", "lw", T.lw16[:], T.lw[:])
     V("tt", "c0", "lw", T.c0[:, 31:512:32], T.lw[:, 16:32], T.lw[:, 0:16], A.subtract)
     V("cp", "c1o", "lw c1z", T.c1[:, 31:512:32], T.lw[:, 0:16])
 
-    iota("cla", T.cl[:, LN:LN + 256], [[2, 16], [-1, 2], [0, 8]], 1)
     parts = [(LS, 16, [[0, 4], [1, 2], [0, 2]], 0), (LP, 84, [[32, 2], [1, 6], [0, 7]], 2), (LP + 84, 84, [[32, 2], [0, 6], [1, 7]], 1),
-             (LP + 169, 24, [[8, 2], [32, 2], [1, 6]], 2), (LP + 193, 12, [[32, 2], [0, 6]], 0), (LQ, 84, [[32, 2], [0, 6], [1, 7]], 9),
-             (LQ + 84, 84, [[32, 2], [1, 6], [0, 7]], 10), (LV, 24, [[8, 2], [32, 2], [1, 6]], 1), (LX, 12, [[32, 2], [0, 6]], 1)]
+             (LP + 169, 24, [[64, 2], [32, 2], [1, 6]], 2), (LP + 193, 12, [[32, 2], [0, 6]], 0), (LQ, 84, [[32, 2], [0, 6], [1, 7]], 65),
+             (LQ + 84, 84, [[32, 2], [1, 6], [0, 7]], 66), (LV, 24, [[64, 2], [32, 2], [1, 6]], 1), (LX, 12, [[32, 2], [0, 6]], 64)]
     for k, (lo, n, pattern, base) in enumerate(parts):
         iota("cl%d" % (k + 1), T.cl[:, lo:lo + n], pattern, base, on="cl0")
-    iota("clx", T.cl[:, LP:LP + 169:7], [[0, 25]], 64, on="cl2 cl3")
-    iota("cly", T.cl[:, LQ:LQ + 169:7], [[0, 25]], 65, on="cl6 cl7")
-    iota("clz", T.cl[:, LV:LV + 24:6], [[0, 4]], 64, on="cl8")
+    iota("clx", T.cl[:, LP:LP + 169:7], [[0, 25]], 128, on="cl2 cl3")
+    iota("cly", T.cl[:, LQ:LQ + 169:7], [[0, 25]], 129, on="cl6 cl7")
+    iota("clz", T.cl[:, LV:LV + 24:6], [[0, 4]], 128, on="cl8")
 
     def wrap(lo, hi, key, reads):
         V("scan", key, reads + " dg", T.clo[:, lo:hi], T.dg[:, 0:hi - lo], T.cl[:, lo:hi], 0.0, A.add, A.min)
-    wrap(LN, LS, "cloa", "cla")
     wrap(LS, LQ, "clob", "cl1 cl4 cl5 clx")
     wrap(LQ, LE, "cloc", "cly clz cl9")
-    V("ts", "cl16a", "cloa pf7", T.cl16[:, 0:LS // 16], T.clo[:, 15:LS:16], fix, None, A.add)
     V("ts", "cl16b", "clob pf7", T.cl16[:, LS // 16:LP // 16], T.clo[:, LS + 15:LP:16], fix, None, A.add)
     V("ts", "cl16c", "clob cloc pf7 pf", T.cl16[:, LP // 16:LE // 16], T.clo[:, LP + 15:LE:16], fix, odd16, A.add, A.add)
 
@@ -252,9 +315,8 @@ def rank_program(g, core, T, topo):
         return T.cl16[:, lo // 16:(lo + n) // 16]
 
     iota("nT", T.nT[:, 0:16], [[32, 8], [0, 2]], 0)
-    iota("f1", T.f1[:], [[0, 256]], 0)
-    iota("f1a", T.f1[:, 0:256:16], [[0, 16]], 1, on="f1")
-    iota("f1b", T.f1[:, 1:256:16], [[0, 16]], 1, on="f1")
+    iota("f1", T.f1[:], [[0, 192]], 0)
+    iota("f1", T.f1[:, 0:192:12], [[0, 16]], 2)
     iota("nw0", T.nw[:, 0:16], [[16, 16]], 0)
     iota("tsz", T.tsel[:, 32:272], [[0, 240]], 0)
     iota("wt0", T.wt[:, 0:168], [[1, 2], [0, 84]], 8)
@@ -267,9 +329,9 @@ def rank_program(g, core, T, topo):
     iota("scab", T.scab[:, 0:24:6], [[0, 4]], 0)
     iota("ffc", T.ff[:, 0:24:6], [[0, 4]], 1)
     op("g", ["one"], ["et"], "asel", T.et[:], T.one[:], [[-1, 520]], A.is_equal, 0.0, 3, 4)
-    iota("t2c", T.t2[:, 64:96], [[0, 32]], 256)
-    iota("t2c", T.t2[:, 65:96:16], [[0, 2]], -5)
-    iota("pqz", T.pq[:, 256:264], [[0, 8]], 512)
+    iota("t2c", T.t2[:, 128:160], [[0, 2], [-1, 16]], 0)
+    iota("pqz", T.pq[:, 256:264], [[0, 8]], 256)
+    iota("pqy", T.pq[:, 520:528], [[0, 8]], 256)
     iota("gpz", T.gp[:, 208:224], [[0, 16]], 0)
     iota("de0", T.de[:], [[0, 200]], -16)
     iota("de1", T.de[:, 16:192:16], [[0, 11]], 239, on="de0")
@@ -285,6 +347,7 @@ def rank_program(g, core, T, topo):
     S("w256a", "idw", T.w256[:, 0:256], T.idw[:, 0:256], ACT.Identity, scale=256 * U, bias=-255 * 256 * U)
     S("w256b", "idw", T.w256[:, 256:512], T.idw[:, 0:256], ACT.Identity, scale=256 * U, bias=256 * U)
     S("nw1", "nw0 pf", T.nw[:, 16:32], T.nw[:, 0:16], ACT.Identity, bias=r16, scale=1.0)
+    S("nwb", "nw1", T.nwb[:], T.nw[:, 16:32], ACT.Copy)
     S("nw2", "nw1", T.nw[:, 32:48], T.nw[:, 16:32], ACT.Identity, bias=-0.5 * U, scale=U)
     S("nw3", "nw1", T.nw[:, 48:64], T.nw[:, 16:32], ACT.Copy, scale=-1024.0)
     S("md", "wt3 wt4 wt5", T.md[:, 0:169], T.wt[:, 0:169], ACT.Copy, scale=1.0 / 128)
@@ -310,43 +373,47 @@ def rank_program(g, core, T, topo):
         def issue():
             for out, in_ in pairs:
                 g.remote_dma(out, in_, T.sem[sem], T.sem.lc, pid, rid, emask)
-        note("g", [key], ["sent" + sem], "lc", nout * len(pairs), issue, 0.0, 300.0 * len(pairs))
+        note("g", key, ["sent" + sem], "lc", nout * len(pairs), issue, 0.0, 300.0 * len(pairs))
         note(None, ["sent" + sem], [arrives], sem, nin * len(pairs), None, length, 0.0)
 
     for t in range(R):
         xk = "xq%d" % t
         xq, xp = T[xk], T["xp%d" % t]
-        for k in ("ps1", "ps2"):
-            mm(k, T.uq2[:, 0:128], "uq2 up2", T.up2[:, 0:128], xq[:, 0:256], xk, xp[:, 0:256], 256)
-        send(xk, "ax%d" % t, "xn%d" % t, [(xq[:, 256:512].bitcast(dt.uint8), xq[:, 0:256].bitcast(dt.uint8)), (xp[:, 256:512], xp[:, 0:256])], FAR)
+        for h, (pv, pa) in enumerate((("ps1", "ps2"), ("ph0", "ph1"))):
+            lo, hi = 128 * h, 128 * h + 128
+            for k in (pv, pa):
+                mm(k, T.uq2[:, 0:128], "uq2 up2", T.up2[:, 0:128], xq[:, lo:hi], xk + "ab"[h], xp[:, lo:hi], 128)
+            V("tt", "c1e%d" % h, pv + " thr c1z", T.c1[:, 2 * lo:2 * hi:2], T[pv][:, 0:128], T.thr[:, 0:128], A.is_gt)
+            V("scan", "c2%d" % h, "c0 c0z c1o c1e%d" % h, T.c2[:, 2 * lo:2 * hi], T.c0[:, 2 * lo:2 * hi], T.c1[:, 2 * lo:2 * hi], 0.0, A.mult, A.add)
+            V("tt", "ms%d" % h, pv + " nmask", T.ms[:, lo:hi], T[pv][:, 0:128], T.nmask[:, 0:128], A.mult)
+            S("ssb%d" % h, pa, T.ssb[:, lo:hi], T[pa][:, 0:128], ACT.Copy)
+            V("scan", "sc%d" % h, "ms%d sc0_" % h, T.sc[:, lo:hi], T.sc0[:, 0:128], T.ms[:, lo:hi], 0.0, A.mult, A.add)
+        V("cp", "wc16", "c20 c21", T.wc16[:], T.c2[:, 31:512:32])
+        dma("y", "das", ["ssb0", "ssb1"], ["asc"], T.asc[0:128:16, :], T.ssb[0:128:16, :])
+        send([xk + "a", xk + "b"], "ax%d" % t, "xn%d" % t, [(xq[:, 256:512].bitcast(dt.uint8), xq[:, 0:256].bitcast(dt.uint8)), (xp[:, 256:512], xp[:, 0:256])], FAR)
         for b in range(4):
-            mm("pd%d" % b, T.eq[:, 128 * b:128 * b + 128], "eq%d" % b, T.ep[:, 128 * b:128 * b + 128], xq[:, 0:512], xk + " xn%d" % t, xp[:, 0:512], 512)
+            mm("pd%d" % b, T.eq[:, 128 * b:128 * b + 128], "eq%d" % b, T.ep[:, 128 * b:128 * b + 128], xq[:, 0:512], "%sa %sb xn%d" % (xk, xk, t), xp[:, 0:512], 512)
             S("f2_%d" % b, "pd%d" % b, T.f2[:, 272 * b:272 * b + 256], T["pd%d" % b][:, 256:512], ACT.Copy, scale=0.5)
             S("fw%d" % b, "pd%d" % b, T.fw[:, 256 * b:256 * b + 256], T["pd%d" % b][:, 0:256], ACT.Copy)
-        V("tt", "c1e", "ps1 thr c1z", T.c1[:, 0:512:2], T.ps1[:, 0:256], T.thr[:], A.is_gt)
-        V("scan", "c2", "c0 c0z c1e c1o", T.c2[:], T.c0[:], T.c1[:], 0.0, A.mult, A.add)
-        V("cp", "wc16", "c2", T.wc16[:], T.c2[:, 31:512:32])
-        V("tt", "ms", "ps1 nmask", T.ms[:], T.ps1[:, 0:256], T.nmask[:], A.mult)
-        S("ssb", "ps2", T.ssb[:], T.ps2[:, 0:256], ACT.Copy)
-        dma("y", "das", ["ssb"], ["asc"], T.asc[0:128:16, :], T.ssb[0:128:16, :])
-        dma("y", "dat", ["ssb"], ["asd"], T.asc[1:128:16, :], T.ssb[1:128:16, :])
-        V("scan", "sc", "ms sc0", T.sc[:], T.sc0[:], T.ms[:], 0.0, A.mult, A.add)
         for c in range(16):
-            S("jk%d acc%d" % (c, c), "ssb sc", T.jk[:, 256 * c:256 * c + 256], T.ssb[:], ACT.Sign, bias=T.sc[:, 16 * c + 15:16 * c + 16], scale=1.0, accum_out=T.acc[:, c:c + 1])
+            S("jk%d acc%d" % (c, c), "ssb0 ssb1 sc%d" % (c // 8), T.jk[:, 256 * c:256 * c + 256], T.ssb[:], ACT.Sign, bias=T.sc[:, 16 * c + 15:16 * c + 16], scale=1.0, accum_out=T.acc[:, c:c + 1])
         cur, key = adds[0], "a0"
         for k in range(1, 6):
             nxt = "va" if k % 2 else "vb"
-            V("tt", nxt, key + (" wc16 asc asd" if k == 5 else " wc16 a%d" % k), T[nxt][:], (cur, T.wc16[:, 0:16]), adds[k], A.add)
+            V("tt", nxt, key + (" wc16 asc" if k == 5 else " wc16 a%d" % k), T[nxt][:], (cur, T.wc16[:, 0:16]), adds[k], A.add)
             cur, key = T[nxt][:, 0:256], nxt
-        V("ts", "qp", key + " lw16 pf3 pf4", T.qp[:], (cur, T.lw16[:, 16:32]), T.pf[:, 3:4], T.pf[:, 4:5], A.mult, A.add)
-        V("tt", "pq", key + " lw16 qp", T.pq[:, 0:256], (cur, T.lw16[:, 0:16]), T.qp[:], A.max)
-        V("tr", "t3", "pq", T.t3[:], T.pq[:, 0:256])
-        V("cp", "t5", "t3", T.nT[:, 48:80], T.t3[:, 7:256:8])
-        V("tt", "f1k", "t3", T.nT[:, 16:32], T.t3[:, 2:256:16], T.t3[:, 10:256:16], A.is_equal)
-        V("tt", "ur", "t3 t5 cl16a", T.ur[:], (T.nT[:, 48:80], lst(LN, 256)), T.t3[:], A.not_equal)
-        V("scan", "wr", "ur f1a f1b", T.wr[:], T.ur[:], T.f1[:], 1.0, A.min, A.max)
+        V("cp", "pq0", key + " lw16", T.pq[:, 0:256], (cur, T.lw16[:, 0:16]))
+        lift[0] = 1000.0
+        S("pq1", key + " lw16", T.pq[:, 264:520], (cur, T.lw16[:, 16:32]), ACT.Copy)
+        lift[0] = 0.0
+        V("tr", "t3p", "pq0", T.t3[:, 0:16, :], T.pq[:, 0:256])
+        V("tr", "t3q", "pq1", T.t3[:, 16:32, :], T.pq[:, 264:520])
+        V("tt", "ne0", "t3p t3q", T.ne[:, 0:192:2], T.t3[:, 0:16, 2:8], T.t3[:, 16:32, 8:14], A.not_equal)
+        V("tt", "ne1", "t3p t3q", T.ne[:, 1:192:2], T.t3[:, 0:16, 8:14], T.t3[:, 16:32, 2:8], A.not_equal)
+        V("tt", "f1k", "t3p t3q", T.nT[:, 16:32], T.t3[:, 0:16, 2], T.t3[:, 16:32, 2], A.is_equal)
+        V("scan", "no", "ne0 ne1 f1", T.no[:], T.f1[:], T.ne[:], 1.0, A.add, A.min)
         V("tt", "f1m", "f1k nT", T.nT[:, 32:48], T.nT[:, 16:32], T.nT[:, 0:16], A.max)
-        V("tt", "f0", "wr f1m", T.f0[:, 0:256:16], T.wr[:, 15:256:16], T.nT[:, 32:48], A.max)
+        V("tt", "f0", "no f1m", T.f0[:, 0:256:16], T.no[:, 11:192:12], T.nT[:, 32:48], A.max)
         V("scan", "fo", "f0 scb", T.fo[:], T.scb[:], T.f0[:], 0.0, A.mult, A.add)
         V("tr", "wr", "fo", T.wr[:], T.fo[:])
         accs = names("acc", 0, 16)
@@ -367,11 +434,13 @@ def rank_program(g, core, T, topo):
         S("kv1", "qq", T.qj[:], T.qq[:], ACT.Relu, scale=-1.0, accum_out=T.kv[:, 1:2])
         V("red", "kv0", "qq", T.kv[:, 0:1], T.qq[:], XAX, A.max)
         V("ts", "off", "kv0 kv1 cl16b", T.off[:], (T.kv[:, 0:2], lst(LS, 16)), -1.0, 256.0, A.mult, A.add)
-        V("cp", "g2", "pqz pq off", T.g2[:], (T.pq[:, 0:264], T.off[:, 0:4]))
-        V("tr", "t2", "g2", T.t2[:, 0:64], T.g2[:])
-        t2 = T.t2[:, 0:96]
-        V("cp", "gp", "t2 t2c cl16c", T.gp[:, 0:208], (t2, lst(LP, 208)))
-        V("tt", "ee", "t2 t2c cl16c gp", T.ee[:], (t2, lst(LQ, 176)), T.gp[:, 0:176], A.is_equal)
+        V("cp", "g20", "pqz pq0 off", T.g2[:, 0:64], (T.pq[:, 0:264], T.off[:, 0:4]))
+        S("g21", "pqy pq1 off", T.g2[:, 64:128], (T.pq[:, 264:528], T.off[:, 0:4]), ACT.Copy)
+        V("tr", "t2", "g20 g21", T.t2[:, 0:128], T.g2[:])
+        t2 = T.t2[:, 0:160]
+        V("cp", "gpa", "t2 t2c cl16c", T.gp[:, 0:96], (t2, lst(LP, 96)))
+        S("gp", "t2 t2c cl16c", T.gp[:, 96:208], (t2, lst(LP + 96, 112)), ACT.Copy)
+        V("tt", "ee", "t2 t2c cl16c gp gpa", T.ee[:], (t2, lst(LQ, 176)), T.gp[:, 0:176], A.is_equal)
         V("tt", "nd", "t2 t2c cl16c gp", T.nd[:], (t2, lst(LV, 32)), T.gp[:, 169:201], A.subtract)
         V("scan", "so", "ee md", T.so[:, 0:169], T.md[:, 0:169], T.ee[:, 0:169], 0.0, A.add, A.max)
         V("tt", "br", "t2 t2c cl16c gp gpz", T.abi[:, 0:32:2], (t2, lst(LX, 16)), T.gp[:, 193:209], A.is_gt)
@@ -379,17 +448,21 @@ def rank_program(g, core, T, topo):
             V("ts", "ff%d" % s, "so", T.ff[:, 6 * s + 1:6 * s + 6], T.so[:, 42 * s + 7:42 * s + 42:7], T.so[:, 42 * s + 42:42 * s + 43], None, A.is_lt)
         V("tt", "d2", "nd ffc ff0 ff1 ff2 ff3", T.d2[:], T.nd[:, 0:24], T.ff[:], A.mult)
         V("scan", "ab", "d2 scab", T.abi[:, 1:48:2], T.scab[:], T.d2[:], 0.0, A.mult, A.subtract)
+        lift[0] = 1000.0
         V("cp", "ab%d" % t, "ab", T.ab[:, 24 * t:24 * t + 24], T.abi[:, 1:48:2])
-        send("ab%d" % t, "al%d" % t, "la%d" % t, [(T.la[:, 24 * t:24 * t + 24], T.ab[:, 24 * t:24 * t + 24])], NEAR)
+        lift[0] = 0.0
+        send(["ab%d" % t], "al%d" % t, "la%d" % t, [(T.la[:, 24 * t:24 * t + 24], T.ab[:, 24 * t:24 * t + 24])], NEAR)
         V("tt", "b0", "ab b0", T.b0[:, 1:24:2], T.abi[:, 25:48:2], T.abi[:, 1:24:2], A.subtract)
         V("scan", "bti", "b0 ab br", T.bti[:], T.b0[:], T.abi[:, 0:24], 0.0, A.mult, A.add)
         V("cp", "bt16", "bti", T.bt16[:], T.bti[:, 1:24:2])
         V("cp", "btv", "idb bt16", T.btv[:], (T.idb[:, 0:272], T.bt16[:, 0:12]))
         for c in range(16):
             if c < NE:
+                lift[0] = 1000.0
                 S("abd%d" % c, "btv nw3", T.abd[:, c, 0:192], T.btv[:], ACT.Abs, bias=T.nw[:, 48 + c:49 + c], scale=1024.0)
+                lift[0] = 0.0
             else:
-                V("ts", "abd%d" % c, "btv nw1", T.abd[:, c, 0:192], T.btv[:], T.nw[:, 16 + c:17 + c], 1024.0, A.not_equal, A.mult)
+                V("ts", "abd%d" % c, "btv nwb", T.abd[:, c, 0:192], T.btv[:], T.nwb[:, c:c + 1], 1024.0, A.not_equal, A.mult)
             V("scan", "ev%d" % c, "abz de1 de2 abd%d" % c, T.abo[:, c, 0:193], T.de[:, 0:193], T.abd[:, c, 0:193], 252.0, A.add, A.min)
         V("ts", "ei", names("ev", 0, 16), T.ei[:, 0:16], T.abo[:, :, 192], 16.0, None, A.mult)
         V("ts", "ek", "ei", T.ei[:, 16:32], T.ei[:, 0:16], 255, None, A.bitwise_and)
@@ -419,21 +492,34 @@ def rank_program(g, core, T, topo):
         for b in range(4):
             mm(ph[b], T.wq[:, 128 * b:128 * b + 128], "wq wp", T.wp[:, 128 * b:128 * b + 128], T.zq[:, 0:192], "zq zp", T.zp[:, 0:192], 192)
             S("hb%d" % b, ph[b], T.hb[:, 208 * b:208 * b + 192], T[ph[b]][:, 0:192], ACT.Copy, scale=0.03125)
-            V("tt", "xs%d" % b, "hbz%d hb%d e16 fw%d" % (b, b, b), T.xs[:, b:1024:4], (T.hb[:, 208 * b:208 * b + 208], T.e16[:, 0:16]), T.fw[:, 256 * b:256 * b + 256], A.add)
-        V("qz", "xq%d" % (t + 1), "xs0 xs1 xs2 xs3", T["xq%d" % (t + 1)][:, 0:256], T["xp%d" % (t + 1)][:, 0:256], T.xs[:, 0:1024])
+        for h in range(2):
+            lo, hi = 128 * h, 128 * h + 128
+            for b in range(4):
+                if b == 3:
+                    V("tt", "xs3%d" % h, "hbz3 hb3 e16 fw3", T.xs[:, 4 * lo + 3:4 * hi:4], (T.hb[:, 624:832], T.e16[:, 8 * h:8 * h + 8]), T.fw[:, 768 + lo:768 + hi], A.add)
+                elif h == 0:
+                    V("tt", "xs%d0 xs%d1" % (b, b), "hbz%d hb%d e16 fw%d" % (b, b, b), T.xs[:, b:1024:4], (T.hb[:, 208 * b:208 * b + 208], T.e16[:, 0:16]),
+                      T.fw[:, 256 * b:256 * b + 256], A.add)
+        for h in range(2):
+            lo, hi = 128 * h, 128 * h + 128
+            V("qz", "xq%d" % (t + 1) + "ab"[h], " ".join("xs%d%d" % (b, h) for b in range(4)), T["xq%d" % (t + 1)][:, lo:hi], T["xp%d" % (t + 1)][:, lo:hi], T.xs[:, 4 * lo:4 * hi])
     xk = "xq%d" % R
     xq, xp = T[xk], T["xp%d" % R]
     S("olr", "lt", T.olr[:], T.lt[:, 0:512], ACT.Copy)
     dma("y", "ool", ["olr"], [], T.ol[:], T.olr[0:128:16, :])
-    mm("ps1", T.vq[:, 0:128], "vq vp", T.vp[:, 0:128], xq[:, 0:256], xk, xp[:, 0:256], 256)
-    dma("y", "ooc", [xk], [], T.oc[:, 0:1024], xq[:, 0:256].bitcast(dt.uint8), 2800.0)
+    for h, pa in enumerate(("ps1", "ps2")):
+        lo, hi = 128 * h, 128 * h + 128
+        mm(pa, T.vq[:, 0:128], "vq vp", T.vp[:, 0:128], xq[:, lo:hi], xk + "ab"[h], xp[:, lo:hi], 128)
+        dma("y", "oc%d" % h, [xk + "ab"[h]], [], T.oc[:, 4 * lo:4 * hi], xq[:, lo:hi].bitcast(dt.uint8), 2500.0)
+        S("ms%d" % h, pa, T.ms[:, lo:hi], T[pa][:, 0:128], ACT.Copy)
+        dma("s", "oy%d" % h, ["ms%d" % h], [], T.y[:, lo:hi], T.ms[:, lo:hi], 2500.0)
     for k in range(4):
-        dma("ys"[k % 2], "os%d" % k, [xk], [], T.osc[4 * k:4 * k + 4, 0:256], xp[32 * k:32 * k + 4, 0:256])
-    S("kv1", "ps1", T.qj[:], T.ps1[:, 0:256], ACT.Copy)
-    dma("s", "oy", ["kv1"], [], T.y[:], T.qj[:], 2800.0)
+        dma("y", "os%d" % k, [xk + "a", xk + "b"], [], T.osc[4 * k:4 * k + 4, 0:256], xp[32 * k:32 * k + 4, 0:256])
 
     total, waited = {}, {q: {} for q in queues}
-    for i in in_order(calls):
+    if len(calls) not in ORDER:
+        ORDER[len(calls)] = in_order(calls)
+    for i in ORDER[len(calls)]:
         c = calls[i]
         if c["q"] is not None:
             best = {}

@@ -5,10 +5,11 @@ N = 8
 R = 3
 C = 256
 NS = 9
-NE = 7
+NE = 6
 U = 2.0 ** -18
-CYC, LAT, DMA, NEAR, FAR, SLACK = 0.85, 220.0, 2100.0, 2200.0, 3500.0, 100.0
-SEED, SPREAD, STEPS, GIVE, SOONER = 1, 0.0, 3000, 150.0, 700.0
+CYC, LAT, DMA, NEAR, FAR, SLACK = 0.85, 220.0, 1800.0, 1500.0, 3500.0, 100.0
+SEED, SPREAD, STEPS, GIVE, SOONER = 1, 0.0, 3000, 100.0, 500.0
+BEHIND = 0.0
 ORDER = {}
 F32, BF, I32, U16, U8, X4 = "float32", "bfloat16", "int32", "uint16", "uint8", "float8_e4m3fn_x4"
 
@@ -19,28 +20,28 @@ def _sb(n, d):
 
 SCRATCH = {
     "xt": _sb(1024, BF), "xs": _sb(1024, BF), "ut": _sb(512, BF), "vt": _sb(512, BF), "et": _sb(520, BF),
-    "one": _sb(520, BF), "rl16": _sb(32, U16),
+    "rl16": _sb(32, U16),
     "uq": _sb(128, X4), "up": _sb(128, U8), "uq2": _sb(128, X4),
     "up2": _sb(128, U8), "vq": _sb(128, X4), "vp": _sb(128, U8), "eq": _sb(512, X4), "ep": _sb(512, U8),
     "wq": _sb(512, X4), "wp": _sb(512, U8),
     "zt": _sb(768, BF), "zq": _sb(192, X4), "zp": _sb(192, U8),
-    "pi": _sb(4, I32), "pf": _sb(16, F32), "sm": _sb(96, F32), "idw": _sb(272, F32), "idb": _sb(272, BF), "rp": _sb(256, F32),
+    "pi": _sb(4, I32), "pf": _sb(16, F32), "sm": _sb(96, F32), "idw": _sb(272, F32), "idb": _sb(272, BF), "rp": _sb(128, F32),
     "nmask": _sb(128, F32), "thr": _sb(128, F32), "sc0": _sb(128, F32), "nw": _sb(64, F32), "nwb": _sb(16, BF), "nT": _sb(96, F32),
-    "scab": _sb(24, F32), "upl": _sb(8, U16), "w256": _sb(512, F32), "tsel": _sb(272, F32),
+    "scab": _sb(48, F32), "upl": _sb(8, U16), "w256": _sb(512, F32), "tsel": _sb(272, F32),
     "dg": _sb(512, BF), "dg1": _sb(80, BF), "cl": _sb(784, BF), "clo": _sb(784, BF),
     "cl16": _sb(50, U16), "wt": _sb(176, F32), "md": _sb(176, BF), "de": _sb(200, BF), "cm": _sb(2, F32),
     "aa": _sb(1280, F32), "asc": _sb(256, F32),
     "ms": _sb(256, F32), "sc": _sb(256, F32), "ssb": _sb(256, F32), "c0": _sb(512, BF), "c1": _sb(512, BF), "c2": _sb(512, BF),
     "wc16": _sb(16, U16), "va": _sb(256, F32), "vb": _sb(256, F32), "pq": _sb(528, F32),
-    "t3": ("sbuf", [128, 32, 16], F32), "ab": _sb(72, U16), "la": _sb(72, U16),
+    "pb": _sb(512, BF), "t3": ("sbuf", [128, 32, 16], BF), "ab": _sb(72, U16), "la": _sb(72, U16),
     "f0": _sb(256, BF), "f1": _sb(192, BF), "ne": _sb(192, BF), "no": _sb(192, BF), "fo": _sb(256, BF), "scb": _sb(256, BF),
     "wr": _sb(256, BF), "ur": _sb(256, BF), "jk": _sb(4096, BF), "jo": _sb(4096, BF), "acc": _sb(16, F32), "acc2": _sb(16, F32),
     "a16": _sb(16, U16), "nB": _sb(32, F32), "kap": _sb(256, F32), "r16": _sb(16, U16),
     "qq": _sb(256, F32), "qj": _sb(256, F32), "kv": _sb(2, F32), "off": _sb(16, U16), "g2": _sb(128, F32), "t2": _sb(160, F32),
-    "gp": _sb(224, F32), "ee": _sb(176, BF), "so": _sb(176, BF), "nd": _sb(32, F32), "ff": _sb(24, F32), "d2": _sb(24, F32),
-    "abi": _sb(48, F32), "b0": _sb(24, F32), "bti": _sb(24, F32), "bt16": _sb(12, U16),
+    "gp": _sb(224, F32), "ee": _sb(176, BF), "so": _sb(176, BF), "nd": _sb(48, F32), "ff": _sb(24, F32), "d2": _sb(48, F32),
+    "abi": _sb(48, F32), "bq": _sb(32, F32), "bt16": _sb(12, U16),
     "btv": _sb(192, BF), "abd": ("sbuf", [128, 16, 200], BF), "abo": ("sbuf", [128, 16, 200], BF),
-    "ei": _sb(64, I32), "e16": _sb(16, U16),
+    "ei": _sb(64, F32), "ek": _sb(32, BF), "e16": _sb(16, U16),
     "li": _sb(12, F32), "ln16": _sb(2, U16), "m16": _sb(2, U16), "mt": _sb(32, BF), "lt": _sb(544, BF), "lo": _sb(512, BF),
     "lw": _sb(32, I32), "lw16": _sb(32, U16), "olr": _sb(512, F32),
     "at": _sb(768, BF), "f2": _sb(1088, BF), "fw": _sb(1024, BF), "hb": _sb(832, F32),
@@ -55,7 +56,7 @@ for _n in PS:
 DMAS = ["dx0", "dx1", "du", "dv", "dwc", "dws", "dn0", "das", "oy0", "oy1", "ool", "oc0", "oc1", "os0", "os1", "os2", "os3"]
 SEMAPHORES = ["sv", "ss", "sp", "sg", "lc"] + ["ax%d" % t for t in range(R)] + ["al%d" % t for t in range(R)] + DMAS
 
-LS, LP, LQ, LV, LX, LE = 0, 32, 256, 448, 480, 496
+LS, LF, LP, LQ, LV, LX, LE = 0, 32, 96, 320, 512, 544, 560
 
 
 def width(ap):
@@ -70,7 +71,7 @@ def in_order(calls):
             after[d].append(i)
     chain = [0.0] * n
     for i in range(n - 1, -1, -1):
-        chain[i] = calls[i]["len"] + max([LAT + chain[k] for k in after[i]] + [0.0])
+        chain[i] = calls[i]["len"] + calls[i]["load"] + max([LAT + chain[k] for k in after[i]] + [0.0])
     x = SEED
     for i in range(n):
         x = (x * 1103515245 + 12345) % 2147483648
@@ -84,7 +85,7 @@ def in_order(calls):
         q = calls[first]["q"]
         best = first
         for i in ready:
-            if calls[i]["q"] == q and chain[i] > chain[best] and start[i] <= start[first] + max(0.0, min(calls[first]["hold"] - SLACK, chain[i] - chain[first])):
+            if calls[i]["q"] == q and chain[i] > chain[best] and start[i] <= start[first] + max(0.0, min(calls[first]["hold"] - SLACK + 0.3 * calls[i]["lift"], chain[i] - chain[first])):
                 best = i
         if q is None:
             best = first
@@ -173,7 +174,7 @@ def rank_program(g, core, T, topo):
     ACT = ActivationFunctionType
     XAX = AxisListType.X
     queues = {"v": g.vector, "s": g.scalar, "p": g.tensor, "g": g, "y": g.sync}
-    calls, wr, rd, lift = [], {}, {}, [0.0]
+    calls, wr, rd, lift = [], {}, {}, [0.0, 0.0]
 
     def note(q, reads, writes, sem, inc, issue, length, hold):
         deps = set()
@@ -187,7 +188,7 @@ def rank_program(g, core, T, topo):
                 deps.add(wr[k])
             deps.update(rd.get(k, []))
         i = len(calls)
-        calls.append({"q": q, "deps": sorted(deps), "sem": sem, "inc": inc, "issue": issue, "len": length, "hold": hold, "lift": lift[0]})
+        calls.append({"q": q, "deps": sorted(deps), "sem": sem, "inc": inc, "issue": issue, "len": length, "hold": hold, "lift": lift[0], "load": lift[1]})
         for k in writes:
             wr[k] = i
             rd[k] = []
@@ -205,7 +206,7 @@ def rank_program(g, core, T, topo):
         args = [a[0].indirect(a[1]) if isinstance(a, tuple) else a for a in args]
         if picks:
             n = width(args[1 - picks[0]])
-            length = 55.0 + (1.56 if picks[0] else 3.8) * CYC * n
+            length = (50.0 if q == "v" else 65.0) + (1.56 if picks[0] else 3.8) * CYC * n
         elif name == "qz":
             length = 12.0 + 0.22 * width(args[2])
         elif name == "mm":
@@ -213,7 +214,7 @@ def rank_program(g, core, T, topo):
         elif name in ("iota", "asel"):
             length = 140.0 + 2 * CYC * width(args[0])
         elif name == "act":
-            length = 50.0 + CYC * max(64, width(args[0]))
+            length = (60.0 if "accum_out" in kw else 40.0) + CYC * max(64, width(args[0]))
         else:
             sides = {"memset": 1, "tt": 3, "scan": 3}.get(name, 2)
             each = 0.5 if name != "red" and all("16" in str(a.dtype) for a in args[:sides]) else 1.0
@@ -241,10 +242,10 @@ def rank_program(g, core, T, topo):
     def names(stem, lo, hi):
         return " ".join(stem + str(c) for c in range(lo, hi))
 
-    dma("y", "dx0", [], ["xta"], T.xt[:, 0:512], T.x[:, 0:512], 3000.0)
-    dma("s", "du", [], ["ut"], T.ut[:], T.u[:], 2900.0)
-    dma("y", "dx1", [], ["xt"], T.xt[:, 512:1024], T.x[:, 512:1024], 3300.0)
-    dma("s", "dn0", [], ["lw"], T.lw[:], T.nb[:], 2500.0)
+    dma("y", "du", [], ["ut"], T.ut[:], T.u[:], 1600.0)
+    dma("s", "dx0", [], ["xta"], T.xt[:, 0:512], T.x[:, 0:512], 1900.0)
+    dma("y", "dx1", [], ["xt"], T.xt[:, 512:1024], T.x[:, 512:1024], 2100.0)
+    dma("s", "dn0", [], ["lw"], T.lw[:], T.nb[:], 1900.0)
     dma("y", "dwc", ["xt"], ["wq"], T.wq[:, 0:512].bitcast(dt.uint8), T.wc[:], 3300.0)
     dma("y", "dws", ["xt"], ["wp"], T.wp[:, 0:512], T.ws[:], 2700.0)
     dma("y", "dv", ["xt"], ["vt"], T.vt[:], T.v[:], 2900.0)
@@ -253,7 +254,7 @@ def rank_program(g, core, T, topo):
     iota("sm1", T.sm[:, 8:14], [[-1, 6]], 7)
     iota("idw", T.idw[:], [[1, 272]], 0)
     iota("sm0", T.sm[:, 0:8], [[16, 8]], 0)
-    iota("rp", T.rp[:], [[0, 16], [1, 16]], 0)
+    iota("rp", T.rp[:], [[0, 8], [1, 16]], 0)
     V("memset", "f0", "", T.f0[:], 0.0)
     V("ts", "pi1", "pi", T.pi[:, 1:2], T.pi[:, 0:1], 15, None, A.bitwise_and)
     V("ts", "pi2", "pi", T.pi[:, 2:3], T.pi[:, 0:1], 31, None, A.bitwise_and)
@@ -262,7 +263,7 @@ def rank_program(g, core, T, topo):
     r16, p32, odd16 = T.pf[:, 0:1], T.pf[:, 1:2], T.pf[:, 2:3]
     V("ts", "smS", "sm1 pf", T.sm[:, 25:30], T.sm[:, 9:14], r16, None, A.is_equal)
     V("ts", "smT", "pf", T.sm[:, 24:25], r16, 7.0, None, A.is_ge)
-    V("memset", "one", "", T.one[:], 1.0)
+    V("memset", "one", "", T.jo[:, 0:520], 1.0)
     V("memset", "cl0", "", T.cl[:, LS:LE], 0.0)
     V("memset", "c0", "", T.c0[:], 1.0)
     V("memset", "c0z", "c0", T.c0[:, 0:512:32], 0.0)
@@ -284,7 +285,8 @@ def rank_program(g, core, T, topo):
     V("ts", "nmask", "rp pf", T.nmask[:], T.rp[:, 0:128], r16, -1.0, A.is_equal, A.mult)
     V("ts", "thr", "rp pf", T.thr[:], T.rp[:, 0:128], r16, 1e29, A.not_equal, A.mult)
     S("sc0_", "rp", T.sc0[:], T.rp[:, 0:128], ACT.Sign)
-    S("scb", "rp", T.scb[:], T.rp[:], ACT.Sign)
+    S("sca", "rp", T.scb[:, 0:128], T.rp[:], ACT.Sign)
+    S("scb", "rp", T.scb[:, 128:256], T.rp[:], ACT.Sign)
     V("qz", "uq up", "ut", T.uq[:, 0:128], T.up[:, 0:128], T.ut[:, 0:512])
     V("cp", "uq2", "uq upl", T.uq2[:, 0:128].bitcast(dt.uint32), (T.uq[:, 0:128].bitcast(dt.uint32), T.upl[:, 0:8]))
     S("up2", "up upl", T.up2[:, 0:128], (T.up[:, 0:128], T.upl[:, 0:8]), ACT.Copy)
@@ -297,7 +299,8 @@ def rank_program(g, core, T, topo):
 
     parts = [(LS, 16, [[0, 4], [1, 2], [0, 2]], 0), (LP, 84, [[32, 2], [1, 6], [0, 7]], 2), (LP + 84, 84, [[32, 2], [0, 6], [1, 7]], 1),
              (LP + 169, 24, [[64, 2], [32, 2], [1, 6]], 2), (LP + 193, 12, [[32, 2], [0, 6]], 0), (LQ, 84, [[32, 2], [0, 6], [1, 7]], 65),
-             (LQ + 84, 84, [[32, 2], [1, 6], [0, 7]], 66), (LV, 24, [[64, 2], [32, 2], [1, 6]], 1), (LX, 12, [[32, 2], [0, 6]], 64)]
+             (LQ + 84, 84, [[32, 2], [1, 6], [0, 7]], 66), (LV, 24, [[64, 2], [32, 2], [1, 6]], 1), (LX, 12, [[32, 2], [0, 6]], 64),
+             (LF, 24, [[1, 24]], 0), (LF + 24, 24, [[6, 2], [1, 6], [12, 2]], 0)]
     for k, (lo, n, pattern, base) in enumerate(parts):
         iota("cl%d" % (k + 1), T.cl[:, lo:lo + n], pattern, base, on="cl0")
     iota("clx", T.cl[:, LP:LP + 169:7], [[0, 25]], 128, on="cl2 cl3")
@@ -306,7 +309,7 @@ def rank_program(g, core, T, topo):
 
     def wrap(lo, hi, key, reads):
         V("scan", key, reads + " dg", T.clo[:, lo:hi], T.dg[:, 0:hi - lo], T.cl[:, lo:hi], 0.0, A.add, A.min)
-    wrap(LS, LQ, "clob", "cl1 cl4 cl5 clx")
+    wrap(LS, LQ, "clob", "cl1 cl4 cl5 clx cl10 cl11")
     wrap(LQ, LE, "cloc", "cly clz cl9")
     V("ts", "cl16b", "clob pf7", T.cl16[:, LS // 16:LP // 16], T.clo[:, LS + 15:LP:16], fix, None, A.add)
     V("ts", "cl16c", "clob cloc pf7 pf", T.cl16[:, LP // 16:LE // 16], T.clo[:, LP + 15:LE:16], fix, odd16, A.add, A.add)
@@ -325,10 +328,11 @@ def rank_program(g, core, T, topo):
     iota("wt3", T.wt[:, 7:85:7], [[0, 2], [-9, 6]], -40, on="wt0")
     iota("wt4", T.wt[:, 91:169:7], [[0, 2], [-8, 6]], -45, on="wt0")
     iota("wt5", T.wt[:, 1:169:42], [[0, 4]], -256, on="wt1 wt2")
-    iota("scab", T.scab[:], [[0, 24]], 1)
-    iota("scab", T.scab[:, 0:24:6], [[0, 4]], 0)
+    iota("scab0", T.scab[:], [[0, 48]], 1)
+    iota("scab1", T.scab[:, 0:24:6], [[0, 4]], 0, on="scab0")
+    iota("scab2", T.scab[:, 24:48:12], [[0, 2]], 0, on="scab0")
     iota("ffc", T.ff[:, 0:24:6], [[0, 4]], 1)
-    op("g", ["one"], ["et"], "asel", T.et[:], T.one[:], [[-1, 520]], A.is_equal, 0.0, 3, 4)
+    op("g", ["one"], ["et"], "asel", T.et[:], T.jo[:, 0:520], [[-1, 520]], A.is_equal, 0.0, 3, 4)
     iota("t2c", T.t2[:, 128:160], [[0, 2], [-1, 16]], 0)
     iota("pqz", T.pq[:, 256:264], [[0, 8]], 256)
     iota("pqy", T.pq[:, 520:528], [[0, 8]], 256)
@@ -337,7 +341,8 @@ def rank_program(g, core, T, topo):
     iota("de1", T.de[:, 16:192:16], [[0, 11]], 239, on="de0")
     iota("de2", T.de[:, 0:193:192], [[251, 2]], 0, on="de0")
     iota("cm", T.cm[:], [[1, 2]], -1)
-    iota("b0", T.b0[:], [[0, 24]], 0)
+    iota("ekz", T.ek[:, 0:32:2], [[0, 16]], 0)
+    iota("emz", T.ei[:, 0:32:2], [[0, 16]], -255)
     iota("ltz", T.lt[:, 512:544], [[0, 32]], 0)
     iota("abz", T.abd[:, :, 192], [[0, 16]], 1024)
     for b in range(4):
@@ -348,7 +353,7 @@ def rank_program(g, core, T, topo):
     S("w256b", "idw", T.w256[:, 256:512], T.idw[:, 0:256], ACT.Identity, scale=256 * U, bias=256 * U)
     S("nw1", "nw0 pf", T.nw[:, 16:32], T.nw[:, 0:16], ACT.Identity, bias=r16, scale=1.0)
     S("nwb", "nw1", T.nwb[:], T.nw[:, 16:32], ACT.Copy)
-    S("nw2", "nw1", T.nw[:, 32:48], T.nw[:, 16:32], ACT.Identity, bias=-0.5 * U, scale=U)
+    S("nw2", "nw1", T.nw[:, 32:48], T.nw[:, 16:32], ACT.Identity, bias=-0.5, scale=1.0)
     S("nw3", "nw1", T.nw[:, 48:64], T.nw[:, 16:32], ACT.Copy, scale=-1024.0)
     S("md", "wt3 wt4 wt5", T.md[:, 0:169], T.wt[:, 0:169], ACT.Copy, scale=1.0 / 128)
     S("idb", "idw", T.idb[:], T.idw[:], ACT.Copy)
@@ -396,40 +401,44 @@ def rank_program(g, core, T, topo):
             S("f2_%d" % b, "pd%d" % b, T.f2[:, 272 * b:272 * b + 256], T["pd%d" % b][:, 256:512], ACT.Copy, scale=0.5)
             S("fw%d" % b, "pd%d" % b, T.fw[:, 256 * b:256 * b + 256], T["pd%d" % b][:, 0:256], ACT.Copy)
         for c in range(16):
+            lift[1] = 280.0 * (15 - c) + (400.0 if c < 12 else 0.0)
             S("jk%d acc%d" % (c, c), "ssb0 ssb1 sc%d" % (c // 8), T.jk[:, 256 * c:256 * c + 256], T.ssb[:], ACT.Sign, bias=T.sc[:, 16 * c + 15:16 * c + 16], scale=1.0, accum_out=T.acc[:, c:c + 1])
         cur, key = adds[0], "a0"
         for k in range(1, 6):
             nxt = "va" if k % 2 else "vb"
             V("tt", nxt, key + (" wc16 asc" if k == 5 else " wc16 a%d" % k), T[nxt][:], (cur, T.wc16[:, 0:16]), adds[k], A.add)
             cur, key = T[nxt][:, 0:256], nxt
-        V("cp", "pq0", key + " lw16", T.pq[:, 0:256], (cur, T.lw16[:, 0:16]))
+        V("cp", "pb0", key + " lw16", T.pb[:, 0:256], (cur, T.lw16[:, 0:16]))
         lift[0] = 1000.0
-        S("pq1", key + " lw16", T.pq[:, 264:520], (cur, T.lw16[:, 16:32]), ACT.Copy)
+        S("pb1", key + " lw16", T.pb[:, 256:512], (cur, T.lw16[:, 16:32]), ACT.Copy)
         lift[0] = 0.0
-        V("tr", "t3p", "pq0", T.t3[:, 0:16, :], T.pq[:, 0:256])
-        V("tr", "t3q", "pq1", T.t3[:, 16:32, :], T.pq[:, 264:520])
+        S("pq0", key + " lw16", T.pq[:, 0:256], (cur, T.lw16[:, 0:16]), ACT.Copy)
+        S("pq1", key + " lw16", T.pq[:, 264:520], (cur, T.lw16[:, 16:32]), ACT.Copy)
+        V("tr", "t3p", "pb0", T.t3[:, 0:16, :], T.pb[:, 0:256])
+        V("tr", "t3q", "pb1", T.t3[:, 16:32, :], T.pb[:, 256:512])
         V("tt", "ne0", "t3p t3q", T.ne[:, 0:192:2], T.t3[:, 0:16, 2:8], T.t3[:, 16:32, 8:14], A.not_equal)
         V("tt", "ne1", "t3p t3q", T.ne[:, 1:192:2], T.t3[:, 0:16, 8:14], T.t3[:, 16:32, 2:8], A.not_equal)
         V("tt", "f1k", "t3p t3q", T.nT[:, 16:32], T.t3[:, 0:16, 2], T.t3[:, 16:32, 2], A.is_equal)
         V("scan", "no", "ne0 ne1 f1", T.no[:], T.f1[:], T.ne[:], 1.0, A.add, A.min)
         V("tt", "f1m", "f1k nT", T.nT[:, 32:48], T.nT[:, 16:32], T.nT[:, 0:16], A.max)
         V("tt", "f0", "no f1m", T.f0[:, 0:256:16], T.no[:, 11:192:12], T.nT[:, 32:48], A.max)
-        V("scan", "fo", "f0 scb", T.fo[:], T.scb[:], T.f0[:], 0.0, A.mult, A.add)
+        V("scan", "fo", "f0 sca scb", T.fo[:], T.scb[:], T.f0[:], 0.0, A.mult, A.add)
         V("tr", "wr", "fo", T.wr[:], T.fo[:])
         accs = names("acc", 0, 16)
         V("ts", "a16", accs, T.a16[:], T.acc[:], 255.0, None, A.add)
-        V("ts", "nb0", accs, T.nB[:, 16:32], T.acc[:], -256.0 * U, None, A.mult)
+        V("ts", "nb0", accs, T.nB[:, 16:32], T.acc[:], 256.0, None, A.mult)
         V("tt", "kap", "a16 w256a w256b wr", T.kap[:], (T.w256[:, 0:512], T.a16[:, 0:16]), T.wr[:], A.add)
-        V("tt", "nB", "nb0 nw2", T.nB[:, 0:16], T.nB[:, 16:32], T.nw[:, 32:48], A.subtract)
+        V("tt", "nB", "nb0 nw2", T.nB[:, 0:16], T.nB[:, 16:32], T.nw[:, 32:48], A.add)
         for c in range(NS):
-            S("jk%d rk%d" % (c, c), "kap nB", T.jk[:, 256 * c:256 * c + 256], T.kap[:], ACT.Sign, bias=T.nB[:, c:c + 1], scale=1.0, accum_out=T.acc2[:, c:c + 1])
+            lift[1] = 280.0 * (NS - 1 - c)
+            S("jk%d rk%d" % (c, c), "kap nB", T.jk[:, 256 * c:256 * c + 256], T.kap[:], ACT.Sign, bias=T.nB[:, c:c + 1], scale=-1.0 / U, accum_out=T.acc2[:, c:c + 1])
         for c in range(NS, 16):
             j = T.jk[:, 256 * c:256 * c + 256]
-            V("ts", "jk%d" % c, "kap nB", j, T.kap[:], T.nB[:, c:c + 1], 0.0, A.add, A.is_lt)
+            V("ts", "jk%d" % c, "kap nB", j, T.kap[:], 1.0 / U, T.nB[:, c:c + 1], A.mult, A.is_lt)
             V("scan", "rk%d" % c, "jk%d" % c, T.jo[:, 256 * c:256 * c + 256], j, j, 0.0, A.add, A.max)
         V("ts", "ur", "wr", T.ur[:], T.wr[:], 256 * U, 256 * U, A.min, A.subtract)
         V("cp", "r16b", names("rk", NS, 16), T.r16[:, NS:16], T.jo[:, 256 * NS + 255:4096:256])
-        V("ts", "r16a", names("rk", 0, NS), T.r16[:, 0:NS], T.acc2[:, 0:NS], -0.5, 128.0, A.mult, A.add)
+        V("ts", "r16a", names("rk", 0, NS), T.r16[:, 0:NS], T.acc2[:, 0:NS], 0.5, 128.0, A.mult, A.add)
         V("tt", "qq", "r16a r16b tsel tsz ur", T.qq[:], (T.tsel[:, 0:272], T.r16[:, 0:16]), T.ur[:], A.mult)
         S("kv1", "qq", T.qj[:], T.qq[:], ACT.Relu, scale=-1.0, accum_out=T.kv[:, 1:2])
         V("red", "kv0", "qq", T.kv[:, 0:1], T.qq[:], XAX, A.max)
@@ -441,21 +450,24 @@ def rank_program(g, core, T, topo):
         V("cp", "gpa", "t2 t2c cl16c", T.gp[:, 0:96], (t2, lst(LP, 96)))
         S("gp", "t2 t2c cl16c", T.gp[:, 96:208], (t2, lst(LP + 96, 112)), ACT.Copy)
         V("tt", "ee", "t2 t2c cl16c gp gpa", T.ee[:], (t2, lst(LQ, 176)), T.gp[:, 0:176], A.is_equal)
-        V("tt", "nd", "t2 t2c cl16c gp", T.nd[:], (t2, lst(LV, 32)), T.gp[:, 169:201], A.subtract)
+        V("tt", "nd nd0 nd1", "t2 t2c cl16c gp", T.nd[:, 0:32], (t2, lst(LV, 32)), T.gp[:, 169:201], A.subtract)
         V("scan", "so", "ee md", T.so[:, 0:169], T.md[:, 0:169], T.ee[:, 0:169], 0.0, A.add, A.max)
-        V("tt", "br", "t2 t2c cl16c gp gpz", T.abi[:, 0:32:2], (t2, lst(LX, 16)), T.gp[:, 193:209], A.is_gt)
+        V("tt", "nbr", "t2 t2c cl16c gp gpz", T.bq[:, 0:16], (t2, lst(LX, 16)), T.gp[:, 193:209], A.is_le)
+        V("tt", "br", "t2 t2c cl16c gp gpz", T.bq[:, 16:32], (t2, lst(LX, 16)), T.gp[:, 193:209], A.is_gt)
+        V("tt", "nd0", "nd nbr", T.nd[:, 24:48:2], T.nd[:, 0:12], T.bq[:, 0:12], A.mult)
+        V("tt", "nd1", "nd br", T.nd[:, 25:48:2], T.nd[:, 12:24], T.bq[:, 16:28], A.mult)
         for s in range(4):
             V("ts", "ff%d" % s, "so", T.ff[:, 6 * s + 1:6 * s + 6], T.so[:, 42 * s + 7:42 * s + 42:7], T.so[:, 42 * s + 42:42 * s + 43], None, A.is_lt)
-        V("tt", "d2", "nd ffc ff0 ff1 ff2 ff3", T.d2[:], T.nd[:, 0:24], T.ff[:], A.mult)
-        V("scan", "ab", "d2 scab", T.abi[:, 1:48:2], T.scab[:], T.d2[:], 0.0, A.mult, A.subtract)
+        V("tt", "d2", "nd nd0 nd1 ffc ff0 ff1 ff2 ff3 cl16b", T.d2[:], (T.ff[:, 0:24], lst(LF, 48)), T.nd[:], A.mult)
+        V("scan", "ab", "d2 scab1 scab2", T.abi[:], T.scab[:], T.d2[:], 0.0, A.mult, A.subtract)
         lift[0] = 1000.0
-        V("cp", "ab%d" % t, "ab", T.ab[:, 24 * t:24 * t + 24], T.abi[:, 1:48:2])
+        V("cp", "ab%d" % t, "ab", T.ab[:, 24 * t:24 * t + 24], T.abi[:, 0:24])
         lift[0] = 0.0
         send(["ab%d" % t], "al%d" % t, "la%d" % t, [(T.la[:, 24 * t:24 * t + 24], T.ab[:, 24 * t:24 * t + 24])], NEAR)
-        V("tt", "b0", "ab b0", T.b0[:, 1:24:2], T.abi[:, 25:48:2], T.abi[:, 1:24:2], A.subtract)
-        V("scan", "bti", "b0 ab br", T.bti[:], T.b0[:], T.abi[:, 0:24], 0.0, A.mult, A.add)
-        V("cp", "bt16", "bti", T.bt16[:], T.bti[:, 1:24:2])
+        V("cp", "bt16", "ab", T.bt16[:], T.abi[:, 25:48:2])
+        lift[1] = BEHIND
         V("cp", "btv", "idb bt16", T.btv[:], (T.idb[:, 0:272], T.bt16[:, 0:12]))
+        lift[1] = 0.0
         for c in range(16):
             if c < NE:
                 lift[0] = 1000.0
@@ -464,11 +476,10 @@ def rank_program(g, core, T, topo):
             else:
                 V("ts", "abd%d" % c, "btv nwb", T.abd[:, c, 0:192], T.btv[:], T.nwb[:, c:c + 1], 1024.0, A.not_equal, A.mult)
             V("scan", "ev%d" % c, "abz de1 de2 abd%d" % c, T.abo[:, c, 0:193], T.de[:, 0:193], T.abd[:, c, 0:193], 252.0, A.add, A.min)
-        V("ts", "ei", names("ev", 0, 16), T.ei[:, 0:16], T.abo[:, :, 192], 16.0, None, A.mult)
-        V("ts", "ek", "ei", T.ei[:, 16:32], T.ei[:, 0:16], 255, None, A.bitwise_and)
-        V("ts", "em", "ei", T.ei[:, 32:48], T.ei[:, 0:16], 8, None, A.arith_shift_right)
-        V("tt", "ex2", "ek em", T.ei[:, 48:64], T.ei[:, 16:32], T.ei[:, 32:48], A.add)
-        V("cp", "e16", "ex2", T.e16[:], T.ei[:, 48:64])
+        V("ts", "ek", names("ev", 0, 16) + " ekz", T.ek[:, 1:32:2], T.abo[:, :, 192], 1.0 / 16, 144 - 0.375, A.mult, A.add)
+        V("ts", "em", names("ev", 0, 16) + " emz", T.ei[:, 1:32:2], T.abo[:, :, 192], 16.0, 255.0 * 144, A.mult, A.add)
+        V("scan", "ex2", "ek em", T.ei[:, 32:64], T.ek[:], T.ei[:, 0:32], 0.0, A.mult, A.add)
+        V("cp", "e16", "ex2", T.e16[:], T.ei[:, 33:64:2])
         for b in range(4):
             w = T.f2[:, 272 * b:272 * b + 272]
             S("at%d" % b, "f2z%d f2_%d la%d" % (b, b, t), T.at[:, 192 * b:192 * b + 192], (w, T.la[:, 24 * t:24 * t + 12]), ACT.Copy)
@@ -478,8 +489,8 @@ def rank_program(g, core, T, topo):
         S("li1", "kv0 kv1", T.li[:, 2:4], T.kv[:], ACT.Relu, bias=1.0, scale=-1.0)
         for h in range(2):
             S("li2%d" % h, "li0 li1 cm", T.li[:, 4 + h:5 + h], T.li[:, 2 + h:3 + h], ACT.Identity, bias=T.li[:, h:h + 1], scale=T.cm[:, h:h + 1])
-            S("li3%d" % h, "br li2%d" % h, T.li[:, 6 + h:7 + h], T.abi[:, 12 * h:12 * h + 1], ACT.Identity, bias=T.li[:, 4 + h:5 + h], scale=-256.0)
-        V("cp", "m16", "ab", T.m16[:], T.abi[:, 11:24:12])
+            S("li3%d" % h, "br li2%d" % h, T.li[:, 6 + h:7 + h], T.bq[:, 16 + 6 * h:17 + 6 * h], ACT.Identity, bias=T.li[:, 4 + h:5 + h], scale=-256.0)
+        V("cp", "m16", "ab", T.m16[:], T.abi[:, 5:12:6])
         S("mt", "idb m16", T.mt[:], (T.idb[:, 0:272], T.m16[:, 0:2]), ACT.Copy)
         V("cp", "ln16", "li30 li31", T.ln16[:], T.li[:, 6:8])
         V("cp", "lt", "mt ln16 ltz", (T.lt[:, 0:544], T.ln16[:, 0:2]), T.mt[:])
@@ -511,10 +522,10 @@ def rank_program(g, core, T, topo):
         lo, hi = 128 * h, 128 * h + 128
         mm(pa, T.vq[:, 0:128], "vq vp", T.vp[:, 0:128], xq[:, lo:hi], xk + "ab"[h], xp[:, lo:hi], 128)
         dma("y", "oc%d" % h, [xk + "ab"[h]], [], T.oc[:, 4 * lo:4 * hi], xq[:, lo:hi].bitcast(dt.uint8), 2500.0)
-        S("ms%d" % h, pa, T.ms[:, lo:hi], T[pa][:, 0:128], ACT.Copy)
-        dma("s", "oy%d" % h, ["ms%d" % h], [], T.y[:, lo:hi], T.ms[:, lo:hi], 2500.0)
+        V("cp", "ms%d" % h, pa, T.ms[:, lo:hi], T[pa][:, 0:128])
+        dma("sy"[h], "oy%d" % h, ["ms%d" % h], [], T.y[:, lo:hi], T.ms[:, lo:hi], 2500.0)
     for k in range(4):
-        dma("y", "os%d" % k, [xk + "a", xk + "b"], [], T.osc[4 * k:4 * k + 4, 0:256], xp[32 * k:32 * k + 4, 0:256])
+        dma("s", "os%d" % k, [xk + "a", xk + "b"], [], T.osc[4 * k:4 * k + 4, 0:256], xp[32 * k:32 * k + 4, 0:256])
 
     total, waited = {}, {q: {} for q in queues}
     if len(calls) not in ORDER:

@@ -5,11 +5,11 @@ N = 8
 R = 3
 C = 256
 NS = 9
-NE = 6
+NE = 8
 U = 2.0 ** -18
 CYC, LAT, DMA, NEAR, FAR, SLACK = 0.85, 220.0, 1800.0, 1500.0, 3500.0, 100.0
-SEED, SPREAD, STEPS, GIVE, SOONER = 1, 0.0, 3000, 100.0, 500.0
-BEHIND = 0.0
+SEED, SPREAD, STEPS, GIVE, SOONER = 1, 0.0, 50000, 15.0, 500.0
+MEAN, AHEAD = 0.5, 500.0
 ORDER = {}
 F32, BF, I32, U16, U8, X4 = "float32", "bfloat16", "int32", "uint16", "uint8", "float8_e4m3fn_x4"
 
@@ -29,16 +29,16 @@ SCRATCH = {
     "nmask": _sb(128, F32), "thr": _sb(128, F32), "sc0": _sb(128, F32), "nw": _sb(64, F32), "nwb": _sb(16, BF), "nT": _sb(96, F32),
     "scab": _sb(48, F32), "upl": _sb(8, U16), "w256": _sb(512, F32), "tsel": _sb(272, F32),
     "dg": _sb(512, BF), "dg1": _sb(80, BF), "cl": _sb(784, BF), "clo": _sb(784, BF),
-    "cl16": _sb(50, U16), "wt": _sb(176, F32), "md": _sb(176, BF), "de": _sb(200, BF), "cm": _sb(2, F32),
+    "cl16": _sb(50, U16), "wt": _sb(480, F32), "md": _sb(240, BF), "de": _sb(200, BF), "cm": _sb(2, F32),
     "aa": _sb(1280, F32), "asc": _sb(256, F32),
     "ms": _sb(256, F32), "sc": _sb(256, F32), "ssb": _sb(256, F32), "c0": _sb(512, BF), "c1": _sb(512, BF), "c2": _sb(512, BF),
-    "wc16": _sb(16, U16), "va": _sb(256, F32), "vb": _sb(256, F32), "pq": _sb(528, F32),
+    "wc16": _sb(16, U16), "va": _sb(256, F32), "vb": _sb(256, F32), "vc": _sb(256, F32), "pq": _sb(528, F32),
     "pb": _sb(512, BF), "t3": ("sbuf", [128, 32, 16], BF), "ab": _sb(72, U16), "la": _sb(72, U16),
-    "f0": _sb(256, BF), "f1": _sb(192, BF), "ne": _sb(192, BF), "no": _sb(192, BF), "fo": _sb(256, BF), "scb": _sb(256, BF),
-    "wr": _sb(256, BF), "ur": _sb(256, BF), "jk": _sb(4096, BF), "jo": _sb(4096, BF), "acc": _sb(16, F32), "acc2": _sb(16, F32),
+    "f0": _sb(256, BF), "f1": _sb(96, BF), "ne": _sb(192, BF), "no": _sb(192, BF), "fo": _sb(256, BF), "scb": _sb(128, BF),
+    "wr": _sb(256, BF), "ur": _sb(256, BF), "jk": _sb(4096, BF), "jo": _sb(4096, BF), "acc": _sb(272, F32), "acc2": _sb(16, F32),
     "a16": _sb(16, U16), "nB": _sb(32, F32), "kap": _sb(256, F32), "r16": _sb(16, U16),
-    "qq": _sb(256, F32), "qj": _sb(256, F32), "kv": _sb(2, F32), "off": _sb(16, U16), "g2": _sb(128, F32), "t2": _sb(160, F32),
-    "gp": _sb(224, F32), "ee": _sb(176, BF), "so": _sb(176, BF), "nd": _sb(48, F32), "ff": _sb(24, F32), "d2": _sb(48, F32),
+    "qq": _sb(264, BF), "qj": _sb(528, BF), "off": _sb(4, U16), "g2": _sb(128, F32), "t2": _sb(160, F32),
+    "gp": _sb(144, F32), "ee": _sb(80, BF), "so": _sb(240, BF), "nd": _sb(48, F32), "ff": _sb(24, F32), "d2": _sb(48, F32),
     "abi": _sb(48, F32), "bq": _sb(32, F32), "bt16": _sb(12, U16),
     "btv": _sb(192, BF), "abd": ("sbuf", [128, 16, 200], BF), "abo": ("sbuf", [128, 16, 200], BF),
     "ei": _sb(64, F32), "ek": _sb(32, BF), "e16": _sb(16, U16),
@@ -56,7 +56,7 @@ for _n in PS:
 DMAS = ["dx0", "dx1", "du", "dv", "dwc", "dws", "dn0", "das", "oy0", "oy1", "ool", "oc0", "oc1", "os0", "os1", "os2", "os3"]
 SEMAPHORES = ["sv", "ss", "sp", "sg", "lc"] + ["ax%d" % t for t in range(R)] + ["al%d" % t for t in range(R)] + DMAS
 
-LS, LF, LP, LQ, LV, LX, LE = 0, 32, 96, 320, 512, 544, 560
+LS, LF, LP, LQ, LV, LX, LE = 0, 0, 64, 224, 320, 352, 368
 
 
 def width(ap):
@@ -107,9 +107,13 @@ def improved(calls, after, order):
     qs, deps, hold = [c["q"] for c in calls], [c["deps"] for c in calls], [c["hold"] for c in calls]
     lens = [[c["len"] - (less if c["len"] == NEAR else 0.0) for c in calls] for less in (0.0, SOONER)]
 
-    def run(order, length):
-        end, cause, free, last = [0.0] * n, [-1] * n, {}, {}
-        for i in order:
+    def run(order, length, first, old):
+        end, cause, free, last = old[0][:], old[1][:], {}, {}
+        for i in order[:first]:
+            last[qs[i]] = i
+        for q, i in last.items():
+            free[q] = end[i] - length[i] + hold[i]
+        for i in order[first:]:
             t, why = 0.0, -1
             for d in deps[i]:
                 if end[d] + LAT > t:
@@ -122,24 +126,32 @@ def improved(calls, after, order):
             end[i], cause[i] = t + length[i], why
         return end, cause
 
-    def judge(order):
-        total, pairs = 0.0, []
-        for length in lens:
-            end, cause = run(order, length)
-            i = max(range(n), key=lambda k: end[k])
-            total += end[i]
+    def judge(order, first, olds):
+        total, pairs, news = 0.0, [], []
+        for length, old in zip(lens, olds):
+            end, cause = run(order, length, first, old)
+            news.append((end, cause))
+            i = end.index(max(end))
+            total += end[i] + MEAN * sum(end) / n
             while cause[i] != -1:
                 if cause[i] < -1:
                     pairs.append((-2 - cause[i], i))
                     i = -2 - cause[i]
                 else:
                     i = cause[i]
-        return total, pairs
-    best, pairs = judge(order)
+        return total, pairs, news
+    best, pairs, now = judge(order, 0, [([0.0] * n, [-1] * n) for _ in lens])
     top, kept, x = best, order, SEED
     for step in range(STEPS):
         x = (x * 1103515245 + 12345) % 2147483648
         a, b = pairs[(x >> 8) % len(pairs)]
+        if x & 128:
+            pa = (x >> 9) % (n - 1)
+            a = order[pa]
+            later = [k for k in order[pa + 1:pa + 40] if qs[k] == qs[a]][:3]
+            if qs[a] is None or not later:
+                continue
+            b = later[(x >> 5) % len(later)]
         pa, pb = order.index(a), order.index(b)
         mid = order[pa + 1:pb]
         if x & 64:
@@ -158,9 +170,9 @@ def improved(calls, after, order):
             if any(d in need for d in deps[b]):
                 continue
             new = order[:pa] + [k for k in mid if k not in need] + [b, a] + [k for k in mid if k in need] + order[pb + 1:]
-        total, p = judge(new)
+        total, p, times = judge(new, pa, now)
         if total <= best + GIVE * (1.0 - step / STEPS) * ((x >> 4) % 64) / 64:
-            order, best, pairs = new, total, p
+            order, best, pairs, now = new, total, p, times
             if total < top:
                 top, kept = total, new
     return kept
@@ -285,8 +297,7 @@ def rank_program(g, core, T, topo):
     V("ts", "nmask", "rp pf", T.nmask[:], T.rp[:, 0:128], r16, -1.0, A.is_equal, A.mult)
     V("ts", "thr", "rp pf", T.thr[:], T.rp[:, 0:128], r16, 1e29, A.not_equal, A.mult)
     S("sc0_", "rp", T.sc0[:], T.rp[:, 0:128], ACT.Sign)
-    S("sca", "rp", T.scb[:, 0:128], T.rp[:], ACT.Sign)
-    S("scb", "rp", T.scb[:, 128:256], T.rp[:], ACT.Sign)
+    S("scb", "rp", T.scb[:], T.rp[:], ACT.Sign)
     V("qz", "uq up", "ut", T.uq[:, 0:128], T.up[:, 0:128], T.ut[:, 0:512])
     V("cp", "uq2", "uq upl", T.uq2[:, 0:128].bitcast(dt.uint32), (T.uq[:, 0:128].bitcast(dt.uint32), T.upl[:, 0:8]))
     S("up2", "up upl", T.up2[:, 0:128], (T.up[:, 0:128], T.upl[:, 0:8]), ACT.Copy)
@@ -297,19 +308,19 @@ def rank_program(g, core, T, topo):
     V("tt", "c0", "lw", T.c0[:, 31:512:32], T.lw[:, 16:32], T.lw[:, 0:16], A.subtract)
     V("cp", "c1o", "lw c1z", T.c1[:, 31:512:32], T.lw[:, 0:16])
 
-    parts = [(LS, 16, [[0, 4], [1, 2], [0, 2]], 0), (LP, 84, [[32, 2], [1, 6], [0, 7]], 2), (LP + 84, 84, [[32, 2], [0, 6], [1, 7]], 1),
-             (LP + 169, 24, [[64, 2], [32, 2], [1, 6]], 2), (LP + 193, 12, [[32, 2], [0, 6]], 0), (LQ, 84, [[32, 2], [0, 6], [1, 7]], 65),
-             (LQ + 84, 84, [[32, 2], [1, 6], [0, 7]], 66), (LV, 24, [[64, 2], [32, 2], [1, 6]], 1), (LX, 12, [[32, 2], [0, 6]], 64),
-             (LF, 24, [[1, 24]], 0), (LF + 24, 24, [[6, 2], [1, 6], [12, 2]], 0)]
+    parts = [(LF, 24, [[1, 24]], 0), (LP, 36, [[1, 6], [0, 6]], 2), (LP + 37, 36, [[1, 6], [0, 6]], 34),
+             (LP + 96, 24, [[64, 2], [32, 2], [1, 6]], 2), (LP + 120, 12, [[32, 2], [0, 6]], 0), (LQ, 36, [[0, 6], [1, 6]], 66),
+             (LQ + 37, 36, [[0, 6], [1, 6]], 98), (LV, 24, [[64, 2], [32, 2], [1, 6]], 1), (LX, 12, [[32, 2], [0, 6]], 64),
+             (LF + 24, 24, [[6, 2], [1, 6], [12, 2]], 0)]
     for k, (lo, n, pattern, base) in enumerate(parts):
         iota("cl%d" % (k + 1), T.cl[:, lo:lo + n], pattern, base, on="cl0")
-    iota("clx", T.cl[:, LP:LP + 169:7], [[0, 25]], 128, on="cl2 cl3")
-    iota("cly", T.cl[:, LQ:LQ + 169:7], [[0, 25]], 129, on="cl6 cl7")
+    iota("clx", T.cl[:, LP + 36:LP + 74:37], [[0, 2]], 128, on="cl2 cl3")
+    iota("cly", T.cl[:, LQ + 36:LQ + 74:37], [[0, 2]], 129, on="cl6 cl7")
     iota("clz", T.cl[:, LV:LV + 24:6], [[0, 4]], 128, on="cl8")
 
     def wrap(lo, hi, key, reads):
         V("scan", key, reads + " dg", T.clo[:, lo:hi], T.dg[:, 0:hi - lo], T.cl[:, lo:hi], 0.0, A.add, A.min)
-    wrap(LS, LQ, "clob", "cl1 cl4 cl5 clx cl10 cl11")
+    wrap(LS, LQ, "clob", "cl1 cl4 cl5 clx cl10")
     wrap(LQ, LE, "cloc", "cly clz cl9")
     V("ts", "cl16b", "clob pf7", T.cl16[:, LS // 16:LP // 16], T.clo[:, LS + 15:LP:16], fix, None, A.add)
     V("ts", "cl16c", "clob cloc pf7 pf", T.cl16[:, LP // 16:LE // 16], T.clo[:, LP + 15:LE:16], fix, odd16, A.add, A.add)
@@ -318,31 +329,30 @@ def rank_program(g, core, T, topo):
         return T.cl16[:, lo // 16:(lo + n) // 16]
 
     iota("nT", T.nT[:, 0:16], [[32, 8], [0, 2]], 0)
-    iota("f1", T.f1[:], [[0, 192]], 0)
-    iota("f1", T.f1[:, 0:192:12], [[0, 16]], 2)
+    iota("f1", T.f1[:], [[0, 96]], 0)
+    iota("f1", T.f1[:, 0:96:12], [[0, 8]], 2)
     iota("nw0", T.nw[:, 0:16], [[16, 16]], 0)
     iota("tsz", T.tsel[:, 32:272], [[0, 240]], 0)
-    iota("wt0", T.wt[:, 0:168], [[1, 2], [0, 84]], 8)
-    iota("wt1", T.wt[:, 1:84:7], [[0, 2], [9, 6]], 0, on="wt0")
-    iota("wt2", T.wt[:, 85:168:7], [[0, 2], [8, 6]], 0, on="wt0")
-    iota("wt3", T.wt[:, 7:85:7], [[0, 2], [-9, 6]], -40, on="wt0")
-    iota("wt4", T.wt[:, 91:169:7], [[0, 2], [-8, 6]], -45, on="wt0")
-    iota("wt5", T.wt[:, 1:169:42], [[0, 4]], -256, on="wt1 wt2")
+    for k, (a, b) in enumerate(((16, 16), (17, 16), (17, 17))):
+        iota("wt%d" % k, T.wt[:, 80 * k:80 * k + 74], [[0, 74]], b)
+        iota("wu%d" % k, T.wt[:, 80 * k + 6:80 * k + 36:6], [[0, 5]], a - 5 * b, on="wt%d" % k)
+        iota("wv%d" % k, T.wt[:, 80 * k + 43:80 * k + 73:6], [[0, 5]], a - 5 * b, on="wt%d" % k)
+        iota("ww%d" % k, T.wt[:, 80 * k + 36:80 * k + 74:37], [[0, 2]], -5 * (a + b), on="wt%d" % k)
+        iota("wx%d" % k, T.wt[:, 80 * k:80 * k + 74:37], [[0, 2]], -512, on="wt%d" % k)
     iota("scab0", T.scab[:], [[0, 48]], 1)
     iota("scab1", T.scab[:, 0:24:6], [[0, 4]], 0, on="scab0")
     iota("scab2", T.scab[:, 24:48:12], [[0, 2]], 0, on="scab0")
-    iota("ffc", T.ff[:, 0:24:6], [[0, 4]], 1)
     op("g", ["one"], ["et"], "asel", T.et[:], T.jo[:, 0:520], [[-1, 520]], A.is_equal, 0.0, 3, 4)
     iota("t2c", T.t2[:, 128:160], [[0, 2], [-1, 16]], 0)
     iota("pqz", T.pq[:, 256:264], [[0, 8]], 256)
     iota("pqy", T.pq[:, 520:528], [[0, 8]], 256)
-    iota("gpz", T.gp[:, 208:224], [[0, 16]], 0)
     iota("de0", T.de[:], [[0, 200]], -16)
     iota("de1", T.de[:, 16:192:16], [[0, 11]], 239, on="de0")
     iota("de2", T.de[:, 0:193:192], [[251, 2]], 0, on="de0")
     iota("cm", T.cm[:], [[1, 2]], -1)
     iota("ekz", T.ek[:, 0:32:2], [[0, 16]], 0)
     iota("emz", T.ei[:, 0:32:2], [[0, 16]], -255)
+    iota("qqz", T.qq[:, 256:264], [[0, 8]], 0)
     iota("ltz", T.lt[:, 512:544], [[0, 32]], 0)
     iota("abz", T.abd[:, :, 192], [[0, 16]], 1024)
     for b in range(4):
@@ -355,7 +365,9 @@ def rank_program(g, core, T, topo):
     S("nwb", "nw1", T.nwb[:], T.nw[:, 16:32], ACT.Copy)
     S("nw2", "nw1", T.nw[:, 32:48], T.nw[:, 16:32], ACT.Identity, bias=-0.5, scale=1.0)
     S("nw3", "nw1", T.nw[:, 48:64], T.nw[:, 16:32], ACT.Copy, scale=-1024.0)
-    S("md", "wt3 wt4 wt5", T.md[:, 0:169], T.wt[:, 0:169], ACT.Copy, scale=1.0 / 128)
+    for k in range(3):
+        S("md%d" % k, "wu%d wv%d ww%d wx%d" % (k, k, k, k), T.md[:, 80 * k:80 * k + 74], T.wt[:, 80 * k:80 * k + 74], ACT.Copy, scale=1.0 / 256)
+    S("ffc", "idw ts2", T.sm[:, 80:86], T.idw[:, 0:6], ACT.Copy, scale=1.0 / 256)
     S("idb", "idw", T.idb[:], T.idw[:], ACT.Copy)
     S("cm", "cm pf8", T.cm[:], T.cm[:], ACT.Identity, bias=T.pf[:, 8:9], scale=1.0)
     S("lt", "idb lw16", T.lt[:, 0:512], (T.idb[:, 0:272], T.lw16[:, 0:32]), ACT.Copy)
@@ -367,9 +379,7 @@ def rank_program(g, core, T, topo):
     dst = T.cores[(rank + 1) % N]
     prv = T.cores[(rank - 1) % N]
 
-    def engs(a, b):
-        e = topo.engines(a, b)
-        return e[::len(e) // 8]
+    engs = topo.engines
     emask = sum(1 << k for k in engs(core, dst))
     rid, pid = topo.addr(dst)[:2]
     nout, nin = len(engs(core, dst)), len(engs(prv, core))
@@ -388,90 +398,99 @@ def rank_program(g, core, T, topo):
             lo, hi = 128 * h, 128 * h + 128
             for k in (pv, pa):
                 mm(k, T.uq2[:, 0:128], "uq2 up2", T.up2[:, 0:128], xq[:, lo:hi], xk + "ab"[h], xp[:, lo:hi], 128)
+            lift[1] = AHEAD
             V("tt", "c1e%d" % h, pv + " thr c1z", T.c1[:, 2 * lo:2 * hi:2], T[pv][:, 0:128], T.thr[:, 0:128], A.is_gt)
             V("scan", "c2%d" % h, "c0 c0z c1o c1e%d" % h, T.c2[:, 2 * lo:2 * hi], T.c0[:, 2 * lo:2 * hi], T.c1[:, 2 * lo:2 * hi], 0.0, A.mult, A.add)
+            lift[1] = 0.0
             V("tt", "ms%d" % h, pv + " nmask", T.ms[:, lo:hi], T[pv][:, 0:128], T.nmask[:, 0:128], A.mult)
             S("ssb%d" % h, pa, T.ssb[:, lo:hi], T[pa][:, 0:128], ACT.Copy)
             V("scan", "sc%d" % h, "ms%d sc0_" % h, T.sc[:, lo:hi], T.sc0[:, 0:128], T.ms[:, lo:hi], 0.0, A.mult, A.add)
-        V("cp", "wc16", "c20 c21", T.wc16[:], T.c2[:, 31:512:32])
+            V("cp", "wc%d" % h, "c2%d" % h, T.wc16[:, 8 * h:8 * h + 8], T.c2[:, 2 * lo + 31:2 * hi:32])
+            V("tt", "vc%d" % h, "a0 a1 wc%d" % h, T.vc[:, lo:hi], (adds[0], T.wc16[:, 8 * h:8 * h + 8]), T.aa[:, 256 + lo:256 + hi], A.add)
         dma("y", "das", ["ssb0", "ssb1"], ["asc"], T.asc[0:128:16, :], T.ssb[0:128:16, :])
         send([xk + "a", xk + "b"], "ax%d" % t, "xn%d" % t, [(xq[:, 256:512].bitcast(dt.uint8), xq[:, 0:256].bitcast(dt.uint8)), (xp[:, 256:512], xp[:, 0:256])], FAR)
         for b in range(4):
             mm("pd%d" % b, T.eq[:, 128 * b:128 * b + 128], "eq%d" % b, T.ep[:, 128 * b:128 * b + 128], xq[:, 0:512], "%sa %sb xn%d" % (xk, xk, t), xp[:, 0:512], 512)
             S("f2_%d" % b, "pd%d" % b, T.f2[:, 272 * b:272 * b + 256], T["pd%d" % b][:, 256:512], ACT.Copy, scale=0.5)
             S("fw%d" % b, "pd%d" % b, T.fw[:, 256 * b:256 * b + 256], T["pd%d" % b][:, 0:256], ACT.Copy)
-        for c in range(16):
+        V("ts", "jk0", "ssb0 ssb1 sc0", T.jk[:, 0:256], T.ssb[:], T.sc[:, 15:16], 0.0, A.add, A.is_gt)
+        V("ts", "jl0", "ssb0 ssb1 sc0", T.jo[:, 768:1024], T.ssb[:], T.sc[:, 15:16], 0.0, A.add, A.is_lt)
+        V("scan", "acc0", "jk0 jl0", T.acc[:, 0:256], T.jk[:, 0:256], T.jo[:, 768:1024], 0.0, A.add, A.subtract)
+        for c in range(1, 16):
             lift[1] = 280.0 * (15 - c) + (400.0 if c < 12 else 0.0)
-            S("jk%d acc%d" % (c, c), "ssb0 ssb1 sc%d" % (c // 8), T.jk[:, 256 * c:256 * c + 256], T.ssb[:], ACT.Sign, bias=T.sc[:, 16 * c + 15:16 * c + 16], scale=1.0, accum_out=T.acc[:, c:c + 1])
-        cur, key = adds[0], "a0"
-        for k in range(1, 6):
+            S("jk%d acc%d" % (c, c), "ssb0 ssb1 sc%d" % (c // 8), T.jk[:, 256 * c:256 * c + 256], T.ssb[:], ACT.Sign, bias=T.sc[:, 16 * c + 15:16 * c + 16], scale=1.0, accum_out=T.acc[:, 255 + c:256 + c])
+        cur, key = T.vc[:, 0:256], "vc0 vc1"
+        for k in range(2, 6):
             nxt = "va" if k % 2 else "vb"
-            V("tt", nxt, key + (" wc16 asc" if k == 5 else " wc16 a%d" % k), T[nxt][:], (cur, T.wc16[:, 0:16]), adds[k], A.add)
+            V("tt", nxt, key + (" wc0 wc1 asc" if k == 5 else " wc0 wc1 a%d" % k), T[nxt][:], (cur, T.wc16[:, 0:16]), adds[k], A.add)
             cur, key = T[nxt][:, 0:256], nxt
-        V("cp", "pb0", key + " lw16", T.pb[:, 0:256], (cur, T.lw16[:, 0:16]))
-        lift[0] = 1000.0
-        S("pb1", key + " lw16", T.pb[:, 256:512], (cur, T.lw16[:, 16:32]), ACT.Copy)
-        lift[0] = 0.0
         S("pq0", key + " lw16", T.pq[:, 0:256], (cur, T.lw16[:, 0:16]), ACT.Copy)
         S("pq1", key + " lw16", T.pq[:, 264:520], (cur, T.lw16[:, 16:32]), ACT.Copy)
-        V("tr", "t3p", "pb0", T.t3[:, 0:16, :], T.pb[:, 0:256])
-        V("tr", "t3q", "pb1", T.t3[:, 16:32, :], T.pb[:, 256:512])
-        V("tt", "ne0", "t3p t3q", T.ne[:, 0:192:2], T.t3[:, 0:16, 2:8], T.t3[:, 16:32, 8:14], A.not_equal)
-        V("tt", "ne1", "t3p t3q", T.ne[:, 1:192:2], T.t3[:, 0:16, 8:14], T.t3[:, 16:32, 2:8], A.not_equal)
-        V("tt", "f1k", "t3p t3q", T.nT[:, 16:32], T.t3[:, 0:16, 2], T.t3[:, 16:32, 2], A.is_equal)
-        V("scan", "no", "ne0 ne1 f1", T.no[:], T.f1[:], T.ne[:], 1.0, A.add, A.min)
-        V("tt", "f1m", "f1k nT", T.nT[:, 32:48], T.nT[:, 16:32], T.nT[:, 0:16], A.max)
-        V("tt", "f0", "no f1m", T.f0[:, 0:256:16], T.no[:, 11:192:12], T.nT[:, 32:48], A.max)
-        V("scan", "fo", "f0 sca scb", T.fo[:], T.scb[:], T.f0[:], 0.0, A.mult, A.add)
-        V("tr", "wr", "fo", T.wr[:], T.fo[:])
-        accs = names("acc", 0, 16)
-        V("ts", "a16", accs, T.a16[:], T.acc[:], 255.0, None, A.add)
-        V("ts", "nb0", accs, T.nB[:, 16:32], T.acc[:], 256.0, None, A.mult)
-        V("tt", "kap", "a16 w256a w256b wr", T.kap[:], (T.w256[:, 0:512], T.a16[:, 0:16]), T.wr[:], A.add)
-        V("tt", "nB", "nb0 nw2", T.nB[:, 0:16], T.nB[:, 16:32], T.nw[:, 32:48], A.add)
+        for h in range(2):
+            lo, hi, a, b, H = 128 * h, 128 * h + 128, 8 * h, 8 * h + 8, str(h)
+            V("ts", "a16" + H, names("acc", a, b), T.a16[:, a:b], T.acc[:, 255 + a:255 + b], 255.0, None, A.add)
+            V("ts", "nb0" + H, names("acc", a, b), T.nB[:, 16 + a:16 + b], T.acc[:, 255 + a:255 + b], 256.0, None, A.mult)
+            V("tt", "nB" + H, "nw2 nb0" + H, T.nB[:, a:b], T.nB[:, 16 + a:16 + b], T.nw[:, 32 + a:32 + b], A.add)
+            V("cp", "pb0" + H, key + " lw16", T.pb[:, lo:hi], (cur, T.lw16[:, a:b]))
+            lift[0] = 1000.0
+            S("pb1" + H, key + " lw16", T.pb[:, 256 + lo:256 + hi], (cur, T.lw16[:, 16 + a:16 + b]), ACT.Copy)
+            lift[0] = 0.0
+            p, q = T.t3[:, a:b, :], T.t3[:, 16 + a:16 + b, :]
+            V("tr", "t3p" + H, "pb0" + H, p, T.pb[:, lo:hi])
+            V("tr", "t3q" + H, "pb1" + H, q, T.pb[:, 256 + lo:256 + hi])
+            both = "t3p%d t3q%d" % (h, h)
+            V("tt", "ne0" + H, both, T.ne[:, 96 * h:96 * h + 96:2], T.t3[:, a:b, 2:8], T.t3[:, 16 + a:16 + b, 8:14], A.not_equal)
+            V("tt", "ne1" + H, both, T.ne[:, 96 * h + 1:96 * h + 96:2], T.t3[:, a:b, 8:14], T.t3[:, 16 + a:16 + b, 2:8], A.not_equal)
+            V("tt", "f1k" + H, both, T.nT[:, 16 + a:16 + b], T.t3[:, a:b, 2], T.t3[:, 16 + a:16 + b, 2], A.is_equal)
+            V("scan", "no" + H, "f1 ne0%d ne1%d" % (h, h), T.no[:, 96 * h:96 * h + 96], T.f1[:, 0:96], T.ne[:, 96 * h:96 * h + 96], 1.0, A.add, A.min)
+            V("tt", "f1m" + H, "nT f1k" + H, T.nT[:, 32 + a:32 + b], T.nT[:, 16 + a:16 + b], T.nT[:, a:b], A.max)
+            V("tt", "f0" + H, "f0 no%d f1m%d" % (h, h), T.f0[:, lo:hi:16], T.no[:, 96 * h + 11:96 * h + 96:12], T.nT[:, 32 + a:32 + b], A.max)
+            V("scan", "fo" + H, "scb f0" + H, T.fo[:, lo:hi], T.scb[:], T.f0[:, lo:hi], 0.0, A.mult, A.add)
+            V("tr", "wr" + H, "fo" + H, T.wr[:, lo:hi], T.fo[:, lo:hi])
+            V("tt", "kap" + H, "w256a w256b a16%d wr%d" % (h, h), T.kap[:, lo:hi], (T.w256[:, 0:512], T.a16[:, a:b]), T.wr[:, lo:hi], A.add)
         for c in range(NS):
             lift[1] = 280.0 * (NS - 1 - c)
-            S("jk%d rk%d" % (c, c), "kap nB", T.jk[:, 256 * c:256 * c + 256], T.kap[:], ACT.Sign, bias=T.nB[:, c:c + 1], scale=-1.0 / U, accum_out=T.acc2[:, c:c + 1])
+            S("jk%d rk%d" % (c, c), "kap0 kap1 nB%d" % (c // 8), T.jk[:, 256 * c:256 * c + 256], T.kap[:], ACT.Sign, bias=T.nB[:, c:c + 1], scale=-1.0 / U, accum_out=T.acc2[:, c:c + 1])
         for c in range(NS, 16):
             j = T.jk[:, 256 * c:256 * c + 256]
-            V("ts", "jk%d" % c, "kap nB", j, T.kap[:], 1.0 / U, T.nB[:, c:c + 1], A.mult, A.is_lt)
+            V("ts", "jk%d" % c, "kap0 kap1 nB1", j, T.kap[:], 1.0 / U, T.nB[:, c:c + 1], A.mult, A.is_lt)
             V("scan", "rk%d" % c, "jk%d" % c, T.jo[:, 256 * c:256 * c + 256], j, j, 0.0, A.add, A.max)
-        V("ts", "ur", "wr", T.ur[:], T.wr[:], 256 * U, 256 * U, A.min, A.subtract)
+        V("ts", "ur", "wr0 wr1", T.ur[:], T.wr[:], 256 * U, 256 * U, A.min, A.subtract)
         V("cp", "r16b", names("rk", NS, 16), T.r16[:, NS:16], T.jo[:, 256 * NS + 255:4096:256])
         V("ts", "r16a", names("rk", 0, NS), T.r16[:, 0:NS], T.acc2[:, 0:NS], 0.5, 128.0, A.mult, A.add)
-        V("tt", "qq", "r16a r16b tsel tsz ur", T.qq[:], (T.tsel[:, 0:272], T.r16[:, 0:16]), T.ur[:], A.mult)
-        S("kv1", "qq", T.qj[:], T.qq[:], ACT.Relu, scale=-1.0, accum_out=T.kv[:, 1:2])
-        V("red", "kv0", "qq", T.kv[:, 0:1], T.qq[:], XAX, A.max)
-        V("ts", "off", "kv0 kv1 cl16b", T.off[:], (T.kv[:, 0:2], lst(LS, 16)), -1.0, 256.0, A.mult, A.add)
-        V("cp", "g20", "pqz pq0 off", T.g2[:, 0:64], (T.pq[:, 0:264], T.off[:, 0:4]))
-        S("g21", "pqy pq1 off", T.g2[:, 64:128], (T.pq[:, 264:528], T.off[:, 0:4]), ACT.Copy)
+        V("tt", "qq", "r16a r16b tsel tsz ur", T.qq[:, 0:256], (T.tsel[:, 0:272], T.r16[:, 0:16]), T.ur[:], A.mult)
+        for h, how in enumerate((A.max, A.min)):
+            V("scan", "kv%d" % h, "qq qqz", T.qj[:, 264 * h:264 * h + 257], T.qq[:, 0:257], T.qq[:, 0:257], 0.0, how, how)
+            V("ts", "off%d" % h, "kv%d" % h, T.off[:, 2 * h:2 * h + 2], T.qj[:, 264 * h + 255:264 * h + 257], 2.0 * h - 1.0, 256.0, A.mult, A.add)
+        V("cp", "g20", "pqz pq0 off0 off1", T.g2[:, 0:64], (T.pq[:, 0:264], T.off[:, 0:4]))
+        S("g21", "pqy pq1 off0 off1", T.g2[:, 64:128], (T.pq[:, 264:528], T.off[:, 0:4]), ACT.Copy)
         V("tr", "t2", "g20 g21", T.t2[:, 0:128], T.g2[:])
         t2 = T.t2[:, 0:160]
-        V("cp", "gpa", "t2 t2c cl16c", T.gp[:, 0:96], (t2, lst(LP, 96)))
-        S("gp", "t2 t2c cl16c", T.gp[:, 96:208], (t2, lst(LP + 96, 112)), ACT.Copy)
-        V("tt", "ee", "t2 t2c cl16c gp gpa", T.ee[:], (t2, lst(LQ, 176)), T.gp[:, 0:176], A.is_equal)
-        V("tt", "nd nd0 nd1", "t2 t2c cl16c gp", T.nd[:, 0:32], (t2, lst(LV, 32)), T.gp[:, 169:201], A.subtract)
-        V("scan", "so", "ee md", T.so[:, 0:169], T.md[:, 0:169], T.ee[:, 0:169], 0.0, A.add, A.max)
-        V("tt", "nbr", "t2 t2c cl16c gp gpz", T.bq[:, 0:16], (t2, lst(LX, 16)), T.gp[:, 193:209], A.is_le)
-        V("tt", "br", "t2 t2c cl16c gp gpz", T.bq[:, 16:32], (t2, lst(LX, 16)), T.gp[:, 193:209], A.is_gt)
+        V("cp", "gpa", "t2 t2c cl16c", T.gp[:, 0:80], (t2, lst(LP, 80)))
+        S("gp", "t2 t2c cl16c", T.gp[:, 96:144], (t2, lst(LP + 96, 48)), ACT.Copy)
+        V("tt", "ee", "t2 t2c cl16c gpa", T.ee[:], (t2, lst(LQ, 80)), T.gp[:, 0:80], A.is_equal)
+        V("tt", "nd nd0 nd1", "t2 t2c cl16c gp", T.nd[:, 0:32], (t2, lst(LV, 32)), T.gp[:, 96:128], A.subtract)
+        for k in (1, 0, 2):
+            V("scan", "so%d" % k, "ee md%d" % k, T.so[:, 80 * k:80 * k + 74], T.md[:, 80 * k:80 * k + 74], T.ee[:, 0:74], 0.0, A.add, A.max)
+        V("tt", "nbr", "t2 t2c cl16c gp", T.bq[:, 0:16], (t2, lst(LX, 16)), T.gp[:, 120:136], A.is_le)
+        V("tt", "br", "t2 t2c cl16c gp", T.bq[:, 16:32], (t2, lst(LX, 16)), T.gp[:, 120:136], A.is_gt)
         V("tt", "nd0", "nd nbr", T.nd[:, 24:48:2], T.nd[:, 0:12], T.bq[:, 0:12], A.mult)
         V("tt", "nd1", "nd br", T.nd[:, 25:48:2], T.nd[:, 12:24], T.bq[:, 16:28], A.mult)
         for s in range(4):
-            V("ts", "ff%d" % s, "so", T.ff[:, 6 * s + 1:6 * s + 6], T.so[:, 42 * s + 7:42 * s + 42:7], T.so[:, 42 * s + 42:42 * s + 43], None, A.is_lt)
-        V("tt", "d2", "nd nd0 nd1 ffc ff0 ff1 ff2 ff3 cl16b", T.d2[:], (T.ff[:, 0:24], lst(LF, 48)), T.nd[:], A.mult)
+            k, e = s // 2, 37 * (s % 2) + 36
+            V("ts", "ff%d" % s, "ffc so%d so%d" % (k, k + 1), T.ff[:, 6 * s:6 * s + 6], T.sm[:, 80:86], T.so[:, 80 * k + 80 + e:80 * k + 81 + e], T.so[:, 80 * k + e:80 * k + e + 1], A.add, A.is_le)
+        V("tt", "d2", "nd nd0 nd1 ff0 ff1 ff2 ff3 cl16b", T.d2[:], (T.ff[:, 0:24], lst(LF, 48)), T.nd[:], A.mult)
         V("scan", "ab", "d2 scab1 scab2", T.abi[:], T.scab[:], T.d2[:], 0.0, A.mult, A.subtract)
         lift[0] = 1000.0
         V("cp", "ab%d" % t, "ab", T.ab[:, 24 * t:24 * t + 24], T.abi[:, 0:24])
         lift[0] = 0.0
         send(["ab%d" % t], "al%d" % t, "la%d" % t, [(T.la[:, 24 * t:24 * t + 24], T.ab[:, 24 * t:24 * t + 24])], NEAR)
         V("cp", "bt16", "ab", T.bt16[:], T.abi[:, 25:48:2])
-        lift[1] = BEHIND
         V("cp", "btv", "idb bt16", T.btv[:], (T.idb[:, 0:272], T.bt16[:, 0:12]))
-        lift[1] = 0.0
         for c in range(16):
             if c < NE:
                 lift[0] = 1000.0
-                S("abd%d" % c, "btv nw3", T.abd[:, c, 0:192], T.btv[:], ACT.Abs, bias=T.nw[:, 48 + c:49 + c], scale=1024.0)
+                S("abd%d" % c, "btv nw3" if c >= 2 else "idb bt16 nw3", T.abd[:, c, 0:192], T.btv[:] if c >= 2 else (T.idb[:, 0:272], T.bt16[:, 0:12]), ACT.Abs, bias=T.nw[:, 48 + c:49 + c], scale=1024.0)
                 lift[0] = 0.0
             else:
                 V("ts", "abd%d" % c, "btv nwb", T.abd[:, c, 0:192], T.btv[:], T.nwb[:, c:c + 1], 1024.0, A.not_equal, A.mult)
@@ -485,10 +504,11 @@ def rank_program(g, core, T, topo):
             S("at%d" % b, "f2z%d f2_%d la%d" % (b, b, t), T.at[:, 192 * b:192 * b + 192], (w, T.la[:, 24 * t:24 * t + 12]), ACT.Copy)
             V("tt", "zt%d" % b, "f2z%d f2_%d la%d at%d" % (b, b, t, b), T.zt[:, b:768:4], (w, T.la[:, 24 * t + 12:24 * t + 24]), T.at[:, 192 * b:192 * b + 192], A.add)
         V("qz", "zq zp", "zt0 zt1 zt2 zt3", T.zq[:, 0:192], T.zp[:, 0:192], T.zt[:, 0:768])
-        S("li0", "kv0 kv1", T.li[:, 0:2], T.kv[:], ACT.Identity, bias=512.0, scale=-1.0)
-        S("li1", "kv0 kv1", T.li[:, 2:4], T.kv[:], ACT.Relu, bias=1.0, scale=-1.0)
         for h in range(2):
-            S("li2%d" % h, "li0 li1 cm", T.li[:, 4 + h:5 + h], T.li[:, 2 + h:3 + h], ACT.Identity, bias=T.li[:, h:h + 1], scale=T.cm[:, h:h + 1])
+            kv = T.qj[:, 264 * h + 256:264 * h + 257]
+            S("li0%d" % h, "kv%d" % h, T.li[:, h:h + 1], kv, ACT.Identity, bias=512.0, scale=2.0 * h - 1.0)
+            S("li1%d" % h, "kv%d" % h, T.li[:, 2 + h:3 + h], kv, ACT.Relu, bias=1.0, scale=2.0 * h - 1.0)
+            S("li2%d" % h, "li0%d li1%d cm" % (h, h), T.li[:, 4 + h:5 + h], T.li[:, 2 + h:3 + h], ACT.Identity, bias=T.li[:, h:h + 1], scale=T.cm[:, h:h + 1])
             S("li3%d" % h, "br li2%d" % h, T.li[:, 6 + h:7 + h], T.bq[:, 16 + 6 * h:17 + 6 * h], ACT.Identity, bias=T.li[:, 4 + h:5 + h], scale=-256.0)
         V("cp", "m16", "ab", T.m16[:], T.abi[:, 5:12:6])
         S("mt", "idb m16", T.mt[:], (T.idb[:, 0:272], T.m16[:, 0:2]), ACT.Copy)

@@ -4,12 +4,15 @@ from concourse.mybir import dt, AluOpType, ActivationFunctionType, AxisListType
 N = 8
 R = 3
 C = 256
-NS = 9
-NE = 8
+NS = 8
+NE = 9
+NF = 7
 U = 2.0 ** -18
-CYC, LAT, DMA, NEAR, FAR, SLACK = 0.85, 220.0, 1800.0, 1500.0, 3500.0, 100.0
-SEED, SPREAD, STEPS, GIVE, SOONER = 1, 0.0, 50000, 15.0, 500.0
-MEAN, AHEAD = 0.5, 500.0
+CYC, LAT, DMA, NEAR, FAR, SLACK = 0.85, 220.0, 1800.0, 1750.0, 3500.0, 100.0
+SEED, SPREAD, STEPS, GIVE, SOONER = 12, 0.0, 70000, 25.0, 200.0
+SLOW = 1.1
+MEAN, AHEAD, EARLY = 1.0, 500.0, 6500.0
+REACH = 6
 ORDER = {}
 F32, BF, I32, U16, U8, X4 = "float32", "bfloat16", "int32", "uint16", "uint8", "float8_e4m3fn_x4"
 
@@ -27,19 +30,19 @@ SCRATCH = {
     "zt": _sb(768, BF), "zq": _sb(192, X4), "zp": _sb(192, U8),
     "pi": _sb(4, I32), "pf": _sb(16, F32), "sm": _sb(96, F32), "idw": _sb(272, F32), "idb": _sb(272, BF), "rp": _sb(128, F32),
     "nmask": _sb(128, F32), "thr": _sb(128, F32), "sc0": _sb(128, F32), "nw": _sb(64, F32), "nwb": _sb(16, BF), "nT": _sb(96, F32),
-    "scab": _sb(48, F32), "upl": _sb(8, U16), "w256": _sb(512, F32), "tsel": _sb(272, F32),
+    "upl": _sb(8, U16), "w256": _sb(512, F32), "tsel": _sb(272, F32),
     "dg": _sb(512, BF), "dg1": _sb(80, BF), "cl": _sb(784, BF), "clo": _sb(784, BF),
     "cl16": _sb(50, U16), "wt": _sb(480, F32), "md": _sb(240, BF), "de": _sb(200, BF), "cm": _sb(2, F32),
     "aa": _sb(1280, F32), "asc": _sb(256, F32),
     "ms": _sb(256, F32), "sc": _sb(256, F32), "ssb": _sb(256, F32), "c0": _sb(512, BF), "c1": _sb(512, BF), "c2": _sb(512, BF),
-    "wc16": _sb(16, U16), "va": _sb(256, F32), "vb": _sb(256, F32), "vc": _sb(256, F32), "pq": _sb(528, F32),
+    "wc16": _sb(16, U16), "va": _sb(512, F32), "vb": _sb(256, F32), "vc": _sb(256, F32), "pq": _sb(528, F32),
     "pb": _sb(512, BF), "t3": ("sbuf", [128, 32, 16], BF), "ab": _sb(72, U16), "la": _sb(72, U16),
-    "f0": _sb(256, BF), "f1": _sb(96, BF), "ne": _sb(192, BF), "no": _sb(192, BF), "fo": _sb(256, BF), "scb": _sb(128, BF),
+    "f0": _sb(256, BF), "f1": _sb(96, BF), "ne": _sb(192, BF), "no": _sb(192, BF), "fo": _sb(256, BF), "lq16": _sb(16, U16),
     "wr": _sb(256, BF), "ur": _sb(256, BF), "jk": _sb(4096, BF), "jo": _sb(4096, BF), "acc": _sb(272, F32), "acc2": _sb(16, F32),
-    "a16": _sb(16, U16), "nB": _sb(32, F32), "kap": _sb(256, F32), "r16": _sb(16, U16),
-    "qq": _sb(264, BF), "qj": _sb(528, BF), "off": _sb(4, U16), "g2": _sb(128, F32), "t2": _sb(160, F32),
-    "gp": _sb(144, F32), "ee": _sb(80, BF), "so": _sb(240, BF), "nd": _sb(48, F32), "ff": _sb(24, F32), "d2": _sb(48, F32),
-    "abi": _sb(48, F32), "bq": _sb(32, F32), "bt16": _sb(12, U16),
+    "a16": _sb(16, U16), "ah": _sb(16, I32), "hi": _sb(16, BF), "k16": _sb(256, U16), "nB": _sb(32, F32), "kap": _sb(256, F32), "r16": _sb(16, U16),
+    "qq": _sb(264, BF), "qj": _sb(528, BF), "off": _sb(4, U16), "g2": _sb(128, F32), "t2": _sb(192, F32),
+    "gp": _sb(144, F32), "ee": _sb(80, BF), "so": _sb(240, BF), "nd": _sb(84, F32), "ff": _sb(84, F32), "kc": _sb(48, F32),
+    "abi": _sb(84, F32), "bq": _sb(48, F32), "bt16": _sb(12, U16),
     "btv": _sb(192, BF), "abd": ("sbuf", [128, 16, 200], BF), "abo": ("sbuf", [128, 16, 200], BF),
     "ei": _sb(64, F32), "ek": _sb(32, BF), "e16": _sb(16, U16),
     "li": _sb(12, F32), "ln16": _sb(2, U16), "m16": _sb(2, U16), "mt": _sb(32, BF), "lt": _sb(544, BF), "lo": _sb(512, BF),
@@ -56,7 +59,7 @@ for _n in PS:
 DMAS = ["dx0", "dx1", "du", "dv", "dwc", "dws", "dn0", "das", "oy0", "oy1", "ool", "oc0", "oc1", "os0", "os1", "os2", "os3"]
 SEMAPHORES = ["sv", "ss", "sp", "sg", "lc"] + ["ax%d" % t for t in range(R)] + ["al%d" % t for t in range(R)] + DMAS
 
-LS, LF, LP, LQ, LV, LX, LE = 0, 0, 64, 224, 320, 352, 368
+LS, LP, LQ, LX, LE = 0, 128, 288, 384, 400
 
 
 def width(ap):
@@ -105,9 +108,12 @@ def in_order(calls):
 def improved(calls, after, order):
     n = len(calls)
     qs, deps, hold = [c["q"] for c in calls], [c["deps"] for c in calls], [c["hold"] for c in calls]
-    lens = [[c["len"] - (less if c["len"] == NEAR else 0.0) for c in calls] for less in (0.0, SOONER)]
+    lens = [([c["len"] for c in calls], hold),
+            ([c["len"] * SLOW if c["len"] == c["hold"] else c["len"] - (SOONER if c["len"] == NEAR else 0.0) for c in calls],
+             [c["hold"] * SLOW if c["len"] == c["hold"] else c["hold"] for c in calls])]
 
-    def run(order, length, first, old):
+    def run(order, case, first, old):
+        length, hold = case
         end, cause, free, last = old[0][:], old[1][:], {}, {}
         for i in order[:first]:
             last[qs[i]] = i
@@ -133,6 +139,8 @@ def improved(calls, after, order):
             news.append((end, cause))
             i = end.index(max(end))
             total += end[i] + MEAN * sum(end) / n
+            if first and end[i] > max(old[0]) + 2 * GIVE:
+                return 1e18, pairs, news
             while cause[i] != -1:
                 if cause[i] < -1:
                     pairs.append((-2 - cause[i], i))
@@ -141,37 +149,57 @@ def improved(calls, after, order):
                     i = cause[i]
         return total, pairs, news
     best, pairs, now = judge(order, 0, [([0.0] * n, [-1] * n) for _ in lens])
-    top, kept, x = best, order, SEED
-    for step in range(STEPS):
-        x = (x * 1103515245 + 12345) % 2147483648
-        a, b = pairs[(x >> 8) % len(pairs)]
-        if x & 128:
-            pa = (x >> 9) % (n - 1)
-            a = order[pa]
-            later = [k for k in order[pa + 1:pa + 40] if qs[k] == qs[a]][:3]
-            if qs[a] is None or not later:
-                continue
-            b = later[(x >> 5) % len(later)]
+    top, kept, state = best, order, [SEED]
+    same = {}
+    for i, c in enumerate(calls):
+        same.setdefault(c["place"], []).append(i)
+
+    def draw(k):
+        state[0] = (state[0] * 1103515245 + 12345) % 2147483648
+        return (state[0] >> 12) % k
+
+    def moved(order, a, b, ahead):
         pa, pb = order.index(a), order.index(b)
+        if pa > pb or not deps[a] and not deps[b] and hold[a] == hold[b] == 60.0:
+            return order, n
         mid = order[pa + 1:pb]
-        if x & 64:
+        if ahead:
             need = {b}
             for k in reversed(mid):
                 if any(s in need for s in after[k]):
                     need.add(k)
             if any(s in need for s in after[a]):
+                return order, n
+            return order[:pa] + [k for k in mid if k in need] + [b, a] + [k for k in mid if k not in need] + order[pb + 1:], pa
+        need = {a}
+        for k in mid:
+            if any(d in need for d in deps[k]):
+                need.add(k)
+        if any(d in need for d in deps[b]):
+            return order, n
+        return order[:pa] + [k for k in mid if k not in need] + [b, a] + [k for k in mid if k in need] + order[pb + 1:], pa
+    for step in range(STEPS):
+        a, b = pairs[draw(len(pairs))]
+        if draw(2):
+            pa = draw(n - 1)
+            a = order[pa]
+            later = [k for k in order[pa + 1:pa + 60] if qs[k] == qs[a]][:REACH]
+            if qs[a] is None or not later:
                 continue
-            new = order[:pa] + [k for k in mid if k in need] + [b, a] + [k for k in mid if k not in need] + order[pb + 1:]
-        else:
-            need = {a}
-            for k in mid:
-                if any(d in need for d in deps[k]):
-                    need.add(k)
-            if any(d in need for d in deps[b]):
-                continue
-            new = order[:pa] + [k for k in mid if k not in need] + [b, a] + [k for k in mid if k in need] + order[pb + 1:]
+            b = later[draw(len(later))]
+        both, ahead = [(a, b)], draw(2)
+        if calls[a]["place"] and calls[b]["place"] and draw(2):
+            ta, tb = same[calls[a]["place"]], same[calls[b]["place"]]
+            shift = tb.index(b) - ta.index(a)
+            both = [(k, tb[j + shift]) for j, k in enumerate(ta) if 0 <= j + shift < len(tb)]
+        new, pa = order, n
+        for a, b in both:
+            new, p = moved(new, a, b, ahead)
+            pa = min(pa, p)
+        if pa == n:
+            continue
         total, p, times = judge(new, pa, now)
-        if total <= best + GIVE * (1.0 - step / STEPS) * ((x >> 4) % 64) / 64:
+        if total <= best + GIVE * len(both) * (1.0 - step / STEPS) * draw(64) / 64:
             order, best, pairs, now = new, total, p, times
             if total < top:
                 top, kept = total, new
@@ -186,6 +214,7 @@ def rank_program(g, core, T, topo):
     ACT = ActivationFunctionType
     XAX = AxisListType.X
     queues = {"v": g.vector, "s": g.scalar, "p": g.tensor, "g": g, "y": g.sync}
+    place = [0]
     calls, wr, rd, lift = [], {}, {}, [0.0, 0.0]
 
     def note(q, reads, writes, sem, inc, issue, length, hold):
@@ -200,7 +229,8 @@ def rank_program(g, core, T, topo):
                 deps.add(wr[k])
             deps.update(rd.get(k, []))
         i = len(calls)
-        calls.append({"q": q, "deps": sorted(deps), "sem": sem, "inc": inc, "issue": issue, "len": length, "hold": hold, "lift": lift[0], "load": lift[1]})
+        calls.append({"q": q, "deps": sorted(deps), "sem": sem, "inc": inc, "issue": issue, "len": length, "hold": hold, "lift": lift[0], "load": lift[1], "place": place[0]})
+        place[0] += place[0] > 0
         for k in writes:
             wr[k] = i
             rd[k] = []
@@ -254,20 +284,19 @@ def rank_program(g, core, T, topo):
     def names(stem, lo, hi):
         return " ".join(stem + str(c) for c in range(lo, hi))
 
+    lift[1] = 3000.0
     dma("y", "du", [], ["ut"], T.ut[:], T.u[:], 1600.0)
-    dma("s", "dx0", [], ["xta"], T.xt[:, 0:512], T.x[:, 0:512], 1900.0)
+    lift[1] = 1500.0
+    dma("s", "dx0", [], ["xta"], T.xt[:, 0:512], T.x[:, 0:512], 1850.0)
+    lift[1] = 0.0
     dma("y", "dx1", [], ["xt"], T.xt[:, 512:1024], T.x[:, 512:1024], 2100.0)
-    dma("s", "dn0", [], ["lw"], T.lw[:], T.nb[:], 1900.0)
-    dma("y", "dwc", ["xt"], ["wq"], T.wq[:, 0:512].bitcast(dt.uint8), T.wc[:], 3300.0)
-    dma("y", "dws", ["xt"], ["wp"], T.wp[:, 0:512], T.ws[:], 2700.0)
-    dma("y", "dv", ["xt"], ["vt"], T.vt[:], T.v[:], 2900.0)
+    dma("s", "dn0", [], ["lw"], T.lw[:], T.nb[:], 2500.0)
 
     iota("pi", T.pi[:, 0:1], [[0, 1]], 0, 1)
     iota("sm1", T.sm[:, 8:14], [[-1, 6]], 7)
     iota("idw", T.idw[:], [[1, 272]], 0)
     iota("sm0", T.sm[:, 0:8], [[16, 8]], 0)
     iota("rp", T.rp[:], [[0, 8], [1, 16]], 0)
-    V("memset", "f0", "", T.f0[:], 0.0)
     V("ts", "pi1", "pi", T.pi[:, 1:2], T.pi[:, 0:1], 15, None, A.bitwise_and)
     V("ts", "pi2", "pi", T.pi[:, 2:3], T.pi[:, 0:1], 31, None, A.bitwise_and)
     V("ts", "pi3", "pi", T.pi[:, 3:4], T.pi[:, 0:1], 16, None, A.bitwise_and)
@@ -289,46 +318,50 @@ def rank_program(g, core, T, topo):
     V("ts", "pf9", "pf", T.pf[:, 9:10], p32, U, None, A.mult)
     fix = T.pf[:, 7:8]
     V("ts", "dg2", "idw pf", T.dg1[:, 16:33], T.idw[:, 0:17], r16, 1024.0, A.is_equal, A.mult)
-    V("ts", "rl16", "idw pf", T.rl16[:], T.idw[:, 0:32], 0.0, r16, A.mult, A.add)
+    V("ts", "rl16", "idw pf", T.rl16[:, 0:8], T.idw[:, 0:8], 0.0, r16, A.mult, A.add)
     V("ts", "dg3", "dg2", T.dg1[:, 49:64], T.dg1[:, 16:31], -0.25, None, A.mult)
     V("memset", "dg4", "", T.dg1[:, 48:49], 0.0)
     V("tt", "dgs", "dg2 dg3 dg4", T.dg1[:, 64:80], T.dg1[:, 16:32], T.dg1[:, 48:64], A.add)
-    S("dg", "dgs rl16", T.dg[:, 0:512], (T.dg1[:, 64:80], T.rl16[:, 0:32]), ACT.Copy)
+    S("dga", "dgs rl16", T.dg[:, 0:128], (T.dg1[:, 64:80], T.rl16[:, 0:8]), ACT.Copy)
+    S("dgb", "dga", T.dg[:, 128:256], T.dg[:, 0:128], ACT.Copy)
+    S("dg", "dgb", T.dg[:, 256:512], T.dg[:, 0:256], ACT.Copy)
     V("ts", "nmask", "rp pf", T.nmask[:], T.rp[:, 0:128], r16, -1.0, A.is_equal, A.mult)
     V("ts", "thr", "rp pf", T.thr[:], T.rp[:, 0:128], r16, 1e29, A.not_equal, A.mult)
     S("sc0_", "rp", T.sc0[:], T.rp[:, 0:128], ACT.Sign)
-    S("scb", "rp", T.scb[:], T.rp[:], ACT.Sign)
     V("qz", "uq up", "ut", T.uq[:, 0:128], T.up[:, 0:128], T.ut[:, 0:512])
     V("cp", "uq2", "uq upl", T.uq2[:, 0:128].bitcast(dt.uint32), (T.uq[:, 0:128].bitcast(dt.uint32), T.upl[:, 0:8]))
     S("up2", "up upl", T.up2[:, 0:128], (T.up[:, 0:128], T.upl[:, 0:8]), ACT.Copy)
     V("qz", "xq0a", "xta", T.xq0[:, 0:128], T.xp0[:, 0:128], T.xt[:, 0:512])
     V("qz", "xq0b", "xt", T.xq0[:, 128:256], T.xp0[:, 128:256], T.xt[:, 512:1024])
-    V("qz", "vq vp", "vt", T.vq[:, 0:128], T.vp[:, 0:128], T.vt[:, 0:512])
     V("cp", "lw16", "lw", T.lw16[:], T.lw[:])
     V("tt", "c0", "lw", T.c0[:, 31:512:32], T.lw[:, 16:32], T.lw[:, 0:16], A.subtract)
     V("cp", "c1o", "lw c1z", T.c1[:, 31:512:32], T.lw[:, 0:16])
 
-    parts = [(LF, 24, [[1, 24]], 0), (LP, 36, [[1, 6], [0, 6]], 2), (LP + 37, 36, [[1, 6], [0, 6]], 34),
-             (LP + 96, 24, [[64, 2], [32, 2], [1, 6]], 2), (LP + 120, 12, [[32, 2], [0, 6]], 0), (LQ, 36, [[0, 6], [1, 6]], 66),
-             (LQ + 37, 36, [[0, 6], [1, 6]], 98), (LV, 24, [[64, 2], [32, 2], [1, 6]], 1), (LX, 12, [[32, 2], [0, 6]], 64),
-             (LF + 24, 24, [[6, 2], [1, 6], [12, 2]], 0)]
+    def apart(reads, link, plus):
+        V("ts", "lq0", "c0", T.nT[:, 0:16], T.c0[:, 31:512:32], 0.0, 256.0, A.is_equal, A.mult)
+        V("tt", "lq1", "lq0 " + reads, T.nT[:, 16:32], link, T.nT[:, 0:16], A.add)
+        V("ts", "lq16", "lq1 " + reads, T.lq16[:], T.nT[:, 16:32], plus, None, A.add)
+    apart("lw", T.lw[:, 16:32], 0.0)
+
+    parts = [(LS, 128, [[12, 8], [0, 16]], 11), (LP, 36, [[1, 6], [0, 6]], 2), (LP + 37, 36, [[1, 6], [0, 6]], 34),
+             (LP + 96, 24, [[96, 2], [32, 2], [1, 6]], 2), (LP + 120, 12, [[32, 2], [0, 6]], 0), (LQ, 36, [[0, 6], [1, 6]], 2),
+             (LQ + 37, 36, [[0, 6], [1, 6]], 34), (LX, 12, [[32, 2], [0, 6]], 0)]
     for k, (lo, n, pattern, base) in enumerate(parts):
         iota("cl%d" % (k + 1), T.cl[:, lo:lo + n], pattern, base, on="cl0")
-    iota("clx", T.cl[:, LP + 36:LP + 74:37], [[0, 2]], 128, on="cl2 cl3")
-    iota("cly", T.cl[:, LQ + 36:LQ + 74:37], [[0, 2]], 129, on="cl6 cl7")
-    iota("clz", T.cl[:, LV:LV + 24:6], [[0, 4]], 128, on="cl8")
+    iota("clx", T.cl[:, LP + 36:LP + 74:37], [[0, 2]], 64, on="cl2 cl3")
+    iota("cly", T.cl[:, LQ + 36:LQ + 74:37], [[0, 2]], 64, on="cl6 cl7")
 
     def wrap(lo, hi, key, reads):
-        V("scan", key, reads + " dg", T.clo[:, lo:hi], T.dg[:, 0:hi - lo], T.cl[:, lo:hi], 0.0, A.add, A.min)
-    wrap(LS, LQ, "clob", "cl1 cl4 cl5 clx cl10")
-    wrap(LQ, LE, "cloc", "cly clz cl9")
+        V("scan", key, reads, T.clo[:, lo:hi], T.dg[:, 0:hi - lo], T.cl[:, lo:hi], 0.0, A.add, A.min)
+    wrap(LS, LP, "clob", "cl1 dga")
+    wrap(LP, LE, "cloc", "cl4 cl5 clx cly cl8 dg")
     V("ts", "cl16b", "clob pf7", T.cl16[:, LS // 16:LP // 16], T.clo[:, LS + 15:LP:16], fix, None, A.add)
-    V("ts", "cl16c", "clob cloc pf7 pf", T.cl16[:, LP // 16:LE // 16], T.clo[:, LP + 15:LE:16], fix, odd16, A.add, A.add)
+    V("ts", "cl16c", "cloc pf7 pf", T.cl16[:, LP // 16:LE // 16], T.clo[:, LP + 15:LE:16], fix, odd16, A.add, A.add)
 
     def lst(lo, n):
         return T.cl16[:, lo // 16:(lo + n) // 16]
 
-    iota("nT", T.nT[:, 0:16], [[32, 8], [0, 2]], 0)
+    iota("f0", T.f0[:], [[32, 8], [0, 32]], 0)
     iota("f1", T.f1[:], [[0, 96]], 0)
     iota("f1", T.f1[:, 0:96:12], [[0, 8]], 2)
     iota("nw0", T.nw[:, 0:16], [[16, 16]], 0)
@@ -339,11 +372,16 @@ def rank_program(g, core, T, topo):
         iota("wv%d" % k, T.wt[:, 80 * k + 43:80 * k + 73:6], [[0, 5]], a - 5 * b, on="wt%d" % k)
         iota("ww%d" % k, T.wt[:, 80 * k + 36:80 * k + 74:37], [[0, 2]], -5 * (a + b), on="wt%d" % k)
         iota("wx%d" % k, T.wt[:, 80 * k:80 * k + 74:37], [[0, 2]], -512, on="wt%d" % k)
-    iota("scab0", T.scab[:], [[0, 48]], 1)
-    iota("scab1", T.scab[:, 0:24:6], [[0, 4]], 0, on="scab0")
-    iota("scab2", T.scab[:, 24:48:12], [[0, 2]], 0, on="scab0")
+    iota("ffa", T.ff[:, 1:48:2], [[0, 24]], 1)
+    iota("ffb", T.ff[:, 50:84:3], [[0, 12]], 1)
+    iota("ndz", T.nd[:, 49:84:3], [[0, 12]], 0)
+    iota("kc", T.kc[:, 0:24], [[256, 2], [0, 2], [1, 6]], 0)
+    iota("vaz", T.va[:, 256:512], [[0, 256]], -1)
+    lift[1] = 9000.0 - EARLY
     op("g", ["one"], ["et"], "asel", T.et[:], T.jo[:, 0:520], [[-1, 520]], A.is_equal, 0.0, 3, 4)
-    iota("t2c", T.t2[:, 128:160], [[0, 2], [-1, 16]], 0)
+    lift[1] = 0.0
+    iota("t2c", T.t2[:, 64:96], [[0, 32]], 0)
+    iota("t2d", T.t2[:, 160:192], [[0, 32]], -1)
     iota("pqz", T.pq[:, 256:264], [[0, 8]], 256)
     iota("pqy", T.pq[:, 520:528], [[0, 8]], 256)
     iota("de0", T.de[:], [[0, 200]], -16)
@@ -358,24 +396,23 @@ def rank_program(g, core, T, topo):
     for b in range(4):
         iota("f2z%d" % b, T.f2[:, 272 * b + 256:272 * b + 272], [[0, 16]], 0)
         iota("hbz%d" % b, T.hb[:, 208 * b + 192:208 * b + 208], [[0, 16]], 0)
-    S("nT", "nT pf9", T.nT[:, 0:16], T.nT[:, 0:16], ACT.Identity, bias=T.pf[:, 9:10], scale=U)
-    S("w256a", "idw", T.w256[:, 0:256], T.idw[:, 0:256], ACT.Identity, scale=256 * U, bias=-255 * 256 * U)
-    S("w256b", "idw", T.w256[:, 256:512], T.idw[:, 0:256], ACT.Identity, scale=256 * U, bias=256 * U)
+    S("f0", "f0 pf9", T.f0[:], T.f0[:], ACT.Identity, bias=T.pf[:, 9:10], scale=U)
+    S("w256a", "idw", T.w256[:, 0:512:2], T.idw[:, 0:256], ACT.Copy, scale=256 * U)
+    S("w256b", "idw", T.w256[:, 1:512:2], T.idw[:, 0:256], ACT.Copy, scale=256 * U)
     S("nw1", "nw0 pf", T.nw[:, 16:32], T.nw[:, 0:16], ACT.Identity, bias=r16, scale=1.0)
     S("nwb", "nw1", T.nwb[:], T.nw[:, 16:32], ACT.Copy)
     S("nw2", "nw1", T.nw[:, 32:48], T.nw[:, 16:32], ACT.Identity, bias=-0.5, scale=1.0)
     S("nw3", "nw1", T.nw[:, 48:64], T.nw[:, 16:32], ACT.Copy, scale=-1024.0)
     for k in range(3):
         S("md%d" % k, "wu%d wv%d ww%d wx%d" % (k, k, k, k), T.md[:, 80 * k:80 * k + 74], T.wt[:, 80 * k:80 * k + 74], ACT.Copy, scale=1.0 / 256)
-    S("ffc", "idw ts2", T.sm[:, 80:86], T.idw[:, 0:6], ACT.Copy, scale=1.0 / 256)
+    S("kc", "kc", T.kc[:, 0:24], T.kc[:, 0:24], ACT.Copy, scale=1.0 / 256)
     S("idb", "idw", T.idb[:], T.idw[:], ACT.Copy)
     S("cm", "cm pf8", T.cm[:], T.cm[:], ACT.Identity, bias=T.pf[:, 8:9], scale=1.0)
     S("lt", "idb lw16", T.lt[:, 0:512], (T.idb[:, 0:272], T.lw16[:, 0:32]), ACT.Copy)
     V("ts", "ts2", "idw pf8", T.sm[:, 40:73], T.idw[:, 0:33], T.pf[:, 8:9], -1.0 / U, A.is_equal, A.mult)
     V("tt", "tsel", "ts2", T.tsel[:, 0:32], T.sm[:, 41:73], T.sm[:, 40:72], A.subtract)
-    for b in range(4):
-        V("qz", "eq%d" % b, "et", T.eq[:, 128 * b:128 * b + 128], T.ep[:, 128 * b:128 * b + 128], T.et[:, 3 - b:515 - b])
 
+    lift[1] = 0.0
     dst = T.cores[(rank + 1) % N]
     prv = T.cores[(rank - 1) % N]
 
@@ -388,10 +425,11 @@ def rank_program(g, core, T, topo):
         def issue():
             for out, in_ in pairs:
                 g.remote_dma(out, in_, T.sem[sem], T.sem.lc, pid, rid, emask)
-        note("g", key, ["sent" + sem], "lc", nout * len(pairs), issue, 0.0, 300.0 * len(pairs))
+        note("g", key, ["sent" + sem], "lc", nout * len(pairs), issue, 0.0, 3000.0 if sem[2] == "0" else 300.0 * len(pairs))
         note(None, ["sent" + sem], [arrives], sem, nin * len(pairs), None, length, 0.0)
 
     for t in range(R):
+        place[0] = 1
         xk = "xq%d" % t
         xq, xp = T[xk], T["xp%d" % t]
         for h, (pv, pa) in enumerate((("ps1", "ps2"), ("ph0", "ph1"))):
@@ -406,10 +444,23 @@ def rank_program(g, core, T, topo):
             S("ssb%d" % h, pa, T.ssb[:, lo:hi], T[pa][:, 0:128], ACT.Copy)
             V("scan", "sc%d" % h, "ms%d sc0_" % h, T.sc[:, lo:hi], T.sc0[:, 0:128], T.ms[:, lo:hi], 0.0, A.mult, A.add)
             V("cp", "wc%d" % h, "c2%d" % h, T.wc16[:, 8 * h:8 * h + 8], T.c2[:, 2 * lo + 31:2 * hi:32])
+            lift[1] = AHEAD
             V("tt", "vc%d" % h, "a0 a1 wc%d" % h, T.vc[:, lo:hi], (adds[0], T.wc16[:, 8 * h:8 * h + 8]), T.aa[:, 256 + lo:256 + hi], A.add)
-        dma("y", "das", ["ssb0", "ssb1"], ["asc"], T.asc[0:128:16, :], T.ssb[0:128:16, :])
-        send([xk + "a", xk + "b"], "ax%d" % t, "xn%d" % t, [(xq[:, 256:512].bitcast(dt.uint8), xq[:, 0:256].bitcast(dt.uint8)), (xp[:, 256:512], xp[:, 0:256])], FAR)
+            lift[1] = 0.0
+        dma("y", "das", ["ssb0", "ssb1"], ["asc", "asd%d" % t], T.asc[0:128:16, :], T.ssb[0:128:16, :])
+        if t == 0:
+            was, place[0] = place[0], 0
+            dma("y", "dwc", ["asd0"], ["wq"], T.wq[:, 0:512].bitcast(dt.uint8), T.wc[:], 3300.0)
+            dma("y", "dws", ["asd0"], ["wp"], T.wp[:, 0:512], T.ws[:], 2700.0)
+            dma("y", "dv", ["asd0"], ["vt"], T.vt[:], T.v[:], 2900.0)
+            V("qz", "vq vp", "vt", T.vq[:, 0:128], T.vp[:, 0:128], T.vt[:, 0:512])
+            place[0] = was
+        send([xk + "a", xk + "b", "asd%d" % t], "ax%d" % t, "xn%d" % t, [(xq[:, 256:512].bitcast(dt.uint8), xq[:, 0:256].bitcast(dt.uint8)), (xp[:, 256:512], xp[:, 0:256])], FAR)
         for b in range(4):
+            if t == 0:
+                was, place[0], lift[1] = place[0], 0, EARLY
+                V("qz", "eq%d" % b, "et vc1", T.eq[:, 128 * b:128 * b + 128], T.ep[:, 128 * b:128 * b + 128], T.et[:, 3 - b:515 - b])
+                place[0], lift[1] = was, 0.0
             mm("pd%d" % b, T.eq[:, 128 * b:128 * b + 128], "eq%d" % b, T.ep[:, 128 * b:128 * b + 128], xq[:, 0:512], "%sa %sb xn%d" % (xk, xk, t), xp[:, 0:512], 512)
             S("f2_%d" % b, "pd%d" % b, T.f2[:, 272 * b:272 * b + 256], T["pd%d" % b][:, 256:512], ACT.Copy, scale=0.5)
             S("fw%d" % b, "pd%d" % b, T.fw[:, 256 * b:256 * b + 256], T["pd%d" % b][:, 0:256], ACT.Copy)
@@ -422,18 +473,19 @@ def rank_program(g, core, T, topo):
         cur, key = T.vc[:, 0:256], "vc0 vc1"
         for k in range(2, 6):
             nxt = "va" if k % 2 else "vb"
-            V("tt", nxt, key + (" wc0 wc1 asc" if k == 5 else " wc0 wc1 a%d" % k), T[nxt][:], (cur, T.wc16[:, 0:16]), adds[k], A.add)
+            V("tt", nxt, key + (" wc0 wc1 asc" if k == 5 else " wc0 wc1 a%d" % k), T[nxt][:, 0:256], (cur, T.wc16[:, 0:16]), adds[k], A.add)
             cur, key = T[nxt][:, 0:256], nxt
         S("pq0", key + " lw16", T.pq[:, 0:256], (cur, T.lw16[:, 0:16]), ACT.Copy)
         S("pq1", key + " lw16", T.pq[:, 264:520], (cur, T.lw16[:, 16:32]), ACT.Copy)
         for h in range(2):
             lo, hi, a, b, H = 128 * h, 128 * h + 128, 8 * h, 8 * h + 8, str(h)
             V("ts", "a16" + H, names("acc", a, b), T.a16[:, a:b], T.acc[:, 255 + a:255 + b], 255.0, None, A.add)
-            V("ts", "nb0" + H, names("acc", a, b), T.nB[:, 16 + a:16 + b], T.acc[:, 255 + a:255 + b], 256.0, None, A.mult)
-            V("tt", "nB" + H, "nw2 nb0" + H, T.nB[:, a:b], T.nB[:, 16 + a:16 + b], T.nw[:, 32 + a:32 + b], A.add)
+            V("ts", "ah" + H, names("acc", a, b), T.ah[:, a:b], T.acc[:, 255 + a:255 + b], 0.5, 127.25, A.mult, A.add)
+            V("ts", "nb0" + H, "ah" + H, T.hi[:, a:b], T.ah[:, a:b], 256.0, None, A.mult)
+            V("tt", "nB" + H, "nw2 nb0" + H, T.nB[:, a:b], T.hi[:, a:b], T.nw[:, 32 + a:32 + b], A.add)
             V("cp", "pb0" + H, key + " lw16", T.pb[:, lo:hi], (cur, T.lw16[:, a:b]))
             lift[0] = 1000.0
-            S("pb1" + H, key + " lw16", T.pb[:, 256 + lo:256 + hi], (cur, T.lw16[:, 16 + a:16 + b]), ACT.Copy)
+            S("pb1" + H, key + " vaz lq16", T.pb[:, 256 + lo:256 + hi], (T.va[:, 0:512], T.lq16[:, a:b]), ACT.Copy)
             lift[0] = 0.0
             p, q = T.t3[:, a:b, :], T.t3[:, 16 + a:16 + b, :]
             V("tr", "t3p" + H, "pb0" + H, p, T.pb[:, lo:hi])
@@ -441,55 +493,65 @@ def rank_program(g, core, T, topo):
             both = "t3p%d t3q%d" % (h, h)
             V("tt", "ne0" + H, both, T.ne[:, 96 * h:96 * h + 96:2], T.t3[:, a:b, 2:8], T.t3[:, 16 + a:16 + b, 8:14], A.not_equal)
             V("tt", "ne1" + H, both, T.ne[:, 96 * h + 1:96 * h + 96:2], T.t3[:, a:b, 8:14], T.t3[:, 16 + a:16 + b, 2:8], A.not_equal)
-            V("tt", "f1k" + H, both, T.nT[:, 16 + a:16 + b], T.t3[:, a:b, 2], T.t3[:, 16 + a:16 + b, 2], A.is_equal)
             V("scan", "no" + H, "f1 ne0%d ne1%d" % (h, h), T.no[:, 96 * h:96 * h + 96], T.f1[:, 0:96], T.ne[:, 96 * h:96 * h + 96], 1.0, A.add, A.min)
-            V("tt", "f1m" + H, "nT f1k" + H, T.nT[:, 32 + a:32 + b], T.nT[:, 16 + a:16 + b], T.nT[:, a:b], A.max)
-            V("tt", "f0" + H, "f0 no%d f1m%d" % (h, h), T.f0[:, lo:hi:16], T.no[:, 96 * h + 11:96 * h + 96:12], T.nT[:, 32 + a:32 + b], A.max)
-            V("scan", "fo" + H, "scb f0" + H, T.fo[:, lo:hi], T.scb[:], T.f0[:, lo:hi], 0.0, A.mult, A.add)
+            V("tt", "fo" + H, "f0 cl16b no" + H, T.fo[:, lo:hi], (T.no[:, 96 * h:96 * h + 96], lst(LS, 128)), T.f0[:, lo:hi], A.max)
             V("tr", "wr" + H, "fo" + H, T.wr[:, lo:hi], T.fo[:, lo:hi])
             V("tt", "kap" + H, "w256a w256b a16%d wr%d" % (h, h), T.kap[:, lo:hi], (T.w256[:, 0:512], T.a16[:, a:b]), T.wr[:, lo:hi], A.add)
-        for c in range(NS):
-            lift[1] = 280.0 * (NS - 1 - c)
-            S("jk%d rk%d" % (c, c), "kap0 kap1 nB%d" % (c // 8), T.jk[:, 256 * c:256 * c + 256], T.kap[:], ACT.Sign, bias=T.nB[:, c:c + 1], scale=-1.0 / U, accum_out=T.acc2[:, c:c + 1])
-        for c in range(NS, 16):
-            j = T.jk[:, 256 * c:256 * c + 256]
-            V("ts", "jk%d" % c, "kap0 kap1 nB1", j, T.kap[:], 1.0 / U, T.nB[:, c:c + 1], A.mult, A.is_lt)
-            V("scan", "rk%d" % c, "jk%d" % c, T.jo[:, 256 * c:256 * c + 256], j, j, 0.0, A.add, A.max)
-        V("ts", "ur", "wr0 wr1", T.ur[:], T.wr[:], 256 * U, 256 * U, A.min, A.subtract)
-        V("cp", "r16b", names("rk", NS, 16), T.r16[:, NS:16], T.jo[:, 256 * NS + 255:4096:256])
-        V("ts", "r16a", names("rk", 0, NS), T.r16[:, 0:NS], T.acc2[:, 0:NS], 0.5, 128.0, A.mult, A.add)
-        V("tt", "qq", "r16a r16b tsel tsz ur", T.qq[:, 0:256], (T.tsel[:, 0:272], T.r16[:, 0:16]), T.ur[:], A.mult)
+            V("ts", "k16" + H, "kap" + H, T.k16[:, lo:hi], T.kap[:, lo:hi], 1.0 / U, None, A.mult)
+        for h in range(2):
+            V("ts", "ur%d" % h, "wr%d" % h, T.ur[:, 128 * h:128 * h + 128], T.wr[:, 128 * h:128 * h + 128], 256 * U, 256 * U, A.min, A.subtract)
+        for h, (a, m, b) in enumerate(((0, 4, 8), (8, 4 + NS, 16))):
+            for c in range(a, m):
+                lift[1] = 280.0 * (NS - 1 - c + 4 * h)
+                S("jk%d rk%d" % (c, c), "kap0 kap1 nB%d" % h, T.jk[:, 256 * c:256 * c + 256], T.kap[:], ACT.Sign, bias=T.nB[:, c:c + 1], scale=-1.0 / U, accum_out=T.acc2[:, c:c + 1])
+            lift[1] = 700.0 * (1 - h)
+            for c in range(m, b):
+                j = T.jk[:, 256 * c:256 * c + 256]
+                V("ts", "jk%d" % c, "k160 k161 nwb nb0%d" % h, j, T.k16[:], T.hi[:, c:c + 1], T.nwb[:, c:c + 1], A.subtract, A.is_lt)
+                V("scan", "rk%d jl%d" % (c, c), "jk%d" % c, T.jo[:, 256 * c:256 * c + 256], j, j, 0.0, A.add, A.max)
+            lift[1] = 0.0
+            V("cp", "r16b%d" % h, names("rk", m, b), T.r16[:, m:b], T.jo[:, 256 * m + 255:256 * b:256])
+            V("ts", "r16a%d" % h, names("rk", a, m), T.r16[:, a:m], T.acc2[:, a:m], 0.5, 128.0, A.mult, A.add)
+            V("tt", "qq%d" % h, "r16a%d r16b%d tsel tsz ur%d" % (h, h, h), T.qq[:, 128 * h:128 * h + 128], (T.tsel[:, 0:272], T.r16[:, a:b]), T.ur[:, 128 * h:128 * h + 128], A.mult)
         for h, how in enumerate((A.max, A.min)):
-            V("scan", "kv%d" % h, "qq qqz", T.qj[:, 264 * h:264 * h + 257], T.qq[:, 0:257], T.qq[:, 0:257], 0.0, how, how)
+            V("scan", "ku%d" % h, "qq0", T.qj[:, 264 * h:264 * h + 128], T.qq[:, 0:128], T.qq[:, 0:128], 0.0, how, how)
+            V("scan", "kv%d" % h, "qq1 qqz ku%d" % h, T.qj[:, 264 * h + 128:264 * h + 257], T.qq[:, 128:257], T.qq[:, 128:257], T.qj[:, 264 * h + 127:264 * h + 128], how, how)
             V("ts", "off%d" % h, "kv%d" % h, T.off[:, 2 * h:2 * h + 2], T.qj[:, 264 * h + 255:264 * h + 257], 2.0 * h - 1.0, 256.0, A.mult, A.add)
         V("cp", "g20", "pqz pq0 off0 off1", T.g2[:, 0:64], (T.pq[:, 0:264], T.off[:, 0:4]))
         S("g21", "pqy pq1 off0 off1", T.g2[:, 64:128], (T.pq[:, 264:528], T.off[:, 0:4]), ACT.Copy)
-        V("tr", "t2", "g20 g21", T.t2[:, 0:128], T.g2[:])
-        t2 = T.t2[:, 0:160]
-        V("cp", "gpa", "t2 t2c cl16c", T.gp[:, 0:80], (t2, lst(LP, 80)))
-        S("gp", "t2 t2c cl16c", T.gp[:, 96:144], (t2, lst(LP + 96, 48)), ACT.Copy)
-        V("tt", "ee", "t2 t2c cl16c gpa", T.ee[:], (t2, lst(LQ, 80)), T.gp[:, 0:80], A.is_equal)
-        V("tt", "nd nd0 nd1", "t2 t2c cl16c gp", T.nd[:, 0:32], (t2, lst(LV, 32)), T.gp[:, 96:128], A.subtract)
+        V("tr", "t2p", "g20", T.t2[:, 0:64], T.g2[:, 0:64])
+        V("tr", "t2", "g21", T.t2[:, 96:160], T.g2[:, 64:128])
+        t2 = T.t2[:, 96:192]
+        V("cp", "gpa", "t2p t2c cl16c", T.gp[:, 0:80], (T.t2[:, 0:96], lst(LP, 80)))
+        S("gp", "t2 t2p t2c cl16c", T.gp[:, 96:144], (T.t2[:, 0:160], lst(LP + 96, 48)), ACT.Copy)
+        V("tt", "ee", "t2 t2d cl16c gpa", T.ee[:], (t2, lst(LQ, 80)), T.gp[:, 0:80], A.is_equal)
         for k in (1, 0, 2):
             V("scan", "so%d" % k, "ee md%d" % k, T.so[:, 80 * k:80 * k + 74], T.md[:, 80 * k:80 * k + 74], T.ee[:, 0:74], 0.0, A.add, A.max)
-        V("tt", "nbr", "t2 t2c cl16c gp", T.bq[:, 0:16], (t2, lst(LX, 16)), T.gp[:, 120:136], A.is_le)
-        V("tt", "br", "t2 t2c cl16c gp", T.bq[:, 16:32], (t2, lst(LX, 16)), T.gp[:, 120:136], A.is_gt)
-        V("tt", "nd0", "nd nbr", T.nd[:, 24:48:2], T.nd[:, 0:12], T.bq[:, 0:12], A.mult)
-        V("tt", "nd1", "nd br", T.nd[:, 25:48:2], T.nd[:, 12:24], T.bq[:, 16:28], A.mult)
+        S("nd0", "gp", T.nd[:, 0:48:2], T.gp[:, 96:120], ACT.Copy, scale=-1.0)
+        S("nd1", "gp", T.nd[:, 1:48:2], T.gp[:, 96:120], ACT.Copy)
+        V("tt", "br", "t2 t2d cl16c gp", T.bq[:, 16:32], (t2, lst(LX, 16)), T.gp[:, 120:136], A.is_gt)
+        V("tt", "dw", "gp", T.bq[:, 0:12], T.gp[:, 108:120], T.gp[:, 96:108], A.subtract)
+        V("tt", "dv", "dw br", T.bq[:, 32:44], T.bq[:, 0:12], T.bq[:, 16:28], A.mult)
+        V("tt", "nd2", "dv nd0", T.nd[:, 48:84:3], T.nd[:, 0:24:2], T.bq[:, 32:44], A.subtract)
+        V("tt", "nd3", "dv gp", T.nd[:, 50:84:3], T.gp[:, 96:108], T.bq[:, 32:44], A.add)
+        V("tt", "kc0", "kc br", T.kc[:, 24:36], T.kc[:, 0:12], T.bq[:, 16:28], A.add)
+        V("tt", "kc1", "kc br", T.kc[:, 36:48], T.kc[:, 12:24], T.bq[:, 16:28], A.subtract)
         for s in range(4):
-            k, e = s // 2, 37 * (s % 2) + 36
-            V("ts", "ff%d" % s, "ffc so%d so%d" % (k, k + 1), T.ff[:, 6 * s:6 * s + 6], T.sm[:, 80:86], T.so[:, 80 * k + 80 + e:80 * k + 81 + e], T.so[:, 80 * k + e:80 * k + e + 1], A.add, A.is_le)
-        V("tt", "d2", "nd nd0 nd1 ff0 ff1 ff2 ff3 cl16b", T.d2[:], (T.ff[:, 0:24], lst(LF, 48)), T.nd[:], A.mult)
-        V("scan", "ab", "d2 scab1 scab2", T.abi[:], T.scab[:], T.d2[:], 0.0, A.mult, A.subtract)
+            k, h = s // 2, s % 2
+            x, y = T.so[:, 80 * k + 116 + 37 * h:80 * k + 117 + 37 * h], T.so[:, 80 * k + 36 + 37 * h:80 * k + 37 + 37 * h]
+            V("ts", "ff%d" % s, "kc so%d so%d" % (k, k + 1), T.ff[:, 12 * s:12 * s + 12:2], T.kc[:, 0:6], x, y, A.add, A.is_gt)
+            V("ts", "fg%d" % s, "kc%d so%d so%d" % (k, k, k + 1), T.ff[:, 48 + 18 * h + k:66 + 18 * h:3], T.kc[:, 24 + 12 * k + 6 * h:30 + 12 * k + 6 * h], x, y, A.add, A.is_gt)
+        V("scan", "ab", "nd0 nd1 ffa ff0 ff1 ff2 ff3", T.abi[:, 0:48], T.nd[:, 0:48], T.ff[:, 0:48], 0.0, A.add, A.mult)
+        V("scan", "bt", "ndz nd2 nd3 ffb fg0 fg1 fg2 fg3", T.abi[:, 48:84], T.nd[:, 48:84], T.ff[:, 48:84], 0.0, A.add, A.mult)
         lift[0] = 1000.0
-        V("cp", "ab%d" % t, "ab", T.ab[:, 24 * t:24 * t + 24], T.abi[:, 0:24])
+        V("cp", "ab%d" % t, "ab", T.ab[:, 24 * t:24 * t + 24], T.abi[:, 1:48:2])
         lift[0] = 0.0
         send(["ab%d" % t], "al%d" % t, "la%d" % t, [(T.la[:, 24 * t:24 * t + 24], T.ab[:, 24 * t:24 * t + 24])], NEAR)
-        V("cp", "bt16", "ab", T.bt16[:], T.abi[:, 25:48:2])
+        V("cp", "bt16", "bt", T.bt16[:], T.abi[:, 50:84:3])
         V("cp", "btv", "idb bt16", T.btv[:], (T.idb[:, 0:272], T.bt16[:, 0:12]))
         for c in range(16):
             if c < NE:
-                lift[0] = 1000.0
+                lift[0] = 1000.0 if c < NF else -600.0
                 S("abd%d" % c, "btv nw3" if c >= 2 else "idb bt16 nw3", T.abd[:, c, 0:192], T.btv[:] if c >= 2 else (T.idb[:, 0:272], T.bt16[:, 0:12]), ACT.Abs, bias=T.nw[:, 48 + c:49 + c], scale=1024.0)
                 lift[0] = 0.0
             else:
@@ -510,15 +572,17 @@ def rank_program(g, core, T, topo):
             S("li1%d" % h, "kv%d" % h, T.li[:, 2 + h:3 + h], kv, ACT.Relu, bias=1.0, scale=2.0 * h - 1.0)
             S("li2%d" % h, "li0%d li1%d cm" % (h, h), T.li[:, 4 + h:5 + h], T.li[:, 2 + h:3 + h], ACT.Identity, bias=T.li[:, h:h + 1], scale=T.cm[:, h:h + 1])
             S("li3%d" % h, "br li2%d" % h, T.li[:, 6 + h:7 + h], T.bq[:, 16 + 6 * h:17 + 6 * h], ACT.Identity, bias=T.li[:, 4 + h:5 + h], scale=-256.0)
-        V("cp", "m16", "ab", T.m16[:], T.abi[:, 5:12:6])
+        V("cp", "m16", "ab", T.m16[:], T.abi[:, 11:24:12])
         S("mt", "idb m16", T.mt[:], (T.idb[:, 0:272], T.m16[:, 0:2]), ACT.Copy)
         V("cp", "ln16", "li30 li31", T.ln16[:], T.li[:, 6:8])
         V("cp", "lt", "mt ln16 ltz", (T.lt[:, 0:544], T.ln16[:, 0:2]), T.mt[:])
         if t < R - 1:
             V("scan", "lo", "lt dg", T.lo[:], T.dg[:, 0:512], T.lt[:, 0:512], 0.0, A.add, A.min)
             V("ts", "lw16", "lo pf7", T.lw16[:], T.lo[:, 15:512:16], fix, None, A.add)
-            V("ts", "c1o", "lo pf7", T.c1[:, 31:512:32], T.lo[:, 15:256:16], fix, None, A.add)
+            S("c1o", "lo pf7", T.c1[:, 31:512:32], T.lo[:, 15:256:16], ACT.Identity, bias=fix, scale=1.0)
             V("tt", "c0", "lo", T.c0[:, 31:512:32], T.lo[:, 271:512:16], T.lo[:, 15:256:16], A.subtract)
+            apart("lo pf7", T.lo[:, 271:512:16], fix)
+        place[0] = 5000
         ph = ["ph0", "ph1", "ps1", "ps2"]
         for b in range(4):
             mm(ph[b], T.wq[:, 128 * b:128 * b + 128], "wq wp", T.wp[:, 128 * b:128 * b + 128], T.zq[:, 0:192], "zq zp", T.zp[:, 0:192], 192)
@@ -534,6 +598,7 @@ def rank_program(g, core, T, topo):
         for h in range(2):
             lo, hi = 128 * h, 128 * h + 128
             V("qz", "xq%d" % (t + 1) + "ab"[h], " ".join("xs%d%d" % (b, h) for b in range(4)), T["xq%d" % (t + 1)][:, lo:hi], T["xp%d" % (t + 1)][:, lo:hi], T.xs[:, 4 * lo:4 * hi])
+    place[0] = 0
     xk = "xq%d" % R
     xq, xp = T[xk], T["xp%d" % R]
     S("olr", "lt", T.olr[:], T.lt[:, 0:512], ACT.Copy)
@@ -543,9 +608,9 @@ def rank_program(g, core, T, topo):
         mm(pa, T.vq[:, 0:128], "vq vp", T.vp[:, 0:128], xq[:, lo:hi], xk + "ab"[h], xp[:, lo:hi], 128)
         dma("y", "oc%d" % h, [xk + "ab"[h]], [], T.oc[:, 4 * lo:4 * hi], xq[:, lo:hi].bitcast(dt.uint8), 2500.0)
         V("cp", "ms%d" % h, pa, T.ms[:, lo:hi], T[pa][:, 0:128])
-        dma("sy"[h], "oy%d" % h, ["ms%d" % h], [], T.y[:, lo:hi], T.ms[:, lo:hi], 2500.0)
+        dma("ys"[h], "oy%d" % h, ["ms%d" % h], [], T.y[:, lo:hi], T.ms[:, lo:hi], 2500.0)
     for k in range(4):
-        dma("s", "os%d" % k, [xk + "a", xk + "b"], [], T.osc[4 * k:4 * k + 4, 0:256], xp[32 * k:32 * k + 4, 0:256])
+        dma("sssy"[k], "os%d" % k, [xk + "a", xk + "b"], [], T.osc[4 * k:4 * k + 4, 0:256], xp[32 * k:32 * k + 4, 0:256])
 
     total, waited = {}, {q: {} for q in queues}
     if len(calls) not in ORDER:

import numpy as np
from concourse.mybir import dt, AluOpType, ActivationFunctionType, AxisListType

N = 8
R = 3
C = 256
NS = 8
NE = 9
NF = 7
U = 2.0 ** -18
CYC, LAT, DMA, NEAR, FAR, SLACK = 0.85, 220.0, 1800.0, 1750.0, 3500.0, 100.0
SEED, SPREAD, STEPS, GIVE, SOONER = 12, 0.0, 70000, 25.0, 200.0
SLOW = 1.1
MEAN, AHEAD, EARLY = 1.0, 500.0, 6500.0
REACH = 6
ORDER = {}
F32, BF, I32, U16, U8, X4 = "float32", "bfloat16", "int32", "uint16", "uint8", "float8_e4m3fn_x4"


def _sb(n, d):
    return ("sbuf", [128, n], d)


SCRATCH = {
    "xt": _sb(1024, BF), "xs": _sb(1024, BF), "ut": _sb(512, BF), "vt": _sb(512, BF), "et": _sb(520, BF),
    "rl16": _sb(32, U16),
    "uq": _sb(128, X4), "up": _sb(128, U8), "uq2": _sb(128, X4),
    "up2": _sb(128, U8), "vq": _sb(128, X4), "vp": _sb(128, U8), "eq": _sb(512, X4), "ep": _sb(512, U8),
    "wq": _sb(512, X4), "wp": _sb(512, U8),
    "zt": _sb(768, BF), "zq": _sb(192, X4), "zp": _sb(192, U8),
    "pi": _sb(4, I32), "pf": _sb(16, F32), "sm": _sb(96, F32), "idw": _sb(272, F32), "idb": _sb(272, BF), "rp": _sb(128, F32),
    "nmask": _sb(128, F32), "thr": _sb(128, F32), "sc0": _sb(128, F32), "nw": _sb(64, F32), "nwb": _sb(16, BF), "nT": _sb(96, F32),
    "upl": _sb(8, U16), "w256": _sb(512, F32), "tsel": _sb(272, F32),
    "dg": _sb(512, BF), "dg1": _sb(80, BF), "cl": _sb(784, BF), "clo": _sb(784, BF),
    "cl16": _sb(50, U16), "wt": _sb(480, F32), "md": _sb(240, BF), "de": _sb(200, BF), "cm": _sb(2, F32),
    "aa": _sb(1280, F32), "asc": _sb(256, F32),
    "ms": _sb(256, F32), "sc": _sb(256, F32), "ssb": _sb(256, F32), "c0": _sb(512, BF), "c1": _sb(512, BF), "c2": _sb(512, BF),
    "wc16": _sb(16, U16), "va": _sb(512, F32), "vb": _sb(256, F32), "vc": _sb(256, F32), "pq": _sb(528, F32),
    "pb": _sb(512, BF), "t3": ("sbuf", [128, 32, 16], BF), "ab": _sb(72, U16), "la": _sb(72, U16),
    "f0": _sb(256, BF), "f1": _sb(96, BF), "ne": _sb(192, BF), "no": _sb(192, BF), "fo": _sb(256, BF), "lq16": _sb(16, U16),
    "wr": _sb(256, BF), "ur": _sb(256, BF), "jk": _sb(4096, BF), "jo": _sb(4096, BF), "acc": _sb(272, F32), "acc2": _sb(16, F32),
    "a16": _sb(16, U16), "ah": _sb(16, I32), "hi": _sb(16, BF), "k16": _sb(256, U16), "nB": _sb(32, F32), "kap": _sb(256, F32), "r16": _sb(16, U16),
    "qq": _sb(264, BF), "qj": _sb(528, BF), "off": _sb(4, U16), "g2": _sb(128, F32), "t2": _sb(192, F32),
    "gp": _sb(144, F32), "ee": _sb(80, BF), "so": _sb(240, BF), "nd": _sb(84, F32), "ff": _sb(84, F32), "kc": _sb(48, F32),
    "abi": _sb(84, F32), "bq": _sb(48, F32), "bt16": _sb(12, U16),
    "btv": _sb(192, BF), "abd": ("sbuf", [128, 16, 200], BF), "abo": ("sbuf", [128, 16, 200], BF),
    "ei": _sb(64, F32), "ek": _sb(32, BF), "e16": _sb(16, U16),
    "li": _sb(12, F32), "ln16": _sb(2, U16), "m16": _sb(2, U16), "mt": _sb(32, BF), "lt": _sb(544, BF), "lo": _sb(512, BF),
    "lw": _sb(32, I32), "lw16": _sb(32, U16), "olr": _sb(512, F32),
    "at": _sb(768, BF), "f2": _sb(1088, BF), "fw": _sb(1024, BF), "hb": _sb(832, F32),
}
PS = ["ps1", "ps2", "pd0", "pd1", "pd2", "pd3", "ph0", "ph1"]
for _t in range(R + 1):
    SCRATCH["xq%d" % _t] = _sb(512, X4)
    SCRATCH["xp%d" % _t] = _sb(512, U8)
for _n in PS:
    SCRATCH[_n] = ("psum", [128, 512], F32)

DMAS = ["dx0", "dx1", "du", "dv", "dwc", "dws", "dn0", "das", "oy0", "oy1", "ool", "oc0", "oc1", "os0", "os1", "os2", "os3"]
SEMAPHORES = ["sv", "ss", "sp", "sg", "lc"] + ["ax%d" % t for t in range(R)] + ["al%d" % t for t in range(R)] + DMAS

LS, LP, LQ, LX, LE = 0, 128, 288, 384, 400


def width(ap):
    return int(np.prod([int(k) for k in ap.shape[1:]]))


def in_order(calls):
    n = len(calls)
    after = [[] for _ in calls]
    for i, c in enumerate(calls):
        for d in c["deps"]:
            after[d].append(i)
    chain = [0.0] * n
    for i in range(n - 1, -1, -1):
        chain[i] = calls[i]["len"] + calls[i]["load"] + max([LAT + chain[k] for k in after[i]] + [0.0])
    x = SEED
    for i in range(n):
        x = (x * 1103515245 + 12345) % 2147483648
        chain[i] += SPREAD * x / 2147483648 + calls[i]["lift"]
    left = [len(c["deps"]) for c in calls]
    ready = {i: 0.0 for i in range(n) if left[i] == 0}
    free, order = {}, []
    while ready:
        start = {i: max(t, free.get(calls[i]["q"], 0.0)) for i, t in ready.items()}
        first = min(start, key=lambda i: (start[i], i))
        q = calls[first]["q"]
        best = first
        for i in ready:
            if calls[i]["q"] == q and chain[i] > chain[best] and start[i] <= start[first] + max(0.0, min(calls[first]["hold"] - SLACK + 0.3 * calls[i]["lift"], chain[i] - chain[first])):
                best = i
        if q is None:
            best = first
        order.append(best)
        t = start[best]
        del ready[best]
        if q is not None:
            free[q] = t + calls[best]["hold"]
        calls[best]["end"] = t + calls[best]["len"]
        for k in after[best]:
            left[k] -= 1
            if left[k] == 0:
                ready[k] = max(calls[d]["end"] + LAT for d in calls[k]["deps"])
    return improved(calls, after, order)


def improved(calls, after, order):
    n = len(calls)
    qs, deps, hold = [c["q"] for c in calls], [c["deps"] for c in calls], [c["hold"] for c in calls]
    lens = [([c["len"] for c in calls], hold),
            ([c["len"] * SLOW if c["len"] == c["hold"] else c["len"] - (SOONER if c["len"] == NEAR else 0.0) for c in calls],
             [c["hold"] * SLOW if c["len"] == c["hold"] else c["hold"] for c in calls])]

    def run(order, case, first, old):
        length, hold = case
        end, cause, free, last = old[0][:], old[1][:], {}, {}
        for i in order[:first]:
            last[qs[i]] = i
        for q, i in last.items():
            free[q] = end[i] - length[i] + hold[i]
        for i in order[first:]:
            t, why = 0.0, -1
            for d in deps[i]:
                if end[d] + LAT > t:
                    t, why = end[d] + LAT, d
            q = qs[i]
            if q is not None:
                if free.get(q, 0.0) > t:
                    t, why = free[q], -2 - last[q]
                free[q], last[q] = t + hold[i], i
            end[i], cause[i] = t + length[i], why
        return end, cause

    def judge(order, first, olds):
        total, pairs, news = 0.0, [], []
        for length, old in zip(lens, olds):
            end, cause = run(order, length, first, old)
            news.append((end, cause))
            i = end.index(max(end))
            total += end[i] + MEAN * sum(end) / n
            if first and end[i] > max(old[0]) + 2 * GIVE:
                return 1e18, pairs, news
            while cause[i] != -1:
                if cause[i] < -1:
                    pairs.append((-2 - cause[i], i))
                    i = -2 - cause[i]
                else:
                    i = cause[i]
        return total, pairs, news
    best, pairs, now = judge(order, 0, [([0.0] * n, [-1] * n) for _ in lens])
    top, kept, state = best, order, [SEED]
    same = {}
    for i, c in enumerate(calls):
        same.setdefault(c["place"], []).append(i)

    def draw(k):
        state[0] = (state[0] * 1103515245 + 12345) % 2147483648
        return (state[0] >> 12) % k

    def moved(order, a, b, ahead):
        pa, pb = order.index(a), order.index(b)
        if pa > pb or not deps[a] and not deps[b] and hold[a] == hold[b] == 60.0:
            return order, n
        mid = order[pa + 1:pb]
        if ahead:
            need = {b}
            for k in reversed(mid):
                if any(s in need for s in after[k]):
                    need.add(k)
            if any(s in need for s in after[a]):
                return order, n
            return order[:pa] + [k for k in mid if k in need] + [b, a] + [k for k in mid if k not in need] + order[pb + 1:], pa
        need = {a}
        for k in mid:
            if any(d in need for d in deps[k]):
                need.add(k)
        if any(d in need for d in deps[b]):
            return order, n
        return order[:pa] + [k for k in mid if k not in need] + [b, a] + [k for k in mid if k in need] + order[pb + 1:], pa
    for step in range(STEPS):
        a, b = pairs[draw(len(pairs))]
        if draw(2):
            pa = draw(n - 1)
            a = order[pa]
            later = [k for k in order[pa + 1:pa + 60] if qs[k] == qs[a]][:REACH]
            if qs[a] is None or not later:
                continue
            b = later[draw(len(later))]
        both, ahead = [(a, b)], draw(2)
        if calls[a]["place"] and calls[b]["place"] and draw(2):
            ta, tb = same[calls[a]["place"]], same[calls[b]["place"]]
            shift = tb.index(b) - ta.index(a)
            both = [(k, tb[j + shift]) for j, k in enumerate(ta) if 0 <= j + shift < len(tb)]
        new, pa = order, n
        for a, b in both:
            new, p = moved(new, a, b, ahead)
            pa = min(pa, p)
        if pa == n:
            continue
        total, p, times = judge(new, pa, now)
        if total <= best + GIVE * len(both) * (1.0 - step / STEPS) * draw(64) / 64:
            order, best, pairs, now = new, total, p, times
            if total < top:
                top, kept = total, new
    return kept


def rank_program(g, core, T, topo):
    rank = T.rank_of(core)
    if rank is None:
        return
    A = AluOpType
    ACT = ActivationFunctionType
    XAX = AxisListType.X
    queues = {"v": g.vector, "s": g.scalar, "p": g.tensor, "g": g, "y": g.sync}
    place = [0]
    calls, wr, rd, lift = [], {}, {}, [0.0, 0.0]

    def note(q, reads, writes, sem, inc, issue, length, hold):
        deps = set()
        for k in reads:
            if k in wr:
                deps.add(wr[k])
            if k in PS:
                deps.update(r for r in rd.get(k, []) if calls[r]["q"] != q)
        for k in writes:
            if k in wr:
                deps.add(wr[k])
            deps.update(rd.get(k, []))
        i = len(calls)
        calls.append({"q": q, "deps": sorted(deps), "sem": sem, "inc": inc, "issue": issue, "len": length, "hold": hold, "lift": lift[0], "load": lift[1], "place": place[0]})
        place[0] += place[0] > 0
        for k in writes:
            wr[k] = i
            rd[k] = []
        for k in reads:
            if k not in writes:
                rd.setdefault(k, []).append(i)

    fns = {"memset": g.vector.memset, "tt": g.vector.tensor_tensor, "ts": g.vector.tensor_scalar,
           "cp": g.vector.tensor_copy, "red": g.vector.tensor_reduce, "scan": g.vector.tensor_tensor_scan,
           "tr": g.vector.transpose, "qz": g.vector.quantize_mx, "act": g.scalar.activation,
           "mm": g.tensor.matmul_mx, "iota": g.iota, "asel": g.affine_select}

    def op(q, reads, writes, name, *args, **kw):
        picks = [k for k, a in enumerate(args[:2]) if isinstance(a, tuple)]
        args = [a[0].indirect(a[1]) if isinstance(a, tuple) else a for a in args]
        if picks:
            n = width(args[1 - picks[0]])
            length = (50.0 if q == "v" else 65.0) + (1.56 if picks[0] else 3.8) * CYC * n
        elif name == "qz":
            length = 12.0 + 0.22 * width(args[2])
        elif name == "mm":
            length = 1.2 * (width(args[0]) + 16)
        elif name in ("iota", "asel"):
            length = 140.0 + 2 * CYC * width(args[0])
        elif name == "act":
            length = (60.0 if "accum_out" in kw else 40.0) + CYC * max(64, width(args[0]))
        else:
            sides = {"memset": 1, "tt": 3, "scan": 3}.get(name, 2)
            each = 0.5 if name != "red" and all("16" in str(a.dtype) for a in args[:sides]) else 1.0
            if name == "tt":
                each = 1.0 if any(k in PS for k in reads) else 2.0
            length = CYC * max(64, each * width(args[sides - 1]))
        note(q, reads, writes, "s" + q, 1, lambda: fns[name](*args, **kw).then_inc(T.sem["s" + q], 1), length, length)

    def dma(q, sem, reads, writes, out, in_, length=DMA):
        note(q, reads, writes, sem, 16, lambda: queues[q].dma_start(out, in_).then_inc(T.sem[sem], 16), length, 60.0)

    def V(name, writes, reads, *args, **kw):
        op("v", reads.split(), writes.split(), name, *args, **kw)

    def S(writes, reads, out, in_, func, **kw):
        op("s", reads.split(), writes.split(), "act", out, in_, func, **kw)

    def iota(key, out, pattern, base, cm=0, on=""):
        kw = {} if key == "pi" else {"allow_small_or_imprecise_dtypes": True}
        op("g", on.split(), [key], "iota", out, pattern, base, cm, **kw)

    def mm(out, st, stk, sc, mv, mvk, mp, n):
        op("p", stk.split() + mvk.split(), [out], "mm", T[out][:, 0:n], st, sc, mv, mp, True, True)

    def names(stem, lo, hi):
        return " ".join(stem + str(c) for c in range(lo, hi))

    lift[1] = 3000.0
    dma("y", "du", [], ["ut"], T.ut[:], T.u[:], 1600.0)
    lift[1] = 1500.0
    dma("s", "dx0", [], ["xta"], T.xt[:, 0:512], T.x[:, 0:512], 1850.0)
    lift[1] = 0.0
    dma("y", "dx1", [], ["xt"], T.xt[:, 512:1024], T.x[:, 512:1024], 2100.0)
    dma("s", "dn0", [], ["lw"], T.lw[:], T.nb[:], 2500.0)

    iota("pi", T.pi[:, 0:1], [[0, 1]], 0, 1)
    iota("sm1", T.sm[:, 8:14], [[-1, 6]], 7)
    iota("idw", T.idw[:], [[1, 272]], 0)
    iota("sm0", T.sm[:, 0:8], [[16, 8]], 0)
    iota("rp", T.rp[:], [[0, 8], [1, 16]], 0)
    V("ts", "pi1", "pi", T.pi[:, 1:2], T.pi[:, 0:1], 15, None, A.bitwise_and)
    V("ts", "pi2", "pi", T.pi[:, 2:3], T.pi[:, 0:1], 31, None, A.bitwise_and)
    V("ts", "pi3", "pi", T.pi[:, 3:4], T.pi[:, 0:1], 16, None, A.bitwise_and)
    V("cp", "pf", "pi1 pi2 pi3", T.pf[:, 0:3], T.pi[:, 1:4])
    r16, p32, odd16 = T.pf[:, 0:1], T.pf[:, 1:2], T.pf[:, 2:3]
    V("ts", "smS", "sm1 pf", T.sm[:, 25:30], T.sm[:, 9:14], r16, None, A.is_equal)
    V("ts", "smT", "pf", T.sm[:, 24:25], r16, 7.0, None, A.is_ge)
    V("memset", "one", "", T.jo[:, 0:520], 1.0)
    V("memset", "cl0", "", T.cl[:, LS:LE], 0.0)
    V("memset", "c0", "", T.c0[:], 1.0)
    V("memset", "c0z", "c0", T.c0[:, 0:512:32], 0.0)
    V("memset", "c1z", "", T.c1[:], 0.0)
    V("cp", "upl", "sm0", T.upl[:], T.sm[:, 0:8])
    adds = [T.aa[:, 256 * k:256 * k + 256] for k in range(5)] + [T.asc[:]]
    for k in range(6):
        S("asc" if k == 5 else "a%d" % k, "idw smS" if k else "idw smT", adds[k], T.idw[:, 0:256], ACT.Copy, scale=T.sm[:, 24 + k:25 + k])
    V("ts", "pf7", "pf", T.pf[:, 7:8], r16, 15.0, 256.0, A.is_lt, A.mult)
    V("ts", "pf8", "pf", T.pf[:, 8:9], r16, 2.0, 1.0, A.mult, A.add)
    V("ts", "pf9", "pf", T.pf[:, 9:10], p32, U, None, A.mult)
    fix = T.pf[:, 7:8]
    V("ts", "dg2", "idw pf", T.dg1[:, 16:33], T.idw[:, 0:17], r16, 1024.0, A.is_equal, A.mult)
    V("ts", "rl16", "idw pf", T.rl16[:, 0:8], T.idw[:, 0:8], 0.0, r16, A.mult, A.add)
    V("ts", "dg3", "dg2", T.dg1[:, 49:64], T.dg1[:, 16:31], -0.25, None, A.mult)
    V("memset", "dg4", "", T.dg1[:, 48:49], 0.0)
    V("tt", "dgs", "dg2 dg3 dg4", T.dg1[:, 64:80], T.dg1[:, 16:32], T.dg1[:, 48:64], A.add)
    S("dga", "dgs rl16", T.dg[:, 0:128], (T.dg1[:, 64:80], T.rl16[:, 0:8]), ACT.Copy)
    S("dgb", "dga", T.dg[:, 128:256], T.dg[:, 0:128], ACT.Copy)
    S("dg", "dgb", T.dg[:, 256:512], T.dg[:, 0:256], ACT.Copy)
    V("ts", "nmask", "rp pf", T.nmask[:], T.rp[:, 0:128], r16, -1.0, A.is_equal, A.mult)
    V("ts", "thr", "rp pf", T.thr[:], T.rp[:, 0:128], r16, 1e29, A.not_equal, A.mult)
    S("sc0_", "rp", T.sc0[:], T.rp[:, 0:128], ACT.Sign)
    V("qz", "uq up", "ut", T.uq[:, 0:128], T.up[:, 0:128], T.ut[:, 0:512])
    V("cp", "uq2", "uq upl", T.uq2[:, 0:128].bitcast(dt.uint32), (T.uq[:, 0:128].bitcast(dt.uint32), T.upl[:, 0:8]))
    S("up2", "up upl", T.up2[:, 0:128], (T.up[:, 0:128], T.upl[:, 0:8]), ACT.Copy)
    V("qz", "xq0a", "xta", T.xq0[:, 0:128], T.xp0[:, 0:128], T.xt[:, 0:512])
    V("qz", "xq0b", "xt", T.xq0[:, 128:256], T.xp0[:, 128:256], T.xt[:, 512:1024])
    V("cp", "lw16", "lw", T.lw16[:], T.lw[:])
    V("tt", "c0", "lw", T.c0[:, 31:512:32], T.lw[:, 16:32], T.lw[:, 0:16], A.subtract)
    V("cp", "c1o", "lw c1z", T.c1[:, 31:512:32], T.lw[:, 0:16])

    def apart(reads, link, plus):
        V("ts", "lq0", "c0", T.nT[:, 0:16], T.c0[:, 31:512:32], 0.0, 256.0, A.is_equal, A.mult)
        V("tt", "lq1", "lq0 " + reads, T.nT[:, 16:32], link, T.nT[:, 0:16], A.add)
        V("ts", "lq16", "lq1 " + reads, T.lq16[:], T.nT[:, 16:32], plus, None, A.add)
    apart("lw", T.lw[:, 16:32], 0.0)

    parts = [(LS, 128, [[12, 8], [0, 16]], 11), (LP, 36, [[1, 6], [0, 6]], 2), (LP + 37, 36, [[1, 6], [0, 6]], 34),
             (LP + 96, 24, [[96, 2], [32, 2], [1, 6]], 2), (LP + 120, 12, [[32, 2], [0, 6]], 0), (LQ, 36, [[0, 6], [1, 6]], 2),
             (LQ + 37, 36, [[0, 6], [1, 6]], 34), (LX, 12, [[32, 2], [0, 6]], 0)]
    for k, (lo, n, pattern, base) in enumerate(parts):
        iota("cl%d" % (k + 1), T.cl[:, lo:lo + n], pattern, base, on="cl0")
    iota("clx", T.cl[:, LP + 36:LP + 74:37], [[0, 2]], 64, on="cl2 cl3")
    iota("cly", T.cl[:, LQ + 36:LQ + 74:37], [[0, 2]], 64, on="cl6 cl7")

    def wrap(lo, hi, key, reads):
        V("scan", key, reads, T.clo[:, lo:hi], T.dg[:, 0:hi - lo], T.cl[:, lo:hi], 0.0, A.add, A.min)
    wrap(LS, LP, "clob", "cl1 dga")
    wrap(LP, LE, "cloc", "cl4 cl5 clx cly cl8 dg")
    V("ts", "cl16b", "clob pf7", T.cl16[:, LS // 16:LP // 16], T.clo[:, LS + 15:LP:16], fix, None, A.add)
    V("ts", "cl16c", "cloc pf7 pf", T.cl16[:, LP // 16:LE // 16], T.clo[:, LP + 15:LE:16], fix, odd16, A.add, A.add)

    def lst(lo, n):
        return T.cl16[:, lo // 16:(lo + n) // 16]

    iota("f0", T.f0[:], [[32, 8], [0, 32]], 0)
    iota("f1", T.f1[:], [[0, 96]], 0)
    iota("f1", T.f1[:, 0:96:12], [[0, 8]], 2)
    iota("nw0", T.nw[:, 0:16], [[16, 16]], 0)
    iota("tsz", T.tsel[:, 32:272], [[0, 240]], 0)
    for k, (a, b) in enumerate(((16, 16), (17, 16), (17, 17))):
        iota("wt%d" % k, T.wt[:, 80 * k:80 * k + 74], [[0, 74]], b)
        iota("wu%d" % k, T.wt[:, 80 * k + 6:80 * k + 36:6], [[0, 5]], a - 5 * b, on="wt%d" % k)
        iota("wv%d" % k, T.wt[:, 80 * k + 43:80 * k + 73:6], [[0, 5]], a - 5 * b, on="wt%d" % k)
        iota("ww%d" % k, T.wt[:, 80 * k + 36:80 * k + 74:37], [[0, 2]], -5 * (a + b), on="wt%d" % k)
        iota("wx%d" % k, T.wt[:, 80 * k:80 * k + 74:37], [[0, 2]], -512, on="wt%d" % k)
    iota("ffa", T.ff[:, 1:48:2], [[0, 24]], 1)
    iota("ffb", T.ff[:, 50:84:3], [[0, 12]], 1)
    iota("ndz", T.nd[:, 49:84:3], [[0, 12]], 0)
    iota("kc", T.kc[:, 0:24], [[256, 2], [0, 2], [1, 6]], 0)
    iota("vaz", T.va[:, 256:512], [[0, 256]], -1)
    lift[1] = 9000.0 - EARLY
    op("g", ["one"], ["et"], "asel", T.et[:], T.jo[:, 0:520], [[-1, 520]], A.is_equal, 0.0, 3, 4)
    lift[1] = 0.0
    iota("t2c", T.t2[:, 64:96], [[0, 32]], 0)
    iota("t2d", T.t2[:, 160:192], [[0, 32]], -1)
    iota("pqz", T.pq[:, 256:264], [[0, 8]], 256)
    iota("pqy", T.pq[:, 520:528], [[0, 8]], 256)
    iota("de0", T.de[:], [[0, 200]], -16)
    iota("de1", T.de[:, 16:192:16], [[0, 11]], 239, on="de0")
    iota("de2", T.de[:, 0:193:192], [[251, 2]], 0, on="de0")
    iota("cm", T.cm[:], [[1, 2]], -1)
    iota("ekz", T.ek[:, 0:32:2], [[0, 16]], 0)
    iota("emz", T.ei[:, 0:32:2], [[0, 16]], -255)
    iota("qqz", T.qq[:, 256:264], [[0, 8]], 0)
    iota("ltz", T.lt[:, 512:544], [[0, 32]], 0)
    iota("abz", T.abd[:, :, 192], [[0, 16]], 1024)
    for b in range(4):
        iota("f2z%d" % b, T.f2[:, 272 * b + 256:272 * b + 272], [[0, 16]], 0)
        iota("hbz%d" % b, T.hb[:, 208 * b + 192:208 * b + 208], [[0, 16]], 0)
    S("f0", "f0 pf9", T.f0[:], T.f0[:], ACT.Identity, bias=T.pf[:, 9:10], scale=U)
    S("w256a", "idw", T.w256[:, 0:512:2], T.idw[:, 0:256], ACT.Copy, scale=256 * U)
    S("w256b", "idw", T.w256[:, 1:512:2], T.idw[:, 0:256], ACT.Copy, scale=256 * U)
    S("nw1", "nw0 pf", T.nw[:, 16:32], T.nw[:, 0:16], ACT.Identity, bias=r16, scale=1.0)
    S("nwb", "nw1", T.nwb[:], T.nw[:, 16:32], ACT.Copy)
    S("nw2", "nw1", T.nw[:, 32:48], T.nw[:, 16:32], ACT.Identity, bias=-0.5, scale=1.0)
    S("nw3", "nw1", T.nw[:, 48:64], T.nw[:, 16:32], ACT.Copy, scale=-1024.0)
    for k in range(3):
        S("md%d" % k, "wu%d wv%d ww%d wx%d" % (k, k, k, k), T.md[:, 80 * k:80 * k + 74], T.wt[:, 80 * k:80 * k + 74], ACT.Copy, scale=1.0 / 256)
    S("kc", "kc", T.kc[:, 0:24], T.kc[:, 0:24], ACT.Copy, scale=1.0 / 256)
    S("idb", "idw", T.idb[:], T.idw[:], ACT.Copy)
    S("cm", "cm pf8", T.cm[:], T.cm[:], ACT.Identity, bias=T.pf[:, 8:9], scale=1.0)
    S("lt", "idb lw16", T.lt[:, 0:512], (T.idb[:, 0:272], T.lw16[:, 0:32]), ACT.Copy)
    V("ts", "ts2", "idw pf8", T.sm[:, 40:73], T.idw[:, 0:33], T.pf[:, 8:9], -1.0 / U, A.is_equal, A.mult)
    V("tt", "tsel", "ts2", T.tsel[:, 0:32], T.sm[:, 41:73], T.sm[:, 40:72], A.subtract)

    lift[1] = 0.0
    dst = T.cores[(rank + 1) % N]
    prv = T.cores[(rank - 1) % N]

    engs = topo.engines
    emask = sum(1 << k for k in engs(core, dst))
    rid, pid = topo.addr(dst)[:2]
    nout, nin = len(engs(core, dst)), len(engs(prv, core))

    def send(key, sem, arrives, pairs, length):
        def issue():
            for out, in_ in pairs:
                g.remote_dma(out, in_, T.sem[sem], T.sem.lc, pid, rid, emask)
        note("g", key, ["sent" + sem], "lc", nout * len(pairs), issue, 0.0, 3000.0 if sem[2] == "0" else 300.0 * len(pairs))
        note(None, ["sent" + sem], [arrives], sem, nin * len(pairs), None, length, 0.0)

    for t in range(R):
        place[0] = 1
        xk = "xq%d" % t
        xq, xp = T[xk], T["xp%d" % t]
        for h, (pv, pa) in enumerate((("ps1", "ps2"), ("ph0", "ph1"))):
            lo, hi = 128 * h, 128 * h + 128
            for k in (pv, pa):
                mm(k, T.uq2[:, 0:128], "uq2 up2", T.up2[:, 0:128], xq[:, lo:hi], xk + "ab"[h], xp[:, lo:hi], 128)
            lift[1] = AHEAD
            V("tt", "c1e%d" % h, pv + " thr c1z", T.c1[:, 2 * lo:2 * hi:2], T[pv][:, 0:128], T.thr[:, 0:128], A.is_gt)
            V("scan", "c2%d" % h, "c0 c0z c1o c1e%d" % h, T.c2[:, 2 * lo:2 * hi], T.c0[:, 2 * lo:2 * hi], T.c1[:, 2 * lo:2 * hi], 0.0, A.mult, A.add)
            lift[1] = 0.0
            V("tt", "ms%d" % h, pv + " nmask", T.ms[:, lo:hi], T[pv][:, 0:128], T.nmask[:, 0:128], A.mult)
            S("ssb%d" % h, pa, T.ssb[:, lo:hi], T[pa][:, 0:128], ACT.Copy)
            V("scan", "sc%d" % h, "ms%d sc0_" % h, T.sc[:, lo:hi], T.sc0[:, 0:128], T.ms[:, lo:hi], 0.0, A.mult, A.add)
            V("cp", "wc%d" % h, "c2%d" % h, T.wc16[:, 8 * h:8 * h + 8], T.c2[:, 2 * lo + 31:2 * hi:32])
            lift[1] = AHEAD
            V("tt", "vc%d" % h, "a0 a1 wc%d" % h, T.vc[:, lo:hi], (adds[0], T.wc16[:, 8 * h:8 * h + 8]), T.aa[:, 256 + lo:256 + hi], A.add)
            lift[1] = 0.0
        dma("y", "das", ["ssb0", "ssb1"], ["asc", "asd%d" % t], T.asc[0:128:16, :], T.ssb[0:128:16, :])
        if t == 0:
            was, place[0] = place[0], 0
            dma("y", "dwc", ["asd0"], ["wq"], T.wq[:, 0:512].bitcast(dt.uint8), T.wc[:], 3300.0)
            dma("y", "dws", ["asd0"], ["wp"], T.wp[:, 0:512], T.ws[:], 2700.0)
            dma("y", "dv", ["asd0"], ["vt"], T.vt[:], T.v[:], 2900.0)
            V("qz", "vq vp", "vt", T.vq[:, 0:128], T.vp[:, 0:128], T.vt[:, 0:512])
            place[0] = was
        send([xk + "a", xk + "b", "asd%d" % t], "ax%d" % t, "xn%d" % t, [(xq[:, 256:512].bitcast(dt.uint8), xq[:, 0:256].bitcast(dt.uint8)), (xp[:, 256:512], xp[:, 0:256])], FAR)
        for b in range(4):
            if t == 0:
                was, place[0], lift[1] = place[0], 0, EARLY
                V("qz", "eq%d" % b, "et vc1", T.eq[:, 128 * b:128 * b + 128], T.ep[:, 128 * b:128 * b + 128], T.et[:, 3 - b:515 - b])
                place[0], lift[1] = was, 0.0
            mm("pd%d" % b, T.eq[:, 128 * b:128 * b + 128], "eq%d" % b, T.ep[:, 128 * b:128 * b + 128], xq[:, 0:512], "%sa %sb xn%d" % (xk, xk, t), xp[:, 0:512], 512)
            S("f2_%d" % b, "pd%d" % b, T.f2[:, 272 * b:272 * b + 256], T["pd%d" % b][:, 256:512], ACT.Copy, scale=0.5)
            S("fw%d" % b, "pd%d" % b, T.fw[:, 256 * b:256 * b + 256], T["pd%d" % b][:, 0:256], ACT.Copy)
        V("ts", "jk0", "ssb0 ssb1 sc0", T.jk[:, 0:256], T.ssb[:], T.sc[:, 15:16], 0.0, A.add, A.is_gt)
        V("ts", "jl0", "ssb0 ssb1 sc0", T.jo[:, 768:1024], T.ssb[:], T.sc[:, 15:16], 0.0, A.add, A.is_lt)
        V("scan", "acc0", "jk0 jl0", T.acc[:, 0:256], T.jk[:, 0:256], T.jo[:, 768:1024], 0.0, A.add, A.subtract)
        for c in range(1, 16):
            lift[1] = 280.0 * (15 - c) + (400.0 if c < 12 else 0.0)
            S("jk%d acc%d" % (c, c), "ssb0 ssb1 sc%d" % (c // 8), T.jk[:, 256 * c:256 * c + 256], T.ssb[:], ACT.Sign, bias=T.sc[:, 16 * c + 15:16 * c + 16], scale=1.0, accum_out=T.acc[:, 255 + c:256 + c])
        cur, key = T.vc[:, 0:256], "vc0 vc1"
        for k in range(2, 6):
            nxt = "va" if k % 2 else "vb"
            V("tt", nxt, key + (" wc0 wc1 asc" if k == 5 else " wc0 wc1 a%d" % k), T[nxt][:, 0:256], (cur, T.wc16[:, 0:16]), adds[k], A.add)
            cur, key = T[nxt][:, 0:256], nxt
        S("pq0", key + " lw16", T.pq[:, 0:256], (cur, T.lw16[:, 0:16]), ACT.Copy)
        S("pq1", key + " lw16", T.pq[:, 264:520], (cur, T.lw16[:, 16:32]), ACT.Copy)
        for h in range(2):
            lo, hi, a, b, H = 128 * h, 128 * h + 128, 8 * h, 8 * h + 8, str(h)
            V("ts", "a16" + H, names("acc", a, b), T.a16[:, a:b], T.acc[:, 255 + a:255 + b], 255.0, None, A.add)
            V("ts", "ah" + H, names("acc", a, b), T.ah[:, a:b], T.acc[:, 255 + a:255 + b], 0.5, 127.25, A.mult, A.add)
            V("ts", "nb0" + H, "ah" + H, T.hi[:, a:b], T.ah[:, a:b], 256.0, None, A.mult)
            V("tt", "nB" + H, "nw2 nb0" + H, T.nB[:, a:b], T.hi[:, a:b], T.nw[:, 32 + a:32 + b], A.add)
            V("cp", "pb0" + H, key + " lw16", T.pb[:, lo:hi], (cur, T.lw16[:, a:b]))
            lift[0] = 1000.0
            S("pb1" + H, key + " vaz lq16", T.pb[:, 256 + lo:256 + hi], (T.va[:, 0:512], T.lq16[:, a:b]), ACT.Copy)
            lift[0] = 0.0
            p, q = T.t3[:, a:b, :], T.t3[:, 16 + a:16 + b, :]
            V("tr", "t3p" + H, "pb0" + H, p, T.pb[:, lo:hi])
            V("tr", "t3q" + H, "pb1" + H, q, T.pb[:, 256 + lo:256 + hi])
            both = "t3p%d t3q%d" % (h, h)
            V("tt", "ne0" + H, both, T.ne[:, 96 * h:96 * h + 96:2], T.t3[:, a:b, 2:8], T.t3[:, 16 + a:16 + b, 8:14], A.not_equal)
            V("tt", "ne1" + H, both, T.ne[:, 96 * h + 1:96 * h + 96:2], T.t3[:, a:b, 8:14], T.t3[:, 16 + a:16 + b, 2:8], A.not_equal)
            V("scan", "no" + H, "f1 ne0%d ne1%d" % (h, h), T.no[:, 96 * h:96 * h + 96], T.f1[:, 0:96], T.ne[:, 96 * h:96 * h + 96], 1.0, A.add, A.min)
            V("tt", "fo" + H, "f0 cl16b no" + H, T.fo[:, lo:hi], (T.no[:, 96 * h:96 * h + 96], lst(LS, 128)), T.f0[:, lo:hi], A.max)
            V("tr", "wr" + H, "fo" + H, T.wr[:, lo:hi], T.fo[:, lo:hi])
            V("tt", "kap" + H, "w256a w256b a16%d wr%d" % (h, h), T.kap[:, lo:hi], (T.w256[:, 0:512], T.a16[:, a:b]), T.wr[:, lo:hi], A.add)
            V("ts", "k16" + H, "kap" + H, T.k16[:, lo:hi], T.kap[:, lo:hi], 1.0 / U, None, A.mult)
        for h in range(2):
            V("ts", "ur%d" % h, "wr%d" % h, T.ur[:, 128 * h:128 * h + 128], T.wr[:, 128 * h:128 * h + 128], 256 * U, 256 * U, A.min, A.subtract)
        for h, (a, m, b) in enumerate(((0, 4, 8), (8, 4 + NS, 16))):
            for c in range(a, m):
                lift[1] = 280.0 * (NS - 1 - c + 4 * h)
                S("jk%d rk%d" % (c, c), "kap0 kap1 nB%d" % h, T.jk[:, 256 * c:256 * c + 256], T.kap[:], ACT.Sign, bias=T.nB[:, c:c + 1], scale=-1.0 / U, accum_out=T.acc2[:, c:c + 1])
            lift[1] = 700.0 * (1 - h)
            for c in range(m, b):
                j = T.jk[:, 256 * c:256 * c + 256]
                V("ts", "jk%d" % c, "k160 k161 nwb nb0%d" % h, j, T.k16[:], T.hi[:, c:c + 1], T.nwb[:, c:c + 1], A.subtract, A.is_lt)
                V("scan", "rk%d jl%d" % (c, c), "jk%d" % c, T.jo[:, 256 * c:256 * c + 256], j, j, 0.0, A.add, A.max)
            lift[1] = 0.0
            V("cp", "r16b%d" % h, names("rk", m, b), T.r16[:, m:b], T.jo[:, 256 * m + 255:256 * b:256])
            V("ts", "r16a%d" % h, names("rk", a, m), T.r16[:, a:m], T.acc2[:, a:m], 0.5, 128.0, A.mult, A.add)
            V("tt", "qq%d" % h, "r16a%d r16b%d tsel tsz ur%d" % (h, h, h), T.qq[:, 128 * h:128 * h + 128], (T.tsel[:, 0:272], T.r16[:, a:b]), T.ur[:, 128 * h:128 * h + 128], A.mult)
        for h, how in enumerate((A.max, A.min)):
            V("scan", "ku%d" % h, "qq0", T.qj[:, 264 * h:264 * h + 128], T.qq[:, 0:128], T.qq[:, 0:128], 0.0, how, how)
            V("scan", "kv%d" % h, "qq1 qqz ku%d" % h, T.qj[:, 264 * h + 128:264 * h + 257], T.qq[:, 128:257], T.qq[:, 128:257], T.qj[:, 264 * h + 127:264 * h + 128], how, how)
            V("ts", "off%d" % h, "kv%d" % h, T.off[:, 2 * h:2 * h + 2], T.qj[:, 264 * h + 255:264 * h + 257], 2.0 * h - 1.0, 256.0, A.mult, A.add)
        V("cp", "g20", "pqz pq0 off0 off1", T.g2[:, 0:64], (T.pq[:, 0:264], T.off[:, 0:4]))
        S("g21", "pqy pq1 off0 off1", T.g2[:, 64:128], (T.pq[:, 264:528], T.off[:, 0:4]), ACT.Copy)
        V("tr", "t2p", "g20", T.t2[:, 0:64], T.g2[:, 0:64])
        V("tr", "t2", "g21", T.t2[:, 96:160], T.g2[:, 64:128])
        t2 = T.t2[:, 96:192]
        V("cp", "gpa", "t2p t2c cl16c", T.gp[:, 0:80], (T.t2[:, 0:96], lst(LP, 80)))
        S("gp", "t2 t2p t2c cl16c", T.gp[:, 96:144], (T.t2[:, 0:160], lst(LP + 96, 48)), ACT.Copy)
        V("tt", "ee", "t2 t2d cl16c gpa", T.ee[:], (t2, lst(LQ, 80)), T.gp[:, 0:80], A.is_equal)
        for k in (1, 0, 2):
            V("scan", "so%d" % k, "ee md%d" % k, T.so[:, 80 * k:80 * k + 74], T.md[:, 80 * k:80 * k + 74], T.ee[:, 0:74], 0.0, A.add, A.max)
        S("nd0", "gp", T.nd[:, 0:48:2], T.gp[:, 96:120], ACT.Copy, scale=-1.0)
        S("nd1", "gp", T.nd[:, 1:48:2], T.gp[:, 96:120], ACT.Copy)
        V("tt", "br", "t2 t2d cl16c gp", T.bq[:, 16:32], (t2, lst(LX, 16)), T.gp[:, 120:136], A.is_gt)
        V("tt", "dw", "gp", T.bq[:, 0:12], T.gp[:, 108:120], T.gp[:, 96:108], A.subtract)
        V("tt", "dv", "dw br", T.bq[:, 32:44], T.bq[:, 0:12], T.bq[:, 16:28], A.mult)
        V("tt", "nd2", "dv nd0", T.nd[:, 48:84:3], T.nd[:, 0:24:2], T.bq[:, 32:44], A.subtract)
        V("tt", "nd3", "dv gp", T.nd[:, 50:84:3], T.gp[:, 96:108], T.bq[:, 32:44], A.add)
        V("tt", "kc0", "kc br", T.kc[:, 24:36], T.kc[:, 0:12], T.bq[:, 16:28], A.add)
        V("tt", "kc1", "kc br", T.kc[:, 36:48], T.kc[:, 12:24], T.bq[:, 16:28], A.subtract)
        for s in range(4):
            k, h = s // 2, s % 2
            x, y = T.so[:, 80 * k + 116 + 37 * h:80 * k + 117 + 37 * h], T.so[:, 80 * k + 36 + 37 * h:80 * k + 37 + 37 * h]
            V("ts", "ff%d" % s, "kc so%d so%d" % (k, k + 1), T.ff[:, 12 * s:12 * s + 12:2], T.kc[:, 0:6], x, y, A.add, A.is_gt)
            V("ts", "fg%d" % s, "kc%d so%d so%d" % (k, k, k + 1), T.ff[:, 48 + 18 * h + k:66 + 18 * h:3], T.kc[:, 24 + 12 * k + 6 * h:30 + 12 * k + 6 * h], x, y, A.add, A.is_gt)
        V("scan", "ab", "nd0 nd1 ffa ff0 ff1 ff2 ff3", T.abi[:, 0:48], T.nd[:, 0:48], T.ff[:, 0:48], 0.0, A.add, A.mult)
        V("scan", "bt", "ndz nd2 nd3 ffb fg0 fg1 fg2 fg3", T.abi[:, 48:84], T.nd[:, 48:84], T.ff[:, 48:84], 0.0, A.add, A.mult)
        lift[0] = 1000.0
        V("cp", "ab%d" % t, "ab", T.ab[:, 24 * t:24 * t + 24], T.abi[:, 1:48:2])
        lift[0] = 0.0
        send(["ab%d" % t], "al%d" % t, "la%d" % t, [(T.la[:, 24 * t:24 * t + 24], T.ab[:, 24 * t:24 * t + 24])], NEAR)
        V("cp", "bt16", "bt", T.bt16[:], T.abi[:, 50:84:3])
        V("cp", "btv", "idb bt16", T.btv[:], (T.idb[:, 0:272], T.bt16[:, 0:12]))
        for c in range(16):
            if c < NE:
                lift[0] = 1000.0 if c < NF else -600.0
                S("abd%d" % c, "btv nw3" if c >= 2 else "idb bt16 nw3", T.abd[:, c, 0:192], T.btv[:] if c >= 2 else (T.idb[:, 0:272], T.bt16[:, 0:12]), ACT.Abs, bias=T.nw[:, 48 + c:49 + c], scale=1024.0)
                lift[0] = 0.0
            else:
                V("ts", "abd%d" % c, "btv nwb", T.abd[:, c, 0:192], T.btv[:], T.nwb[:, c:c + 1], 1024.0, A.not_equal, A.mult)
            V("scan", "ev%d" % c, "abz de1 de2 abd%d" % c, T.abo[:, c, 0:193], T.de[:, 0:193], T.abd[:, c, 0:193], 252.0, A.add, A.min)
        V("ts", "ek", names("ev", 0, 16) + " ekz", T.ek[:, 1:32:2], T.abo[:, :, 192], 1.0 / 16, 144 - 0.375, A.mult, A.add)
        V("ts", "em", names("ev", 0, 16) + " emz", T.ei[:, 1:32:2], T.abo[:, :, 192], 16.0, 255.0 * 144, A.mult, A.add)
        V("scan", "ex2", "ek em", T.ei[:, 32:64], T.ek[:], T.ei[:, 0:32], 0.0, A.mult, A.add)
        V("cp", "e16", "ex2", T.e16[:], T.ei[:, 33:64:2])
        for b in range(4):
            w = T.f2[:, 272 * b:272 * b + 272]
            S("at%d" % b, "f2z%d f2_%d la%d" % (b, b, t), T.at[:, 192 * b:192 * b + 192], (w, T.la[:, 24 * t:24 * t + 12]), ACT.Copy)
            V("tt", "zt%d" % b, "f2z%d f2_%d la%d at%d" % (b, b, t, b), T.zt[:, b:768:4], (w, T.la[:, 24 * t + 12:24 * t + 24]), T.at[:, 192 * b:192 * b + 192], A.add)
        V("qz", "zq zp", "zt0 zt1 zt2 zt3", T.zq[:, 0:192], T.zp[:, 0:192], T.zt[:, 0:768])
        for h in range(2):
            kv = T.qj[:, 264 * h + 256:264 * h + 257]
            S("li0%d" % h, "kv%d" % h, T.li[:, h:h + 1], kv, ACT.Identity, bias=512.0, scale=2.0 * h - 1.0)
            S("li1%d" % h, "kv%d" % h, T.li[:, 2 + h:3 + h], kv, ACT.Relu, bias=1.0, scale=2.0 * h - 1.0)
            S("li2%d" % h, "li0%d li1%d cm" % (h, h), T.li[:, 4 + h:5 + h], T.li[:, 2 + h:3 + h], ACT.Identity, bias=T.li[:, h:h + 1], scale=T.cm[:, h:h + 1])
            S("li3%d" % h, "br li2%d" % h, T.li[:, 6 + h:7 + h], T.bq[:, 16 + 6 * h:17 + 6 * h], ACT.Identity, bias=T.li[:, 4 + h:5 + h], scale=-256.0)
        V("cp", "m16", "ab", T.m16[:], T.abi[:, 11:24:12])
        S("mt", "idb m16", T.mt[:], (T.idb[:, 0:272], T.m16[:, 0:2]), ACT.Copy)
        V("cp", "ln16", "li30 li31", T.ln16[:], T.li[:, 6:8])
        V("cp", "lt", "mt ln16 ltz", (T.lt[:, 0:544], T.ln16[:, 0:2]), T.mt[:])
        if t < R - 1:
            V("scan", "lo", "lt dg", T.lo[:], T.dg[:, 0:512], T.lt[:, 0:512], 0.0, A.add, A.min)
            V("ts", "lw16", "lo pf7", T.lw16[:], T.lo[:, 15:512:16], fix, None, A.add)
            S("c1o", "lo pf7", T.c1[:, 31:512:32], T.lo[:, 15:256:16], ACT.Identity, bias=fix, scale=1.0)
            V("tt", "c0", "lo", T.c0[:, 31:512:32], T.lo[:, 271:512:16], T.lo[:, 15:256:16], A.subtract)
            apart("lo pf7", T.lo[:, 271:512:16], fix)
        place[0] = 5000
        ph = ["ph0", "ph1", "ps1", "ps2"]
        for b in range(4):
            mm(ph[b], T.wq[:, 128 * b:128 * b + 128], "wq wp", T.wp[:, 128 * b:128 * b + 128], T.zq[:, 0:192], "zq zp", T.zp[:, 0:192], 192)
            S("hb%d" % b, ph[b], T.hb[:, 208 * b:208 * b + 192], T[ph[b]][:, 0:192], ACT.Copy, scale=0.03125)
        for h in range(2):
            lo, hi = 128 * h, 128 * h + 128
            for b in range(4):
                if b == 3:
                    V("tt", "xs3%d" % h, "hbz3 hb3 e16 fw3", T.xs[:, 4 * lo + 3:4 * hi:4], (T.hb[:, 624:832], T.e16[:, 8 * h:8 * h + 8]), T.fw[:, 768 + lo:768 + hi], A.add)
                elif h == 0:
                    V("tt", "xs%d0 xs%d1" % (b, b), "hbz%d hb%d e16 fw%d" % (b, b, b), T.xs[:, b:1024:4], (T.hb[:, 208 * b:208 * b + 208], T.e16[:, 0:16]),
                      T.fw[:, 256 * b:256 * b + 256], A.add)
        for h in range(2):
            lo, hi = 128 * h, 128 * h + 128
            V("qz", "xq%d" % (t + 1) + "ab"[h], " ".join("xs%d%d" % (b, h) for b in range(4)), T["xq%d" % (t + 1)][:, lo:hi], T["xp%d" % (t + 1)][:, lo:hi], T.xs[:, 4 * lo:4 * hi])
    place[0] = 0
    xk = "xq%d" % R
    xq, xp = T[xk], T["xp%d" % R]
    S("olr", "lt", T.olr[:], T.lt[:, 0:512], ACT.Copy)
    dma("y", "ool", ["olr"], [], T.ol[:], T.olr[0:128:16, :])
    for h, pa in enumerate(("ps1", "ps2")):
        lo, hi = 128 * h, 128 * h + 128
        mm(pa, T.vq[:, 0:128], "vq vp", T.vp[:, 0:128], xq[:, lo:hi], xk + "ab"[h], xp[:, lo:hi], 128)
        dma("y", "oc%d" % h, [xk + "ab"[h]], [], T.oc[:, 4 * lo:4 * hi], xq[:, lo:hi].bitcast(dt.uint8), 2500.0)
        V("cp", "ms%d" % h, pa, T.ms[:, lo:hi], T[pa][:, 0:128])
        dma("ys"[h], "oy%d" % h, ["ms%d" % h], [], T.y[:, lo:hi], T.ms[:, lo:hi], 2500.0)
    for k in range(4):
        dma("sssy"[k], "os%d" % k, [xk + "a", xk + "b"], [], T.osc[4 * k:4 * k + 4, 0:256], xp[32 * k:32 * k + 4, 0:256])

    total, waited = {}, {q: {} for q in queues}
    if len(calls) not in ORDER:
        ORDER[len(calls)] = in_order(calls)
    for i in ORDER[len(calls)]:
        c = calls[i]
        if c["q"] is not None:
            best = {}
            for d in c["deps"]:
                s, n = calls[d]["done"]
                best[s] = max(best.get(s, 0), n)
            for s in sorted(best):
                if waited[c["q"]].get(s, 0) < best[s]:
                    queues[c["q"]].wait_ge(T.sem[s], best[s])
                    waited[c["q"]][s] = best[s]
            c["issue"]()
        total[c["sem"]] = total.get(c["sem"], 0) + c["inc"]
        c["done"] = (c["sem"], total[c["sem"]])
    for s in sorted(total):
        g.wait_ge(T.sem[s], total[s])
